import numpy as np
import ml_dtypes


def mxq(x, axis, fmt="e4m3"):
    dtype, down = {"e4m3": (ml_dtypes.float8_e4m3fn, 7), "e5m2": (ml_dtypes.float8_e5m2, 14)}[fmt]
    v = np.moveaxis(np.asarray(x, np.float32).astype(ml_dtypes.bfloat16).astype(np.float64), axis, -1)
    blocks = v.reshape(v.shape[:-1] + (-1, 32))
    amax = np.abs(blocks).max(-1, keepdims=True)
    byte = np.maximum(np.where(amax > 0, np.frexp(amax)[1] - 1 + 127, 0) - down, 1)
    scale = np.exp2(byte - 127.0)
    codes = (blocks / scale).astype(np.float32).astype(dtype).astype(np.float64)
    return np.moveaxis((codes * scale).reshape(v.shape), -1, axis)


WIDE = False


def mx_kscale(k):
    if not WIDE:
        return np.ones(k)
    levels = np.array([18, -18])
    if k % 512:
        return np.exp2(np.random.permutation(np.resize(levels, k // 32))).repeat(32)
    a = np.empty((k // 512, 16))
    for p in range(k // 512):
        a[p, :8] = np.random.permutation(np.resize(levels, 8))
        for g in range(8):
            far = levels[np.abs(levels - a[p, g]) >= 10]
            a[p, g + 8] = far[np.random.randint(len(far))]
    return np.exp2(a.ravel()).repeat(32)


def f64(x):
    return np.asarray(x).astype(np.float64)


def striped(idx):
    return np.tile(np.asarray(idx).reshape(-1, 16).T, (8, 1)).astype(np.uint16)


def unstriped(offs):
    return offs[:16].T.reshape(-1).astype(np.int64)


B, N, T, D, DV, R = 2, 512, 2048, 512, 512, 512


def setup_inputs():
    n = np.random.standard_normal
    idx = np.random.permutation(T)[:B * N]
    s = mx_kscale(D)[:, None]
    z = mx_kscale(R)[:, None]
    v = mx_kscale(DV)[:, None]
    q = n((B, D, R))
    do = n((B, DV, R))
    return {
        "qT": (q * s).astype(np.float32),
        "kT": (n((D, T)) * (1.00 / np.sqrt(D)) / s).astype(np.float32),
        "vT": (n((DV, T)) / np.sqrt(DV) / v).astype(np.float32),
        "doT": (do * v).astype(np.float32),
        "rw": (np.random.uniform(0.5, 1.5, (B, R, 1)) * 1.0 / np.sqrt(R) * z).astype(np.float32),
        "qm": (q.transpose(0, 2, 1) / z).astype(np.float32),
        "offs": striped(idx),
    }


def reference(qT, kT, vT, doT, rw, qm, offs):
    idx = unstriped(offs)
    pick = lambda x: x[:, idx].reshape(x.shape[0], B, N).transpose(1, 0, 2)
    a = mxq(f64(qT), 1, "e4m3").transpose(0, 2, 1) @ mxq(pick(f64(kT)), 1, "e4m3")
    p = 1.0 / (1.0 + np.exp(-a))
    dp = mxq(f64(doT), 1, "e5m2").transpose(0, 2, 1) @ mxq(pick(f64(vT)), 1, "e4m3")
    ds = f64(rw) * dp * p * (1.0 - p)
    dk = mxq(f64(qm), 1, "e4m3").transpose(0, 2, 1) @ mxq(ds, 1, "e5m2")
    gk = np.zeros((D, T))
    gk[:, idx] = dk.transpose(1, 0, 2).reshape(D, B * N)
    return gk

@@ -1,0 +1,224 @@
+from contextlib import ExitStack
+
+import concourse.mybir as mybir
+
+B, N, T, D, R = 2, 512, 2048, 512, 512
+FLOPS = 3 * 2 * B * N * D * R
+
+F32 = mybir.dt.float32
+BF16 = mybir.dt.bfloat16
+U32 = mybir.dt.uint32
+U16 = mybir.dt.uint16
+U8 = mybir.dt.uint8
+E4M3 = mybir.dt.float8_e4m3fn_x4
+E5M2 = mybir.dt.float8_e5m2_x4
+ACT = mybir.ActivationFunctionType
+ALU = mybir.AluOpType
+
+P = 128
+PACK = 4
+W = 512
+LIST_COLS = N // 16
+
+
+def tile_attend_gat_sig_k_kernel(tc, qT, kT, vT, doT, rw, qm, offs, out):
+    nc = tc.nc
+    with ExitStack() as ctx:
+        keep = ctx.enter_context(tc.tile_pool(name="keep", bufs=1))
+        planes = ctx.enter_context(tc.tile_pool(name="planes", bufs=5))
+        raws = ctx.enter_context(tc.tile_pool(name="raws", bufs=3))
+        groups = ctx.enter_context(tc.tile_pool(name="groups", bufs=5))
+        psum = ctx.enter_context(tc.psum_pool(name="psum", bufs=8))
+
+        offsets = keep.tile([P, B * LIST_COLS], U16, name="offsets")
+        nc.sync.dma_start(offsets[:], offs)
+        gate = keep.tile([P, B, PACK], F32, name="gate")
+        nc.sync.dma_start(gate[:], rw.rearrange("b (p t) o -> p b (t o)", t=PACK))
+
+        windows = [keep.tile([P, T], F32, name="window%d" % j) for j in range(D // P)]
+        for j, window in enumerate(windows):
+            (nc.vector if j % 2 == 0 else nc.gpsimd).memset(window[:], 0.0)
+
+        gate_pos = keep.tile([P, B, PACK], F32, name="gate_pos")
+        gate_neg = keep.tile([P, B, PACK], F32, name="gate_neg")
+        nc.vector.tensor_scalar(out=gate_pos[:], in0=gate[:], scalar1=0.25, scalar2=None, op0=ALU.mult)
+        nc.vector.tensor_scalar(out=gate_neg[:], in0=gate[:], scalar1=-0.25, scalar2=None, op0=ALU.mult)
+
+        def seq_list(b):
+            return offsets[:, b * LIST_COLS : (b + 1) * LIST_COLS]
+
+        def load_plane(pool_dram, t):
+            plane = planes.tile([P, T], F32, name="plane")
+            nc.sync.dma_start(plane[:], pool_dram.rearrange("(p t) n -> p t n", t=PACK)[:, t, :])
+            return plane
+
+        def load_rows(rows):
+            raw = raws.tile([P, PACK, W], F32, name="raw")
+            nc.sync.dma_start(raw[:], rows.rearrange("(p j) w -> p j w", j=PACK))
+            return raw
+
+        def new_group():
+            return groups.tile([P, W * PACK], BF16, name="group", align_bytes=64)
+
+        def copy_on(engine, dst, src):
+            if engine == "vector":
+                nc.vector.tensor_copy(out=dst, in_=src)
+            else:
+                nc.scalar.copy(out=dst, in_=src)
+
+        def interleave(engine, group, src, c0=0, c1=W):
+            copy_on(
+                engine,
+                group[:, c0 * PACK : c1 * PACK].rearrange("p (c i j) -> p c j i", i=4, j=PACK),
+                src[:, :, c0:c1].rearrange("p j (c i) -> p c j i", i=4),
+            )
+
+        def interleave_queries(engine, group, src, m0=0, m1=P):
+            copy_on(
+                engine,
+                group[:].rearrange("p (t m j) -> p m j t", t=PACK, j=PACK)[:, m0:m1],
+                src[:].rearrange("p j (m t) -> p m j t", t=PACK)[:, m0:m1],
+            )
+
+        def new_operand(name):
+            codes = keep.tile([P, W], U32, name=name + "_codes", align_bytes=64)
+            scales = keep.tile([P, W], U8, name=name + "_scales", align_bytes=64)
+            return codes, scales
+
+        def quantize(operand, group, fmt, pieces=1):
+            codes, scales = operand
+            w = W // pieces
+            for s in range(pieces):
+                nc.vector.quantize_mx(
+                    out=codes[:, s * w : (s + 1) * w].bitcast(fmt),
+                    scales=scales[:, s * w : (s + 1) * w],
+                    in_=group[:, s * w * PACK : (s + 1) * w * PACK],
+                )
+
+        def product(stationary, fmt_s, block, moving, fmt_m):
+            acc = psum.tile([P, W], F32, name="acc")
+            cols = slice(block * P, (block + 1) * P)
+            nc.tensor.matmul_mx(
+                out=acc[:],
+                lhsT=stationary[0][:, cols].bitcast(fmt_s),
+                lhsT_scale=stationary[1][:, cols],
+                rhs=moving[0][:].bitcast(fmt_m),
+                rhs_scale=moving[1][:],
+                start=True,
+                stop=True,
+            )
+            return acc
+
+        def prepared(name, engine, src, fmt, queries=False):
+            group = new_group()
+            if queries:
+                interleave_queries(engine, group, src)
+            else:
+                interleave(engine, group, src)
+            operand = new_operand(name)
+            quantize(operand, group, fmt)
+            return operand
+
+        def tanh_squared(b, q_op, k_op):
+            sq = keep.tile([P, PACK, W], F32, name="weight%d" % b)
+            for t in range(PACK):
+                a = product(q_op, E4M3, t, k_op, E4M3)
+                nc.scalar.activation(out=sq[:, t, :], in_=a[:], func=ACT.Tanh, scale=0.5)
+            nc.scalar.activation(out=sq[:], in_=sq[:], func=ACT.Square)
+            return sq
+
+        def key_gradient(b, qm_op, ds_op):
+            tiles = []
+            for j in range(D // P):
+                acc = product(qm_op, E4M3, j, ds_op, E5M2)
+                dk = keep.tile([P, W], F32, name="dk%d_%d" % (b, j))
+                nc.scalar.copy(out=dk[:], in_=acc[:])
+                tiles.append(dk)
+            return tiles
+
+        keys = keep.tile([P, PACK, B * N], F32, name="keys")
+        values = keep.tile([P, PACK, B * N], F32, name="values")
+
+        def gather_pool(pool_dram, gathered):
+            for t in range(PACK - 1):
+                plane = load_plane(pool_dram, t)
+                nc.vector.tensor_copy(out=gathered[:, t, :], in_=plane[:].indirect(offsets[:]))
+            plane = load_plane(pool_dram, PACK - 1)
+            nc.vector.tensor_copy(out=gathered[:, PACK - 1, 0:N], in_=plane[:].indirect(seq_list(0)))
+            return plane
+
+        def gather_rest(plane, gathered):
+            nc.vector.tensor_copy(out=gathered[:, PACK - 1, N : 2 * N], in_=plane[:].indirect(seq_list(1)))
+
+        k_last = gather_pool(kT, keys)
+        gather_rest(k_last, keys)
+        q_raw = load_rows(qT[0])
+        k_group = new_group()
+        interleave("scalar", k_group, keys[:, :, 0:N])
+        q_group = new_group()
+        interleave_queries("vector", q_group, q_raw)
+        k0 = new_operand("k0")
+        quantize(k0, k_group, E4M3)
+        q0 = new_operand("q0")
+        quantize(q0, q_group, E4M3)
+        k1_group = new_group()
+        interleave("scalar", k1_group, keys[:, :, N : 2 * N])
+        weight = tanh_squared(0, q0, k0)
+        for t in range(PACK):
+            nc.scalar.activation(
+                out=weight[:, t, :], in_=weight[:, t, :], func=ACT.Identity,
+                scale=gate_neg[:, 0, t : t + 1], bias=gate_pos[:, 0, t : t + 1],
+            )
+
+        v_last = gather_pool(vT, values)
+        do_raw = load_rows(doT[0])
+        v_group = new_group()
+        interleave("vector", v_group, values[:, :, 0:N])
+        do_group = new_group()
+        interleave_queries("scalar", do_group, do_raw, 0, 64)
+        interleave_queries("vector", do_group, do_raw, 64, P)
+        v0 = new_operand("v0")
+        quantize(v0, v_group, E4M3)
+        do0 = new_operand("do0")
+        quantize(do0, do_group, E5M2, pieces=PACK)
+        for t in range(PACK):
+            dp = product(do0, E5M2, t, v0, E4M3)
+            nc.vector.tensor_tensor(out=weight[:, t, :], in0=dp[:], in1=weight[:, t, :], op=ALU.mult)
+        qm0 = prepared("qm0", "scalar", load_rows(qm[0]), E4M3)
+        ds_group = new_group()
+        interleave("vector", ds_group, weight, 0, 320)
+        interleave("scalar", ds_group, weight, 320, W)
+        ds0 = new_operand("ds0")
+        quantize(ds0, ds_group, E5M2)
+        dk0 = key_gradient(0, qm0, ds0)
+
+        k1 = new_operand("k1")
+        quantize(k1, k1_group, E4M3)
+        gather_rest(v_last, values)
+        q1 = prepared("q1", "scalar", load_rows(qT[1]), E4M3, queries=True)
+        sq = tanh_squared(1, q1, k1)
+        v1 = prepared("v1", "scalar", values[:, :, N : 2 * N], E4M3)
+        do1 = prepared("do1", "scalar", load_rows(doT[1]), E5M2, queries=True)
+        gated = keep.tile([P, PACK, W], F32, name="gated")
+        for t in range(PACK):
+            dp = product(do1, E5M2, t, v1, E4M3)
+            nc.scalar.activation(out=gated[:, t, :], in_=dp[:], func=ACT.Copy, scale=gate_neg[:, 1, t : t + 1])
+        ds_group = new_group()
+        nc.vector.scalar_tensor_tensor(
+            out=ds_group[:].rearrange("p (i t) -> p i t", t=PACK),
+            in0=sq[:].rearrange("p t i -> p i t"),
+            scalar=1.0,
+            in1=gated[:].rearrange("p t i -> p i t"),
+            op0=ALU.subtract,
+            op1=ALU.mult,
+        )
+        ds1 = new_operand("ds1")
+        quantize(ds1, ds_group, E5M2)
+        qm1 = prepared("qm1", "scalar", load_rows(qm[1]), E4M3)
+        dk1 = key_gradient(1, qm1, ds1)
+
+        for j in range(D // P):
+            nc.vector.tensor_copy(out=windows[j][:].indirect(seq_list(0)), in_=dk0[j][:])
+        for j in range(D // P):
+            nc.vector.tensor_copy(out=windows[j][:].indirect(seq_list(1)), in_=dk1[j][:])
+            nc.sync.dma_start(out[j * P : (j + 1) * P, :], windows[j][:])

@@ -25,10 +25,8 @@ def tile_attend_gat_sig_k_kernel(tc, qT, kT, vT, doT, rw, qm, offs, out):
     nc = tc.nc
     with ExitStack() as ctx:
         keep = ctx.enter_context(tc.tile_pool(name="keep", bufs=1))
-        planes = ctx.enter_context(tc.tile_pool(name="planes", bufs=5))
-        raws = ctx.enter_context(tc.tile_pool(name="raws", bufs=3))
-        groups = ctx.enter_context(tc.tile_pool(name="groups", bufs=5))
-        psum = ctx.enter_context(tc.psum_pool(name="psum", bufs=8))
+        groups = ctx.enter_context(tc.tile_pool(name="groups", bufs=3))
+        psum = ctx.enter_context(tc.psum_pool(name="psum", bufs=1))
 
         offsets = keep.tile([P, B * LIST_COLS], U16, name="offsets")
         nc.sync.dma_start(offsets[:], offs)
@@ -47,17 +45,19 @@ def tile_attend_gat_sig_k_kernel(tc, qT, kT, vT, doT, rw, qm, offs, out):
         def seq_list(b):
             return offsets[:, b * LIST_COLS : (b + 1) * LIST_COLS]
 
-        def load_plane(pool_dram, t):
-            plane = planes.tile([P, T], F32, name="plane")
+        def load_plane(pool_dram, t, slot):
+            plane = keep.tile([P, T], F32, name="plane", tag=slot)
             nc.sync.dma_start(plane[:], pool_dram.rearrange("(p t) n -> p t n", t=PACK)[:, t, :])
             return plane
 
-        def load_rows(rows):
-            raw = raws.tile([P, PACK, W], F32, name="raw")
+        def load_rows(rows, slot):
+            raw = keep.tile([P, PACK, W], F32, name="raw", tag=slot)
             nc.sync.dma_start(raw[:], rows.rearrange("(p j) w -> p j w", j=PACK))
             return raw
 
-        def new_group():
+        def new_group(slot=None):
+            if slot is not None:
+                return keep.tile([P, W * PACK], BF16, name="group", tag=slot, align_bytes=64)
             return groups.tile([P, W * PACK], BF16, name="group", align_bytes=64)
 
         def copy_on(engine, dst, src):
@@ -80,8 +80,8 @@ def tile_attend_gat_sig_k_kernel(tc, qT, kT, vT, doT, rw, qm, offs, out):
                 src[:].rearrange("p j (m t) -> p m j t", t=PACK)[:, m0:m1],
             )
 
-        def new_operand(name):
-            codes = keep.tile([P, W], U32, name=name + "_codes", align_bytes=64)
+        def new_operand(name, slot=None):
+            codes = keep.tile([P, W], U32, name=name + "_codes", tag=slot or name + "_codes", align_bytes=64)
             scales = keep.tile([P, W], U8, name=name + "_scales", align_bytes=64)
             return codes, scales
 
@@ -95,8 +95,8 @@ def tile_attend_gat_sig_k_kernel(tc, qT, kT, vT, doT, rw, qm, offs, out):
                     in_=group[:, s * w * PACK : (s + 1) * w * PACK],
                 )
 
-        def product(stationary, fmt_s, block, moving, fmt_m):
-            acc = psum.tile([P, W], F32, name="acc")
+        def product(bank, stationary, fmt_s, block, moving, fmt_m):
+            acc = psum.tile([P, W], F32, name="acc", tag="bank%d" % bank)
             cols = slice(block * P, (block + 1) * P)
             nc.tensor.matmul_mx(
                 out=acc[:],
@@ -109,50 +109,48 @@ def tile_attend_gat_sig_k_kernel(tc, qT, kT, vT, doT, rw, qm, offs, out):
             )
             return acc
 
-        def prepared(name, engine, src, fmt, queries=False):
-            group = new_group()
-            if queries:
-                interleave_queries(engine, group, src)
-            else:
-                interleave(engine, group, src)
-            operand = new_operand(name)
+        def prepared(name, engine, src, fmt, queries=False, slot=None, codes_slot=None):
+            group = new_group(slot)
+            for h in range(2):
+                if queries:
+                    interleave_queries(engine, group, src, h * P // 2, (h + 1) * P // 2)
+                else:
+                    interleave(engine, group, src, h * W // 2, (h + 1) * W // 2)
+            operand = new_operand(name, codes_slot)
             quantize(operand, group, fmt)
             return operand
 
         def tanh_squared(b, q_op, k_op):
-            sq = keep.tile([P, PACK, W], F32, name="weight%d" % b)
+            sq = keep.tile([P, PACK, W], F32, name="weight%d" % b, tag=("slot9", "qm0_codes")[b], align_bytes=64)
             for t in range(PACK):
-                a = product(q_op, E4M3, t, k_op, E4M3)
+                a = product(PACK * b + t, q_op, E4M3, t, k_op, E4M3)
                 nc.scalar.activation(out=sq[:, t, :], in_=a[:], func=ACT.Tanh, scale=0.5)
-            nc.scalar.activation(out=sq[:], in_=sq[:], func=ACT.Square)
+                nc.scalar.activation(out=sq[:, t, :], in_=sq[:, t, :], func=ACT.Square)
             return sq
 
-        def key_gradient(b, qm_op, ds_op):
-            tiles = []
-            for j in range(D // P):
-                acc = product(qm_op, E4M3, j, ds_op, E5M2)
-                dk = keep.tile([P, W], F32, name="dk%d_%d" % (b, j))
-                nc.scalar.copy(out=dk[:], in_=acc[:])
-                tiles.append(dk)
-            return tiles
+        def key_gradient(b, j, qm_op, ds_op, slot):
+            acc = product(j, qm_op, E4M3, j, ds_op, E5M2)
+            dk = keep.tile([P, W], F32, name="dk%d_%d" % (b, j), tag=slot)
+            nc.scalar.copy(out=dk[:], in_=acc[:])
+            return dk
 
         keys = keep.tile([P, PACK, B * N], F32, name="keys")
         values = keep.tile([P, PACK, B * N], F32, name="values")
 
-        def gather_pool(pool_dram, gathered):
+        def gather_pool(pool_dram, gathered, first_slot):
             for t in range(PACK - 1):
-                plane = load_plane(pool_dram, t)
+                plane = load_plane(pool_dram, t, "slot%d" % (first_slot + t))
                 nc.vector.tensor_copy(out=gathered[:, t, :], in_=plane[:].indirect(offsets[:]))
-            plane = load_plane(pool_dram, PACK - 1)
+            plane = load_plane(pool_dram, PACK - 1, "slot%d" % (first_slot + PACK - 1))
             nc.vector.tensor_copy(out=gathered[:, PACK - 1, 0:N], in_=plane[:].indirect(seq_list(0)))
             return plane
 
         def gather_rest(plane, gathered):
             nc.vector.tensor_copy(out=gathered[:, PACK - 1, N : 2 * N], in_=plane[:].indirect(seq_list(1)))
 
-        k_last = gather_pool(kT, keys)
+        k_last = gather_pool(kT, keys, 0)
         gather_rest(k_last, keys)
-        q_raw = load_rows(qT[0])
+        q_raw = load_rows(qT[0], "slot8")
         k_group = new_group()
         interleave("scalar", k_group, keys[:, :, 0:N])
         q_group = new_group()
@@ -170,38 +168,37 @@ def tile_attend_gat_sig_k_kernel(tc, qT, kT, vT, doT, rw, qm, offs, out):
                 scale=gate_neg[:, 0, t : t + 1], bias=gate_pos[:, 0, t : t + 1],
             )
 
-        v_last = gather_pool(vT, values)
-        do_raw = load_rows(doT[0])
+        v_last = gather_pool(vT, values, PACK)
+        do_raw = load_rows(doT[0], "slot0")
         v_group = new_group()
         interleave("vector", v_group, values[:, :, 0:N])
         do_group = new_group()
-        interleave_queries("scalar", do_group, do_raw, 0, 64)
-        interleave_queries("vector", do_group, do_raw, 64, P)
+        interleave_queries("scalar", do_group, do_raw)
         v0 = new_operand("v0")
         quantize(v0, v_group, E4M3)
         do0 = new_operand("do0")
         quantize(do0, do_group, E5M2, pieces=PACK)
         for t in range(PACK):
-            dp = product(do0, E5M2, t, v0, E4M3)
+            dp = product(PACK + t, do0, E5M2, t, v0, E4M3)
             nc.vector.tensor_tensor(out=weight[:, t, :], in0=dp[:], in1=weight[:, t, :], op=ALU.mult)
-        qm0 = prepared("qm0", "scalar", load_rows(qm[0]), E4M3)
-        ds_group = new_group()
-        interleave("vector", ds_group, weight, 0, 320)
-        interleave("scalar", ds_group, weight, 320, W)
+        qm0 = prepared("qm0", "scalar", load_rows(qm[0], "slot1"), E4M3)
+        ds_group = new_group("group_ds0")
+        interleave("vector", ds_group, weight)
         ds0 = new_operand("ds0")
         quantize(ds0, ds_group, E5M2)
-        dk0 = key_gradient(0, qm0, ds0)
 
         k1 = new_operand("k1")
         quantize(k1, k1_group, E4M3)
         gather_rest(v_last, values)
-        q1 = prepared("q1", "scalar", load_rows(qT[1]), E4M3, queries=True)
+        q1 = prepared("q1", "scalar", load_rows(qT[1], "slot2"), E4M3, queries=True, slot="group_q1", codes_slot="group_ds0")
+        do1 = prepared("do1", "scalar", load_rows(doT[1], "slot3"), E5M2, queries=True, slot="late", codes_slot="group_q1")
+        dk0 = [key_gradient(0, 0, qm0, ds0, "dk0_0"), key_gradient(0, 1, qm0, ds0, "dk0_1")]
+        v1 = prepared("v1", "scalar", values[:, :, N : 2 * N], E4M3, slot="late")
+        dk0.append(key_gradient(0, 2, qm0, ds0, "dk0_2"))
         sq = tanh_squared(1, q1, k1)
-        v1 = prepared("v1", "scalar", values[:, :, N : 2 * N], E4M3)
-        do1 = prepared("do1", "scalar", load_rows(doT[1]), E5M2, queries=True)
-        gated = keep.tile([P, PACK, W], F32, name="gated")
+        gated = keep.tile([P, PACK, W], F32, name="gated", tag="slot6")
         for t in range(PACK):
-            dp = product(do1, E5M2, t, v1, E4M3)
+            dp = product(PACK + t, do1, E5M2, t, v1, E4M3)
             nc.scalar.activation(out=gated[:, t, :], in_=dp[:], func=ACT.Copy, scale=gate_neg[:, 1, t : t + 1])
         ds_group = new_group()
         nc.vector.scalar_tensor_tensor(
@@ -214,8 +211,9 @@ def tile_attend_gat_sig_k_kernel(tc, qT, kT, vT, doT, rw, qm, offs, out):
         )
         ds1 = new_operand("ds1")
         quantize(ds1, ds_group, E5M2)
-        qm1 = prepared("qm1", "scalar", load_rows(qm[1]), E4M3)
-        dk1 = key_gradient(1, qm1, ds1)
+        qm1 = prepared("qm1", "scalar", load_rows(qm[1], "slot8"), E4M3, slot="v1_codes")
+        dk0.append(key_gradient(0, 3, qm0, ds0, "slot6"))
+        dk1 = [key_gradient(1, j, qm1, ds1, "dk1_%d" % j) for j in range(D // P)]
 
         for j in range(D // P):
             nc.vector.tensor_copy(out=windows[j][:].indirect(seq_list(0)), in_=dk0[j][:])

@@ -30,28 +30,21 @@ def tile_attend_gat_sig_k_kernel(tc, qT, kT, vT, doT, rw, qm, offs, out):
 
         offsets = keep.tile([P, B * LIST_COLS], U16, name="offsets")
         nc.sync.dma_start(offsets[:], offs)
-        gate = keep.tile([P, B, PACK], F32, name="gate")
-        nc.sync.dma_start(gate[:], rw.rearrange("b (p t) o -> p b (t o)", t=PACK))
 
         windows = [keep.tile([P, T], F32, name="window%d" % j) for j in range(D // P)]
-        for j, window in enumerate(windows):
-            (nc.vector if j % 2 == 0 else nc.gpsimd).memset(window[:], 0.0)
-
-        gate_pos = keep.tile([P, B, PACK], F32, name="gate_pos")
-        gate_neg = keep.tile([P, B, PACK], F32, name="gate_neg")
-        nc.vector.tensor_scalar(out=gate_pos[:], in0=gate[:], scalar1=0.25, scalar2=None, op0=ALU.mult)
-        nc.vector.tensor_scalar(out=gate_neg[:], in0=gate[:], scalar1=-0.25, scalar2=None, op0=ALU.mult)
+        for window in windows:
+            nc.vector.memset(window[:], 0.0)
 
         def seq_list(b):
             return offsets[:, b * LIST_COLS : (b + 1) * LIST_COLS]
 
         def load_plane(pool_dram, t, slot):
-            plane = keep.tile([P, T], F32, name="plane", tag=slot)
+            plane = keep.tile([P, T], F32, name="plane", tag=slot, align_bytes=64)
             nc.sync.dma_start(plane[:], pool_dram.rearrange("(p t) n -> p t n", t=PACK)[:, t, :])
             return plane
 
         def load_rows(rows, slot):
-            raw = keep.tile([P, PACK, W], F32, name="raw", tag=slot)
+            raw = keep.tile([P, PACK, W], F32, name="raw", tag=slot, align_bytes=64)
             nc.sync.dma_start(raw[:], rows.rearrange("(p j) w -> p j w", j=PACK))
             return raw
 
@@ -63,6 +56,8 @@ def tile_attend_gat_sig_k_kernel(tc, qT, kT, vT, doT, rw, qm, offs, out):
         def copy_on(engine, dst, src):
             if engine == "vector":
                 nc.vector.tensor_copy(out=dst, in_=src)
+            elif engine == "gpsimd":
+                nc.gpsimd.tensor_scalar(out=dst, in0=src, scalar1=1.0, scalar2=0.0, op0=ALU.mult, op1=ALU.add)
             else:
                 nc.scalar.copy(out=dst, in_=src)
 
@@ -130,12 +125,12 @@ def tile_attend_gat_sig_k_kernel(tc, qT, kT, vT, doT, rw, qm, offs, out):
 
         def key_gradient(b, j, qm_op, ds_op, slot):
             acc = product(j, qm_op, E4M3, j, ds_op, E5M2)
-            dk = keep.tile([P, W], F32, name="dk%d_%d" % (b, j), tag=slot)
+            dk = keep.tile([P, W], F32, name="dk%d_%d" % (b, j), tag=slot, align_bytes=64)
             nc.scalar.copy(out=dk[:], in_=acc[:])
             return dk
 
         keys = keep.tile([P, PACK, B * N], F32, name="keys")
-        values = keep.tile([P, PACK, B * N], F32, name="values")
+        values = keep.tile([P, PACK, B * N], F32, name="values", tag="values", align_bytes=64)
 
         def gather_pool(pool_dram, gathered, first_slot):
             for t in range(PACK - 1):
@@ -151,6 +146,13 @@ def tile_attend_gat_sig_k_kernel(tc, qT, kT, vT, doT, rw, qm, offs, out):
         k_last = gather_pool(kT, keys, 0)
         gather_rest(k_last, keys)
         q_raw = load_rows(qT[0], "slot8")
+        gate = keep.tile([P, B, PACK], F32, name="gate")
+        nc.sync.dma_start(gate[:], rw.rearrange("b (p t) o -> p b (t o)", t=PACK))
+        gate_pos = keep.tile([P, B, PACK], F32, name="gate_pos")
+        gate_neg = keep.tile([P, B, PACK], F32, name="gate_neg")
+        nc.gpsimd.tensor_scalar(out=gate_pos[:], in0=gate[:], scalar1=0.25, scalar2=None, op0=ALU.mult)
+        nc.gpsimd.tensor_scalar(out=gate_neg[:], in0=gate[:], scalar1=-0.25, scalar2=None, op0=ALU.mult)
+
         k_group = new_group()
         interleave("scalar", k_group, keys[:, :, 0:N])
         q_group = new_group()
@@ -192,11 +194,12 @@ def tile_attend_gat_sig_k_kernel(tc, qT, kT, vT, doT, rw, qm, offs, out):
         gather_rest(v_last, values)
         q1 = prepared("q1", "scalar", load_rows(qT[1], "slot2"), E4M3, queries=True, slot="group_q1", codes_slot="group_ds0")
         do1 = prepared("do1", "scalar", load_rows(doT[1], "slot3"), E5M2, queries=True, slot="late", codes_slot="group_q1")
-        dk0 = [key_gradient(0, 0, qm0, ds0, "dk0_0"), key_gradient(0, 1, qm0, ds0, "dk0_1")]
-        v1 = prepared("v1", "scalar", values[:, :, N : 2 * N], E4M3, slot="late")
-        dk0.append(key_gradient(0, 2, qm0, ds0, "dk0_2"))
+        dk0 = [key_gradient(0, 0, qm0, ds0, "dk0_0")]
+        v1 = prepared("v1", "gpsimd", values[:, :, N : 2 * N], E4M3, slot="late")
+        dk0.append(key_gradient(0, 1, qm0, ds0, "values"))
         sq = tanh_squared(1, q1, k1)
-        gated = keep.tile([P, PACK, W], F32, name="gated", tag="slot6")
+        dk0.append(key_gradient(0, 2, qm0, ds0, "group_q1"))
+        gated = keep.tile([P, PACK, W], F32, name="gated", tag="slot6", align_bytes=64)
         for t in range(PACK):
             dp = product(PACK + t, do1, E5M2, t, v1, E4M3)
             nc.scalar.activation(out=gated[:, t, :], in_=dp[:], func=ACT.Copy, scale=gate_neg[:, 1, t : t + 1])
@@ -209,10 +212,10 @@ def tile_attend_gat_sig_k_kernel(tc, qT, kT, vT, doT, rw, qm, offs, out):
             op0=ALU.subtract,
             op1=ALU.mult,
         )
+        qm1 = prepared("qm1", "gpsimd", load_rows(qm[1], "slot8"), E4M3, slot="late", codes_slot="slot6")
         ds1 = new_operand("ds1")
         quantize(ds1, ds_group, E5M2)
-        qm1 = prepared("qm1", "scalar", load_rows(qm[1], "slot8"), E4M3, slot="v1_codes")
-        dk0.append(key_gradient(0, 3, qm0, ds0, "slot6"))
+        dk0.append(key_gradient(0, 3, qm0, ds0, "late"))
         dk1 = [key_gradient(1, j, qm1, ds1, "dk1_%d" % j) for j in range(D // P)]
 
         for j in range(D // P):

@@ -77,7 +77,7 @@ def tile_attend_gat_sig_k_kernel(tc, qT, kT, vT, doT, rw, qm, offs, out):
 
         def new_operand(name, slot=None):
             codes = keep.tile([P, W], U32, name=name + "_codes", tag=slot or name + "_codes", align_bytes=64)
-            scales = keep.tile([P, W], U8, name=name + "_scales", align_bytes=64)
+            scales = keep.tile([P, W], U8, name=name + "_scales", tag=name + "_scales", align_bytes=64)
             return codes, scales
 
         def quantize(operand, group, fmt, pieces=1):
@@ -116,7 +116,7 @@ def tile_attend_gat_sig_k_kernel(tc, qT, kT, vT, doT, rw, qm, offs, out):
             return operand
 
         def tanh_squared(b, q_op, k_op):
-            sq = keep.tile([P, PACK, W], F32, name="weight%d" % b, tag=("slot9", "qm0_codes")[b], align_bytes=64)
+            sq = keep.tile([P, PACK, W], F32, name="weight%d" % b, tag="slot9", align_bytes=64)
             for t in range(PACK):
                 a = product(PACK * b + t, q_op, E4M3, t, k_op, E4M3)
                 nc.scalar.activation(out=sq[:, t, :], in_=a[:], func=ACT.Tanh, scale=0.5)
@@ -183,13 +183,13 @@ def tile_attend_gat_sig_k_kernel(tc, qT, kT, vT, doT, rw, qm, offs, out):
         for t in range(PACK):
             dp = product(PACK + t, do0, E5M2, t, v0, E4M3)
             nc.vector.tensor_tensor(out=weight[:, t, :], in0=dp[:], in1=weight[:, t, :], op=ALU.mult)
-        qm0 = prepared("qm0", "scalar", load_rows(qm[0], "slot1"), E4M3)
+        qm0 = prepared("qm0", "scalar", load_rows(qm[0], "slot1"), E4M3, codes_slot="slot9")
         ds_group = new_group("group_ds0")
         interleave("vector", ds_group, weight)
         ds0 = new_operand("ds0")
         quantize(ds0, ds_group, E5M2)
 
-        k1 = new_operand("k1")
+        k1 = new_operand("k1", "slot7")
         quantize(k1, k1_group, E4M3)
         gather_rest(v_last, values)
         q1 = prepared("q1", "scalar", load_rows(qT[1], "slot2"), E4M3, queries=True, slot="group_q1", codes_slot="group_ds0")
@@ -198,28 +198,40 @@ def tile_attend_gat_sig_k_kernel(tc, qT, kT, vT, doT, rw, qm, offs, out):
         v1 = prepared("v1", "gpsimd", values[:, :, N : 2 * N], E4M3, slot="late")
         dk0.append(key_gradient(0, 1, qm0, ds0, "values"))
         sq = tanh_squared(1, q1, k1)
-        dk0.append(key_gradient(0, 2, qm0, ds0, "group_q1"))
-        gated = keep.tile([P, PACK, W], F32, name="gated", tag="slot6", align_bytes=64)
         for t in range(PACK):
-            dp = product(PACK + t, do1, E5M2, t, v1, E4M3)
-            nc.scalar.activation(out=gated[:, t, :], in_=dp[:], func=ACT.Copy, scale=gate_neg[:, 1, t : t + 1])
+            nc.gpsimd.tensor_scalar(out=sq[:, t, :], in0=sq[:, t, :], scalar1=1.0, scalar2=-1.0, op0=ALU.mult, op1=ALU.add)
+        gated = keep.tile([P, PACK, W], F32, name="gated", tag="slot6", align_bytes=64)
+        dp1 = [product(PACK + t, do1, E5M2, t, v1, E4M3) for t in range(PACK)]
         ds_group = new_group()
-        nc.vector.scalar_tensor_tensor(
-            out=ds_group[:].rearrange("p (i t) -> p i t", t=PACK),
-            in0=sq[:].rearrange("p t i -> p i t"),
-            scalar=1.0,
-            in1=gated[:].rearrange("p t i -> p i t"),
-            op0=ALU.subtract,
-            op1=ALU.mult,
-        )
-        qm1 = prepared("qm1", "gpsimd", load_rows(qm[1], "slot8"), E4M3, slot="late", codes_slot="slot6")
+        halves = (slice(0, W // 2), slice(W // 2, W))
+
+        def ds1_half(cols):
+            for t in range(PACK):
+                nc.scalar.activation(out=gated[:, t, cols], in_=dp1[t][:, cols], func=ACT.Copy, scale=gate_neg[:, 1, t : t + 1])
+            nc.gpsimd.tensor_tensor(
+                out=ds_group[:, cols.start * PACK : cols.stop * PACK].rearrange("p (c i t) -> p c t i", i=4, t=PACK),
+                in0=sq[:, :, cols].rearrange("p t (c i) -> p c t i", i=4),
+                in1=gated[:, :, cols].rearrange("p t (c i) -> p c t i", i=4),
+                op=ALU.mult,
+            )
+
+        ds1_half(halves[0])
+        dk0.append(key_gradient(0, 2, qm0, ds0, "group_q1"))
+        ds1_half(halves[1])
+        last = product(3, qm0, E4M3, 3, ds0, E5M2)
+        last_a = keep.tile([P, W // 2], F32, name="last_a", tag="v1_scales", align_bytes=64)
+        nc.scalar.copy(out=last_a[:], in_=last[:, halves[0]])
+        qm1 = prepared("qm1", "scalar", load_rows(qm[1], "slot8"), E4M3, slot="v1_codes")
         ds1 = new_operand("ds1")
         quantize(ds1, ds_group, E5M2)
-        dk0.append(key_gradient(0, 3, qm0, ds0, "late"))
+        last_b = keep.tile([P, W // 2], F32, name="last_b", tag="slot6", align_bytes=64)
+        nc.scalar.copy(out=last_b[:], in_=last[:, halves[1]])
         dk1 = [key_gradient(1, j, qm1, ds1, "dk1_%d" % j) for j in range(D // P)]
 
-        for j in range(D // P):
+        for j in range(D // P - 1):
             nc.vector.tensor_copy(out=windows[j][:].indirect(seq_list(0)), in_=dk0[j][:])
+        nc.vector.tensor_copy(out=windows[3][:].indirect(offsets[:, 0 : LIST_COLS // 2]), in_=last_a[:])
+        nc.vector.tensor_copy(out=windows[3][:].indirect(offsets[:, LIST_COLS // 2 : LIST_COLS]), in_=last_b[:])
         for j in range(D // P):
             nc.vector.tensor_copy(out=windows[j][:].indirect(seq_list(1)), in_=dk1[j][:])
             nc.sync.dma_start(out[j * P : (j + 1) * P, :], windows[j][:])

@@ -75,20 +75,17 @@ def tile_attend_gat_sig_k_kernel(tc, qT, kT, vT, doT, rw, qm, offs, out):
                 src[:].rearrange("p j (m t) -> p m j t", t=PACK)[:, m0:m1],
             )
 
-        def new_operand(name, slot=None):
-            codes = keep.tile([P, W], U32, name=name + "_codes", tag=slot or name + "_codes", align_bytes=64)
+        def new_operand(name, slot=None, codes=None):
+            if codes is None:
+                codes = keep.tile([P, W], U32, name=name + "_codes", tag=slot or name + "_codes", align_bytes=64)
             scales = keep.tile([P, W], U8, name=name + "_scales", tag=name + "_scales", align_bytes=64)
             return codes, scales
 
-        def quantize(operand, group, fmt, pieces=1):
+        def quantize(operand, group, fmt, c0=0, c1=W):
             codes, scales = operand
-            w = W // pieces
-            for s in range(pieces):
-                nc.vector.quantize_mx(
-                    out=codes[:, s * w : (s + 1) * w].bitcast(fmt),
-                    scales=scales[:, s * w : (s + 1) * w],
-                    in_=group[:, s * w * PACK : (s + 1) * w * PACK],
-                )
+            nc.vector.quantize_mx(
+                out=codes[:, c0:c1].bitcast(fmt), scales=scales[:, c0:c1], in_=group[:, c0 * PACK : c1 * PACK]
+            )
 
         def product(bank, stationary, fmt_s, block, moving, fmt_m):
             acc = psum.tile([P, W], F32, name="acc", tag="bank%d" % bank)
@@ -97,7 +94,7 @@ def tile_attend_gat_sig_k_kernel(tc, qT, kT, vT, doT, rw, qm, offs, out):
                 out=acc[:],
                 lhsT=stationary[0][:, cols].bitcast(fmt_s),
                 lhsT_scale=stationary[1][:, cols],
-                rhs=moving[0][:].bitcast(fmt_m),
+                rhs=moving[0][:, 0:W].bitcast(fmt_m),
                 rhs_scale=moving[1][:],
                 start=True,
                 stop=True,
@@ -115,13 +112,11 @@ def tile_attend_gat_sig_k_kernel(tc, qT, kT, vT, doT, rw, qm, offs, out):
             quantize(operand, group, fmt)
             return operand
 
-        def tanh_squared(b, q_op, k_op):
-            sq = keep.tile([P, PACK, W], F32, name="weight%d" % b, tag="slot9", align_bytes=64)
-            for t in range(PACK):
-                a = product(PACK * b + t, q_op, E4M3, t, k_op, E4M3)
-                nc.scalar.activation(out=sq[:, t, :], in_=a[:], func=ACT.Tanh, scale=0.5)
-                nc.scalar.activation(out=sq[:, t, :], in_=sq[:, t, :], func=ACT.Square)
-            return sq
+        def tanh_squared(sq, t, bank, q_op, k_op):
+            a = product(bank, q_op, E4M3, t, k_op, E4M3)
+            th = keep.tile([P, W], F32, name="tanh%d" % t, tag="tanh%d" % t, align_bytes=64)
+            nc.scalar.activation(out=th[:], in_=a[:], func=ACT.Tanh, scale=0.5)
+            nc.scalar.activation(out=sq[:, t, :], in_=th[:], func=ACT.Square)
 
         def key_gradient(b, j, qm_op, ds_op, slot):
             acc = product(j, qm_op, E4M3, j, ds_op, E5M2)
@@ -163,7 +158,9 @@ def tile_attend_gat_sig_k_kernel(tc, qT, kT, vT, doT, rw, qm, offs, out):
         quantize(q0, q_group, E4M3)
         k1_group = new_group()
         interleave("scalar", k1_group, keys[:, :, N : 2 * N])
-        weight = tanh_squared(0, q0, k0)
+        weight = keep.tile([P, PACK, W], F32, name="weight0", align_bytes=64)
+        for t in range(PACK):
+            tanh_squared(weight, t, t, q0, k0)
         for t in range(PACK):
             nc.scalar.activation(
                 out=weight[:, t, :], in_=weight[:, t, :], func=ACT.Identity,
@@ -174,30 +171,52 @@ def tile_attend_gat_sig_k_kernel(tc, qT, kT, vT, doT, rw, qm, offs, out):
         do_raw = load_rows(doT[0], "slot0")
         v_group = new_group()
         interleave("vector", v_group, values[:, :, 0:N])
-        do_group = new_group()
+        do_group = new_group("group_do0")
         interleave_queries("scalar", do_group, do_raw)
         v0 = new_operand("v0")
         quantize(v0, v_group, E4M3)
         do0 = new_operand("do0")
-        quantize(do0, do_group, E5M2, pieces=PACK)
+        for t in range(PACK):
+            quantize(do0, do_group, E5M2, t * P, (t + 1) * P)
         for t in range(PACK):
             dp = product(PACK + t, do0, E5M2, t, v0, E4M3)
             nc.vector.tensor_tensor(out=weight[:, t, :], in0=dp[:], in1=weight[:, t, :], op=ALU.mult)
-        qm0 = prepared("qm0", "scalar", load_rows(qm[0], "slot1"), E4M3, codes_slot="slot9")
+        gather_rest(v_last, values)
+        k1 = new_operand("k1", "slot7")
+        quantize(k1, k1_group, E4M3)
+        qm0_raw = load_rows(qm[0], "slot1")
+        qm0_group = new_group("group_qm0")
+        for h in range(2):
+            interleave("scalar", qm0_group, qm0_raw, h * W // 2, (h + 1) * W // 2)
+        q1 = prepared("q1", "scalar", load_rows(qT[1], "slot2"), E4M3, queries=True, slot="group_q1")
+        qm0_first = new_operand("qm0_first")
+        quantize(qm0_first, qm0_group, E4M3, 0, P)
         ds_group = new_group("group_ds0")
         interleave("vector", ds_group, weight)
         ds0 = new_operand("ds0")
         quantize(ds0, ds_group, E5M2)
 
-        k1 = new_operand("k1", "slot7")
-        quantize(k1, k1_group, E4M3)
-        gather_rest(v_last, values)
-        q1 = prepared("q1", "scalar", load_rows(qT[1], "slot2"), E4M3, queries=True, slot="group_q1", codes_slot="group_ds0")
-        do1 = prepared("do1", "scalar", load_rows(doT[1], "slot3"), E5M2, queries=True, slot="late", codes_slot="group_q1")
-        dk0 = [key_gradient(0, 0, qm0, ds0, "dk0_0")]
-        v1 = prepared("v1", "gpsimd", values[:, :, N : 2 * N], E4M3, slot="late")
-        dk0.append(key_gradient(0, 1, qm0, ds0, "values"))
-        sq = tanh_squared(1, q1, k1)
+        do1_raw = load_rows(doT[1], "slot3")
+        do1_group = new_group("group_do1")
+        for h in range(2):
+            interleave_queries("scalar", do1_group, do1_raw, h * P // 2, (h + 1) * P // 2)
+        late_codes = keep.tile([P, 2, W], U32, name="late_codes", tag="group_ds0", align_bytes=64)
+        do1 = new_operand("do1", codes=late_codes[:, 0, :])
+        quantize(do1, do1_group, E5M2)
+        qm0 = new_operand("qm0", codes=late_codes[:, 1, :])
+        quantize(qm0, qm0_group, E4M3, P, 2 * P)
+        quantize(qm0, qm0_group, E4M3, 2 * P, W)
+        v1_group = new_group("group_do0")
+        for c in range(PACK):
+            interleave("gpsimd" if c < PACK - 1 else "scalar", v1_group, values[:, :, N : 2 * N], c * P, (c + 1) * P)
+        dk0 = [key_gradient(0, 0, qm0_first, ds0, "dk0_0")]
+        v1 = new_operand("v1")
+        quantize(v1, v1_group, E4M3)
+        sq = keep.tile([P, PACK, W], F32, name="weight1", align_bytes=64)
+        for t in range(PACK):
+            tanh_squared(sq, t, PACK + t, q1, k1)
+            if t == 1:
+                dk0.append(key_gradient(0, 1, qm0, ds0, "tanh0"))
         for t in range(PACK):
             nc.gpsimd.tensor_scalar(out=sq[:, t, :], in0=sq[:, t, :], scalar1=1.0, scalar2=-1.0, op0=ALU.mult, op1=ALU.add)
         gated = keep.tile([P, PACK, W], F32, name="gated", tag="slot6", align_bytes=64)
@@ -215,8 +234,8 @@ def tile_attend_gat_sig_k_kernel(tc, qT, kT, vT, doT, rw, qm, offs, out):
                 op=ALU.mult,
             )
 
+        dk0.append(key_gradient(0, 2, qm0, ds0, "tanh2"))
         ds1_half(halves[0])
-        dk0.append(key_gradient(0, 2, qm0, ds0, "group_q1"))
         ds1_half(halves[1])
         last = product(3, qm0, E4M3, 3, ds0, E5M2)
         last_a = keep.tile([P, W // 2], F32, name="last_a", tag="v1_scales", align_bytes=64)

@@ -125,7 +125,7 @@ def tile_attend_gat_sig_k_kernel(tc, qT, kT, vT, doT, rw, qm, offs, out):
             return dk
 
         keys = keep.tile([P, PACK, B * N], F32, name="keys")
-        values = keep.tile([P, PACK, B * N], F32, name="values", tag="values", align_bytes=64)
+        values = [keep.tile([P, PACK, N], F32, name="values%d" % b, align_bytes=64) for b in range(B)]
 
         def gather_pool(pool_dram, gathered, first_slot):
             for t in range(PACK - 1):
@@ -145,8 +145,8 @@ def tile_attend_gat_sig_k_kernel(tc, qT, kT, vT, doT, rw, qm, offs, out):
         nc.sync.dma_start(gate[:], rw.rearrange("b (p t) o -> p b (t o)", t=PACK))
         gate_pos = keep.tile([P, B, PACK], F32, name="gate_pos")
         gate_neg = keep.tile([P, B, PACK], F32, name="gate_neg")
-        nc.gpsimd.tensor_scalar(out=gate_pos[:], in0=gate[:], scalar1=0.25, scalar2=None, op0=ALU.mult)
-        nc.gpsimd.tensor_scalar(out=gate_neg[:], in0=gate[:], scalar1=-0.25, scalar2=None, op0=ALU.mult)
+        nc.scalar.activation(out=gate_pos[:], in_=gate[:], func=ACT.Copy, scale=0.25)
+        nc.scalar.activation(out=gate_neg[:], in_=gate[:], func=ACT.Copy, scale=-0.25)
 
         k_group = new_group()
         interleave("scalar", k_group, keys[:, :, 0:N])
@@ -158,68 +158,75 @@ def tile_attend_gat_sig_k_kernel(tc, qT, kT, vT, doT, rw, qm, offs, out):
         quantize(q0, q_group, E4M3)
         k1_group = new_group()
         interleave("scalar", k1_group, keys[:, :, N : 2 * N])
-        weight = keep.tile([P, PACK, W], F32, name="weight0", align_bytes=64)
+        weight = keep.tile([P, PACK, W], F32, name="weight0", tag="weight0", align_bytes=64)
         for t in range(PACK):
             tanh_squared(weight, t, t, q0, k0)
         for t in range(PACK):
-            nc.scalar.activation(
-                out=weight[:, t, :], in_=weight[:, t, :], func=ACT.Identity,
-                scale=gate_neg[:, 0, t : t + 1], bias=gate_pos[:, 0, t : t + 1],
+            nc.gpsimd.tensor_scalar(
+                out=weight[:, t, :], in0=weight[:, t, :], scalar1=gate_neg[:, 0, t : t + 1],
+                scalar2=gate_pos[:, 0, t : t + 1], op0=ALU.mult, op1=ALU.add,
             )
 
-        v_last = gather_pool(vT, values, PACK)
+        for t in range(2):
+            plane = load_plane(vT, t, "slot%d" % (PACK + t))
+            for b in range(B):
+                nc.vector.tensor_copy(out=values[b][:, t, :], in_=plane[:].indirect(seq_list(b)))
+        v_late = keep.tile([P, 2 * T], F32, name="v_late", tag="slot7", align_bytes=64)
+        for t in range(2):
+            nc.sync.dma_start(v_late[:, t * T : (t + 1) * T], vT.rearrange("(p t) n -> p t n", t=PACK)[:, 2 + t, :])
+        for t in range(2):
+            nc.vector.tensor_copy(out=values[0][:, 2 + t, :], in_=v_late[:, t * T : (t + 1) * T].indirect(seq_list(0)))
+        nc.vector.tensor_copy(out=values[1][:, 2, :], in_=v_late[:].indirect(seq_list(1)))
+        nc.vector.tensor_copy(out=values[1][:, 3, :], in_=v_late[:, T : 2 * T].indirect(seq_list(1)))
         do_raw = load_rows(doT[0], "slot0")
-        v_group = new_group()
-        interleave("vector", v_group, values[:, :, 0:N])
-        do_group = new_group("group_do0")
-        interleave_queries("scalar", do_group, do_raw)
+        v_group = new_group("group_v0")
+        interleave("scalar", v_group, values[0], 0, 2 * P)
+        for c in (2, 3):
+            interleave("gpsimd", v_group, values[0], c * P, (c + 1) * P)
+        do_halves = [keep.tile([P, W * 2], BF16, name="do_half", tag="do_half%d" % u, align_bytes=64) for u in range(2)]
+        for u in range(2):
+            nc.scalar.copy(
+                out=do_halves[u][:].rearrange("p (e m j) -> p m j e", e=2, j=PACK),
+                in_=do_raw[:].rearrange("p j (m u e) -> p u m j e", u=2, e=2)[:, u],
+            )
         v0 = new_operand("v0")
         quantize(v0, v_group, E4M3)
         do0 = new_operand("do0")
-        for t in range(PACK):
-            quantize(do0, do_group, E5M2, t * P, (t + 1) * P)
+        k1 = new_operand("k1", "do_half0")
+        for u in range(2):
+            cols = slice(u * W // 2, (u + 1) * W // 2)
+            nc.vector.quantize_mx(out=do0[0][:, cols].bitcast(E5M2), scales=do0[1][:, cols], in_=do_halves[u][:])
+        quantize(k1, k1_group, E4M3)
+        behind_do0 = keep.tile([P, (PACK + 1) * W], F32, name="behind_do0", tag="do_half1", align_bytes=64)
+        ds_planes = behind_do0[:, 0 : PACK * W].rearrange("p (t c) -> p t c", t=PACK)
+        v1_halves = [behind_do0[:, PACK * W :].bitcast(BF16)]
         for t in range(PACK):
             dp = product(PACK + t, do0, E5M2, t, v0, E4M3)
-            nc.vector.tensor_tensor(out=weight[:, t, :], in0=dp[:], in1=weight[:, t, :], op=ALU.mult)
-        gather_rest(v_last, values)
-        k1 = new_operand("k1", "slot7")
-        quantize(k1, k1_group, E4M3)
-        qm0_raw = load_rows(qm[0], "slot1")
-        qm0_group = new_group("group_qm0")
-        for h in range(2):
-            interleave("scalar", qm0_group, qm0_raw, h * W // 2, (h + 1) * W // 2)
-        q1 = prepared("q1", "scalar", load_rows(qT[1], "slot2"), E4M3, queries=True, slot="group_q1")
-        qm0_first = new_operand("qm0_first")
-        quantize(qm0_first, qm0_group, E4M3, 0, P)
+            nc.vector.tensor_tensor(out=ds_planes[:, t, :], in0=dp[:], in1=weight[:, t, :], op=ALU.mult)
         ds_group = new_group("group_ds0")
-        interleave("vector", ds_group, weight)
+        interleave("vector", ds_group, ds_planes)
+        qm0 = prepared("qm0", "scalar", load_rows(qm[0], "slot1"), E4M3, slot="group_qm0", codes_slot="weight0")
         ds0 = new_operand("ds0")
         quantize(ds0, ds_group, E5M2)
 
-        do1_raw = load_rows(doT[1], "slot3")
-        do1_group = new_group("group_do1")
-        for h in range(2):
-            interleave_queries("scalar", do1_group, do1_raw, h * P // 2, (h + 1) * P // 2)
-        late_codes = keep.tile([P, 2, W], U32, name="late_codes", tag="group_ds0", align_bytes=64)
-        do1 = new_operand("do1", codes=late_codes[:, 0, :])
-        quantize(do1, do1_group, E5M2)
-        qm0 = new_operand("qm0", codes=late_codes[:, 1, :])
-        quantize(qm0, qm0_group, E4M3, P, 2 * P)
-        quantize(qm0, qm0_group, E4M3, 2 * P, W)
-        v1_group = new_group("group_do0")
-        for c in range(PACK):
-            interleave("gpsimd" if c < PACK - 1 else "scalar", v1_group, values[:, :, N : 2 * N], c * P, (c + 1) * P)
-        dk0 = [key_gradient(0, 0, qm0_first, ds0, "dk0_0")]
-        v1 = new_operand("v1")
-        quantize(v1, v1_group, E4M3)
-        sq = keep.tile([P, PACK, W], F32, name="weight1", align_bytes=64)
+        q1 = prepared("q1", "scalar", load_rows(qT[1], "slot2"), E4M3, queries=True, slot="group_v0")
+        do1 = prepared("do1", "scalar", load_rows(doT[1], "slot3"), E5M2, queries=True, slot="group_do1")
+        dk0 = [key_gradient(0, 0, qm0, ds0, "dk0_0")]
+        v1_halves.append(keep.tile([P, W * 2], BF16, name="v1_late", tag="group_do1", align_bytes=64))
+        v1 = new_operand("v1", "group_ds0")
+        for u in range(2):
+            for c in range(2):
+                interleave("gpsimd", v1_halves[u], values[1][:, :, u * W // 2 : (u + 1) * W // 2], c * P, (c + 1) * P)
+            cols = slice(u * W // 2, (u + 1) * W // 2)
+            nc.vector.quantize_mx(out=v1[0][:, cols].bitcast(E4M3), scales=v1[1][:, cols], in_=v1_halves[u][:, 0 : W * 2])
+        sq = keep.tile([P, PACK, W], F32, name="weight1", tag="slot4", align_bytes=64)
         for t in range(PACK):
             tanh_squared(sq, t, PACK + t, q1, k1)
             if t == 1:
                 dk0.append(key_gradient(0, 1, qm0, ds0, "tanh0"))
         for t in range(PACK):
             nc.gpsimd.tensor_scalar(out=sq[:, t, :], in0=sq[:, t, :], scalar1=1.0, scalar2=-1.0, op0=ALU.mult, op1=ALU.add)
-        gated = keep.tile([P, PACK, W], F32, name="gated", tag="slot6", align_bytes=64)
+        gated = keep.tile([P, PACK, W], F32, name="gated", tag="slot5", align_bytes=64)
         dp1 = [product(PACK + t, do1, E5M2, t, v1, E4M3) for t in range(PACK)]
         ds_group = new_group()
         halves = (slice(0, W // 2), slice(W // 2, W))
@@ -235,15 +242,15 @@ def tile_attend_gat_sig_k_kernel(tc, qT, kT, vT, doT, rw, qm, offs, out):
             )
 
         dk0.append(key_gradient(0, 2, qm0, ds0, "tanh2"))
-        ds1_half(halves[0])
-        ds1_half(halves[1])
+        for cols in (slice(0, P), slice(P, 2 * P), halves[1]):
+            ds1_half(cols)
         last = product(3, qm0, E4M3, 3, ds0, E5M2)
         last_a = keep.tile([P, W // 2], F32, name="last_a", tag="v1_scales", align_bytes=64)
         nc.scalar.copy(out=last_a[:], in_=last[:, halves[0]])
-        qm1 = prepared("qm1", "scalar", load_rows(qm[1], "slot8"), E4M3, slot="v1_codes")
+        qm1 = prepared("qm1", "scalar", load_rows(qm[1], "slot8"), E4M3, slot="do1_codes")
         ds1 = new_operand("ds1")
         quantize(ds1, ds_group, E5M2)
-        last_b = keep.tile([P, W // 2], F32, name="last_b", tag="slot6", align_bytes=64)
+        last_b = keep.tile([P, W // 2], F32, name="last_b", tag="slot5", align_bytes=64)
         nc.scalar.copy(out=last_b[:], in_=last[:, halves[1]])
         dk1 = [key_gradient(1, j, qm1, ds1, "dk1_%d" % j) for j in range(D // P)]
 

@@ -19,6 +19,8 @@ P = 128
 PACK = 4
 W = 512
 LIST_COLS = N // 16
+DO0_SPLIT = 64
+V0_ON_SCALAR = 288
 
 
 def tile_attend_gat_sig_k_kernel(tc, qT, kT, vT, doT, rw, qm, offs, out):
@@ -116,10 +118,10 @@ def tile_attend_gat_sig_k_kernel(tc, qT, kT, vT, doT, rw, qm, offs, out):
             a = product(bank, q_op, E4M3, t, k_op, E4M3)
             th = keep.tile([P, W], F32, name="tanh%d" % t, tag="tanh%d" % t, align_bytes=64)
             nc.scalar.activation(out=th[:], in_=a[:], func=ACT.Tanh, scale=0.5)
-            nc.scalar.activation(out=sq[:, t, :], in_=th[:], func=ACT.Square)
+            nc.scalar.activation(out=sq, in_=th[:], func=ACT.Square)
 
-        def key_gradient(b, j, qm_op, ds_op, slot):
-            acc = product(j, qm_op, E4M3, j, ds_op, E5M2)
+        def key_gradient(b, j, qm_op, ds_op, slot, bank):
+            acc = product(bank, qm_op, E4M3, j, ds_op, E5M2)
             dk = keep.tile([P, W], F32, name="dk%d_%d" % (b, j), tag=slot, align_bytes=64)
             nc.scalar.copy(out=dk[:], in_=acc[:])
             return dk
@@ -156,14 +158,14 @@ def tile_attend_gat_sig_k_kernel(tc, qT, kT, vT, doT, rw, qm, offs, out):
         quantize(k0, k_group, E4M3)
         q0 = new_operand("q0")
         quantize(q0, q_group, E4M3)
-        k1_group = new_group()
+        k1_group = new_group("group_k1")
         interleave("scalar", k1_group, keys[:, :, N : 2 * N])
-        weight = keep.tile([P, PACK, W], F32, name="weight0", tag="weight0", align_bytes=64)
+        weight = [keep.tile([P, W], F32, name="weight0_%d" % t, tag="weight0_%d" % t, align_bytes=64) for t in range(PACK)]
         for t in range(PACK):
-            tanh_squared(weight, t, t, q0, k0)
+            tanh_squared(weight[t][:], t, t, q0, k0)
         for t in range(PACK):
             nc.gpsimd.tensor_scalar(
-                out=weight[:, t, :], in0=weight[:, t, :], scalar1=gate_neg[:, 0, t : t + 1],
+                out=weight[t][:], in0=weight[t][:], scalar1=gate_neg[:, 0, t : t + 1],
                 scalar2=gate_pos[:, 0, t : t + 1], op0=ALU.mult, op1=ALU.add,
             )
 
@@ -180,54 +182,56 @@ def tile_attend_gat_sig_k_kernel(tc, qT, kT, vT, doT, rw, qm, offs, out):
         nc.vector.tensor_copy(out=values[1][:, 3, :], in_=v_late[:, T : 2 * T].indirect(seq_list(1)))
         do_raw = load_rows(doT[0], "slot0")
         v_group = new_group("group_v0")
-        interleave("scalar", v_group, values[0], 0, 2 * P)
-        for c in (2, 3):
-            interleave("gpsimd", v_group, values[0], c * P, (c + 1) * P)
+        interleave("scalar", v_group, values[0], 0, V0_ON_SCALAR)
+        interleave("gpsimd", v_group, values[0], V0_ON_SCALAR, W)
         do_halves = [keep.tile([P, W * 2], BF16, name="do_half", tag="do_half%d" % u, align_bytes=64) for u in range(2)]
-        for u in range(2):
-            nc.scalar.copy(
-                out=do_halves[u][:].rearrange("p (e m j) -> p m j e", e=2, j=PACK),
-                in_=do_raw[:].rearrange("p j (m u e) -> p u m j e", u=2, e=2)[:, u],
+        for engine, u, m0, m1 in (("scalar", 0, 0, P), ("scalar", 1, 0, DO0_SPLIT), ("vector", 1, DO0_SPLIT, P)):
+            copy_on(
+                engine,
+                do_halves[u][:].rearrange("p (e m j) -> p m j e", e=2, j=PACK)[:, m0:m1],
+                do_raw[:].rearrange("p j (m u e) -> p u m j e", u=2, e=2)[:, u, m0:m1],
             )
         v0 = new_operand("v0")
         quantize(v0, v_group, E4M3)
         do0 = new_operand("do0")
-        k1 = new_operand("k1", "do_half0")
         for u in range(2):
             cols = slice(u * W // 2, (u + 1) * W // 2)
             nc.vector.quantize_mx(out=do0[0][:, cols].bitcast(E5M2), scales=do0[1][:, cols], in_=do_halves[u][:])
+        k1 = new_operand("k1", "slot0")
         quantize(k1, k1_group, E4M3)
-        behind_do0 = keep.tile([P, (PACK + 1) * W], F32, name="behind_do0", tag="do_half1", align_bytes=64)
-        ds_planes = behind_do0[:, 0 : PACK * W].rearrange("p (t c) -> p t c", t=PACK)
-        v1_halves = [behind_do0[:, PACK * W :].bitcast(BF16)]
+        ds_planes = keep.tile([P, PACK, W], F32, name="ds_planes", tag="slot5", align_bytes=64)
+        v1_halves = [keep.tile([P, W * 2], BF16, name="v1_early", tag="group_k1", align_bytes=64)]
         for t in range(PACK):
             dp = product(PACK + t, do0, E5M2, t, v0, E4M3)
-            nc.vector.tensor_tensor(out=ds_planes[:, t, :], in0=dp[:], in1=weight[:, t, :], op=ALU.mult)
+            nc.vector.tensor_tensor(out=ds_planes[:, t, :], in0=dp[:], in1=weight[t][:], op=ALU.mult)
+        qm0 = prepared("qm0", "scalar", load_rows(qm[0], "slot1"), E4M3, slot="group_qm0", codes_slot="weight0_2")
         ds_group = new_group("group_ds0")
         interleave("vector", ds_group, ds_planes)
-        qm0 = prepared("qm0", "scalar", load_rows(qm[0], "slot1"), E4M3, slot="group_qm0", codes_slot="weight0")
         ds0 = new_operand("ds0")
         quantize(ds0, ds_group, E5M2)
 
         q1 = prepared("q1", "scalar", load_rows(qT[1], "slot2"), E4M3, queries=True, slot="group_v0")
-        do1 = prepared("do1", "scalar", load_rows(doT[1], "slot3"), E5M2, queries=True, slot="group_do1")
-        dk0 = [key_gradient(0, 0, qm0, ds0, "dk0_0")]
+        do1_raw = load_rows(doT[1], "slot3")
+        do1_group = new_group("group_do1")
+        interleave_queries("scalar", do1_group, do1_raw)
+        do1 = new_operand("do1")
+        quantize(do1, do1_group, E5M2)
+        dk0 = [key_gradient(0, 0, qm0, ds0, "dk0_0", 0)]
         v1_halves.append(keep.tile([P, W * 2], BF16, name="v1_late", tag="group_do1", align_bytes=64))
-        v1 = new_operand("v1", "group_ds0")
+        v1 = new_operand("v1", "weight0_3")
         for u in range(2):
-            for c in range(2):
-                interleave("gpsimd", v1_halves[u], values[1][:, :, u * W // 2 : (u + 1) * W // 2], c * P, (c + 1) * P)
+            interleave("gpsimd", v1_halves[u], values[1][:, :, u * W // 2 : (u + 1) * W // 2], 0, W // 2)
             cols = slice(u * W // 2, (u + 1) * W // 2)
             nc.vector.quantize_mx(out=v1[0][:, cols].bitcast(E4M3), scales=v1[1][:, cols], in_=v1_halves[u][:, 0 : W * 2])
         sq = keep.tile([P, PACK, W], F32, name="weight1", tag="slot4", align_bytes=64)
         for t in range(PACK):
-            tanh_squared(sq, t, PACK + t, q1, k1)
+            tanh_squared(sq[:, t, :], t, 1 + t, q1, k1)
             if t == 1:
-                dk0.append(key_gradient(0, 1, qm0, ds0, "tanh0"))
+                dk0.append(key_gradient(0, 1, qm0, ds0, "tanh0", 1))
         for t in range(PACK):
             nc.gpsimd.tensor_scalar(out=sq[:, t, :], in0=sq[:, t, :], scalar1=1.0, scalar2=-1.0, op0=ALU.mult, op1=ALU.add)
         gated = keep.tile([P, PACK, W], F32, name="gated", tag="slot5", align_bytes=64)
-        dp1 = [product(PACK + t, do1, E5M2, t, v1, E4M3) for t in range(PACK)]
+        dp1 = [product(bank, do1, E5M2, t, v1, E4M3) for t, bank in enumerate((5, 6, 7, 3))]
         ds_group = new_group()
         halves = (slice(0, W // 2), slice(W // 2, W))
 
@@ -241,10 +245,11 @@ def tile_attend_gat_sig_k_kernel(tc, qT, kT, vT, doT, rw, qm, offs, out):
                 op=ALU.mult,
             )
 
-        dk0.append(key_gradient(0, 2, qm0, ds0, "tanh2"))
-        for cols in (slice(0, P), slice(P, 2 * P), halves[1]):
-            ds1_half(cols)
-        last = product(3, qm0, E4M3, 3, ds0, E5M2)
+        dk0.append(key_gradient(0, 2, qm0, ds0, "tanh2", 2))
+        ds1_half(slice(0, P))
+        ds1_half(slice(P, 2 * P))
+        ds1_half(halves[1])
+        last = product(0, qm0, E4M3, 3, ds0, E5M2)
         last_a = keep.tile([P, W // 2], F32, name="last_a", tag="v1_scales", align_bytes=64)
         nc.scalar.copy(out=last_a[:], in_=last[:, halves[0]])
         qm1 = prepared("qm1", "scalar", load_rows(qm[1], "slot8"), E4M3, slot="do1_codes")
@@ -252,7 +257,7 @@ def tile_attend_gat_sig_k_kernel(tc, qT, kT, vT, doT, rw, qm, offs, out):
         quantize(ds1, ds_group, E5M2)
         last_b = keep.tile([P, W // 2], F32, name="last_b", tag="slot5", align_bytes=64)
         nc.scalar.copy(out=last_b[:], in_=last[:, halves[1]])
-        dk1 = [key_gradient(1, j, qm1, ds1, "dk1_%d" % j) for j in range(D // P)]
+        dk1 = [key_gradient(1, j, qm1, ds1, "dk1_%d" % j, PACK + j) for j in range(D // P)]
 
         for j in range(D // P - 1):
             nc.vector.tensor_copy(out=windows[j][:].indirect(seq_list(0)), in_=dk0[j][:])

@@ -30,6 +30,8 @@ def tile_attend_gat_sig_k_kernel(tc, qT, kT, vT, doT, rw, qm, offs, out):
         groups = ctx.enter_context(tc.tile_pool(name="groups", bufs=3))
         psum = ctx.enter_context(tc.psum_pool(name="psum", bufs=1))
 
+        first_plane = keep.tile([P, T], F32, name="plane", tag="slot0", align_bytes=64)
+        nc.sync.dma_start(first_plane[:], kT.rearrange("(p t) n -> p t n", t=PACK)[:, 0, :])
         offsets = keep.tile([P, B * LIST_COLS], U16, name="offsets")
         nc.sync.dma_start(offsets[:], offs)
 
@@ -131,7 +133,7 @@ def tile_attend_gat_sig_k_kernel(tc, qT, kT, vT, doT, rw, qm, offs, out):
 
         def gather_pool(pool_dram, gathered, first_slot):
             for t in range(PACK - 1):
-                plane = load_plane(pool_dram, t, "slot%d" % (first_slot + t))
+                plane = first_plane if t == 0 else load_plane(pool_dram, t, "slot%d" % (first_slot + t))
                 nc.vector.tensor_copy(out=gathered[:, t, :], in_=plane[:].indirect(offsets[:]))
             plane = load_plane(pool_dram, PACK - 1, "slot%d" % (first_slot + PACK - 1))
             nc.vector.tensor_copy(out=gathered[:, PACK - 1, 0:N], in_=plane[:].indirect(seq_list(0)))
@@ -143,10 +145,10 @@ def tile_attend_gat_sig_k_kernel(tc, qT, kT, vT, doT, rw, qm, offs, out):
         k_last = gather_pool(kT, keys, 0)
         gather_rest(k_last, keys)
         q_raw = load_rows(qT[0], "slot8")
-        gate = keep.tile([P, B, PACK], F32, name="gate")
-        nc.sync.dma_start(gate[:], rw.rearrange("b (p t) o -> p b (t o)", t=PACK))
-        gate_pos = keep.tile([P, B, PACK], F32, name="gate_pos")
-        gate_neg = keep.tile([P, B, PACK], F32, name="gate_neg")
+        gate = keep.tile([P, PACK], F32, name="gate")
+        nc.sync.dma_start(gate[:], rw[0].rearrange("(p t) o -> p (t o)", t=PACK))
+        gate_pos = keep.tile([P, PACK], F32, name="gate_pos")
+        gate_neg = keep.tile([P, PACK], F32, name="gate_neg")
         nc.scalar.activation(out=gate_pos[:], in_=gate[:], func=ACT.Copy, scale=0.25)
         nc.scalar.activation(out=gate_neg[:], in_=gate[:], func=ACT.Copy, scale=-0.25)
 
@@ -165,8 +167,8 @@ def tile_attend_gat_sig_k_kernel(tc, qT, kT, vT, doT, rw, qm, offs, out):
             tanh_squared(weight[t][:], t, t, q0, k0)
         for t in range(PACK):
             nc.gpsimd.tensor_scalar(
-                out=weight[t][:], in0=weight[t][:], scalar1=gate_neg[:, 0, t : t + 1],
-                scalar2=gate_pos[:, 0, t : t + 1], op0=ALU.mult, op1=ALU.add,
+                out=weight[t][:], in0=weight[t][:], scalar1=gate_neg[:, t : t + 1],
+                scalar2=gate_pos[:, t : t + 1], op0=ALU.mult, op1=ALU.add,
             )
 
         for t in range(2):
@@ -229,15 +231,18 @@ def tile_attend_gat_sig_k_kernel(tc, qT, kT, vT, doT, rw, qm, offs, out):
             if t == 1:
                 dk0.append(key_gradient(0, 1, qm0, ds0, "tanh0", 1))
         for t in range(PACK):
-            nc.gpsimd.tensor_scalar(out=sq[:, t, :], in0=sq[:, t, :], scalar1=1.0, scalar2=-1.0, op0=ALU.mult, op1=ALU.add)
+            nc.gpsimd.tensor_scalar(out=sq[:, t, :], in0=sq[:, t, :], scalar1=-0.25, scalar2=0.25, op0=ALU.mult, op1=ALU.add)
         gated = keep.tile([P, PACK, W], F32, name="gated", tag="slot5", align_bytes=64)
         dp1 = [product(bank, do1, E5M2, t, v1, E4M3) for t, bank in enumerate((5, 6, 7, 3))]
+        qm1_raw = load_rows(qm[1], "slot8")
+        gate1 = keep.tile([P, PACK], F32, name="gate1")
+        nc.sync.dma_start(gate1[:], rw[1].rearrange("(p t) o -> p (t o)", t=PACK))
         ds_group = new_group()
         halves = (slice(0, W // 2), slice(W // 2, W))
 
         def ds1_half(cols):
             for t in range(PACK):
-                nc.scalar.activation(out=gated[:, t, cols], in_=dp1[t][:, cols], func=ACT.Copy, scale=gate_neg[:, 1, t : t + 1])
+                nc.scalar.activation(out=gated[:, t, cols], in_=dp1[t][:, cols], func=ACT.Copy, scale=gate1[:, t : t + 1])
             nc.gpsimd.tensor_tensor(
                 out=ds_group[:, cols.start * PACK : cols.stop * PACK].rearrange("p (c i t) -> p c t i", i=4, t=PACK),
                 in0=sq[:, :, cols].rearrange("p t (c i) -> p c t i", i=4),
@@ -252,7 +257,7 @@ def tile_attend_gat_sig_k_kernel(tc, qT, kT, vT, doT, rw, qm, offs, out):
         last = product(0, qm0, E4M3, 3, ds0, E5M2)
         last_a = keep.tile([P, W // 2], F32, name="last_a", tag="v1_scales", align_bytes=64)
         nc.scalar.copy(out=last_a[:], in_=last[:, halves[0]])
-        qm1 = prepared("qm1", "scalar", load_rows(qm[1], "slot8"), E4M3, slot="do1_codes")
+        qm1 = prepared("qm1", "scalar", qm1_raw, E4M3, slot="do1_codes")
         ds1 = new_operand("ds1")
         quantize(ds1, ds_group, E5M2)
         last_b = keep.tile([P, W // 2], F32, name="last_b", tag="slot5", align_bytes=64)

@@ -230,8 +230,9 @@ def tile_attend_gat_sig_k_kernel(tc, qT, kT, vT, doT, rw, qm, offs, out):
             tanh_squared(sq[:, t, :], t, 1 + t, q1, k1)
             if t == 1:
                 dk0.append(key_gradient(0, 1, qm0, ds0, "tanh0", 1))
-        for t in range(PACK):
-            nc.gpsimd.tensor_scalar(out=sq[:, t, :], in0=sq[:, t, :], scalar1=-0.25, scalar2=0.25, op0=ALU.mult, op1=ALU.add)
+        factor = keep.tile([P, PACK, W], F32, name="factor1", tag="group_do1", align_bytes=64)
+        for u in range(2):
+            nc.gpsimd.tensor_scalar(out=factor[:, 2 * u : 2 * u + 2, :], in0=sq[:, 2 * u : 2 * u + 2, :], scalar1=-0.25, scalar2=0.25, op0=ALU.mult, op1=ALU.add)
         gated = keep.tile([P, PACK, W], F32, name="gated", tag="slot5", align_bytes=64)
         dp1 = [product(bank, do1, E5M2, t, v1, E4M3) for t, bank in enumerate((5, 6, 7, 3))]
         qm1_raw = load_rows(qm[1], "slot8")
@@ -245,7 +246,7 @@ def tile_attend_gat_sig_k_kernel(tc, qT, kT, vT, doT, rw, qm, offs, out):
                 nc.scalar.activation(out=gated[:, t, cols], in_=dp1[t][:, cols], func=ACT.Copy, scale=gate1[:, t : t + 1])
             nc.gpsimd.tensor_tensor(
                 out=ds_group[:, cols.start * PACK : cols.stop * PACK].rearrange("p (c i t) -> p c t i", i=4, t=PACK),
-                in0=sq[:, :, cols].rearrange("p t (c i) -> p c t i", i=4),
+                in0=factor[:, :, cols].rearrange("p t (c i) -> p c t i", i=4),
                 in1=gated[:, :, cols].rearrange("p t (c i) -> p c t i", i=4),
                 op=ALU.mult,
             )

@@ -20,14 +20,16 @@ PACK = 4
 W = 512
 LIST_COLS = N // 16
 DO0_SPLIT = 64
-V0_ON_SCALAR = 288
+TAIL_ON_SCALAR = 256
+K_TAIL_ON_SCALAR = 320
+Q0_ON_VECTOR = 88
 
 
 def tile_attend_gat_sig_k_kernel(tc, qT, kT, vT, doT, rw, qm, offs, out):
     nc = tc.nc
     with ExitStack() as ctx:
         keep = ctx.enter_context(tc.tile_pool(name="keep", bufs=1))
-        groups = ctx.enter_context(tc.tile_pool(name="groups", bufs=3))
+        groups = ctx.enter_context(tc.tile_pool(name="groups", bufs=1))
         psum = ctx.enter_context(tc.psum_pool(name="psum", bufs=1))
 
         first_plane = keep.tile([P, T], F32, name="plane", tag="slot0", align_bytes=64)
@@ -65,11 +67,11 @@ def tile_attend_gat_sig_k_kernel(tc, qT, kT, vT, doT, rw, qm, offs, out):
             else:
                 nc.scalar.copy(out=dst, in_=src)
 
-        def interleave(engine, group, src, c0=0, c1=W):
+        def interleave(engine, group, src, c0=0, c1=W, j0=0, j1=PACK):
             copy_on(
                 engine,
-                group[:, c0 * PACK : c1 * PACK].rearrange("p (c i j) -> p c j i", i=4, j=PACK),
-                src[:, :, c0:c1].rearrange("p j (c i) -> p c j i", i=4),
+                group[:, c0 * PACK : c1 * PACK].rearrange("p (c i j) -> p c j i", i=4, j=PACK)[:, :, j0:j1],
+                src[:, j0:j1, c0:c1].rearrange("p j (c i) -> p c j i", i=4),
             )
 
         def interleave_queries(engine, group, src, m0=0, m1=P):
@@ -145,21 +147,25 @@ def tile_attend_gat_sig_k_kernel(tc, qT, kT, vT, doT, rw, qm, offs, out):
         k_last = gather_pool(kT, keys, 0)
         gather_rest(k_last, keys)
         q_raw = load_rows(qT[0], "slot8")
-        gate = keep.tile([P, PACK], F32, name="gate")
+        gate = keep.tile([P, PACK], F32, name="gate", tag="group_k1", align_bytes=64)
         nc.sync.dma_start(gate[:], rw[0].rearrange("(p t) o -> p (t o)", t=PACK))
+
+        kq_group = keep.tile([P, 2 * W * PACK], BF16, name="kq_group", align_bytes=64)
+        k_group, q_group = kq_group[:, 0 : W * PACK], kq_group[:, W * PACK : 2 * W * PACK]
+        interleave("scalar", k_group, keys[:, :, 0:N], j1=2)
+        interleave("scalar", k_group, keys[:, :, 0:N], 0, K_TAIL_ON_SCALAR, j0=2)
+        interleave("gpsimd", k_group, keys[:, :, 0:N], K_TAIL_ON_SCALAR, W, j0=2)
+        interleave_queries("vector", q_group, q_raw, 0, Q0_ON_VECTOR)
+        interleave_queries("scalar", q_group, q_raw, Q0_ON_VECTOR, P)
+        kq_codes = keep.tile([P, 2 * W], U32, name="kq_codes", align_bytes=64)
+        kq_scales = keep.tile([P, 2 * W], U8, name="kq_scales", align_bytes=64)
+        nc.vector.quantize_mx(out=kq_codes[:].bitcast(E4M3), scales=kq_scales[:], in_=kq_group[:])
+        k0 = (kq_codes[:, 0:W], kq_scales[:, 0:W])
+        q0 = (kq_codes[:, W : 2 * W], kq_scales[:, W : 2 * W])
         gate_pos = keep.tile([P, PACK], F32, name="gate_pos")
         gate_neg = keep.tile([P, PACK], F32, name="gate_neg")
         nc.scalar.activation(out=gate_pos[:], in_=gate[:], func=ACT.Copy, scale=0.25)
         nc.scalar.activation(out=gate_neg[:], in_=gate[:], func=ACT.Copy, scale=-0.25)
-
-        k_group = new_group()
-        interleave("scalar", k_group, keys[:, :, 0:N])
-        q_group = new_group()
-        interleave_queries("vector", q_group, q_raw)
-        k0 = new_operand("k0")
-        quantize(k0, k_group, E4M3)
-        q0 = new_operand("q0")
-        quantize(q0, q_group, E4M3)
         k1_group = new_group("group_k1")
         interleave("scalar", k1_group, keys[:, :, N : 2 * N])
         weight = [keep.tile([P, W], F32, name="weight0_%d" % t, tag="weight0_%d" % t, align_bytes=64) for t in range(PACK)]
@@ -171,21 +177,15 @@ def tile_attend_gat_sig_k_kernel(tc, qT, kT, vT, doT, rw, qm, offs, out):
                 scalar2=gate_pos[:, t : t + 1], op0=ALU.mult, op1=ALU.add,
             )
 
-        for t in range(2):
+        for t in range(PACK):
             plane = load_plane(vT, t, "slot%d" % (PACK + t))
             for b in range(B):
                 nc.vector.tensor_copy(out=values[b][:, t, :], in_=plane[:].indirect(seq_list(b)))
-        v_late = keep.tile([P, 2 * T], F32, name="v_late", tag="slot7", align_bytes=64)
-        for t in range(2):
-            nc.sync.dma_start(v_late[:, t * T : (t + 1) * T], vT.rearrange("(p t) n -> p t n", t=PACK)[:, 2 + t, :])
-        for t in range(2):
-            nc.vector.tensor_copy(out=values[0][:, 2 + t, :], in_=v_late[:, t * T : (t + 1) * T].indirect(seq_list(0)))
-        nc.vector.tensor_copy(out=values[1][:, 2, :], in_=v_late[:].indirect(seq_list(1)))
-        nc.vector.tensor_copy(out=values[1][:, 3, :], in_=v_late[:, T : 2 * T].indirect(seq_list(1)))
         do_raw = load_rows(doT[0], "slot0")
         v_group = new_group("group_v0")
-        interleave("scalar", v_group, values[0], 0, V0_ON_SCALAR)
-        interleave("gpsimd", v_group, values[0], V0_ON_SCALAR, W)
+        interleave("scalar", v_group, values[0], j1=2)
+        interleave("scalar", v_group, values[0], 0, TAIL_ON_SCALAR, j0=2)
+        interleave("gpsimd", v_group, values[0], TAIL_ON_SCALAR, W, j0=2)
         do_halves = [keep.tile([P, W * 2], BF16, name="do_half", tag="do_half%d" % u, align_bytes=64) for u in range(2)]
         for engine, u, m0, m1 in (("scalar", 0, 0, P), ("scalar", 1, 0, DO0_SPLIT), ("vector", 1, DO0_SPLIT, P)):
             copy_on(
@@ -206,34 +206,54 @@ def tile_attend_gat_sig_k_kernel(tc, qT, kT, vT, doT, rw, qm, offs, out):
         for t in range(PACK):
             dp = product(PACK + t, do0, E5M2, t, v0, E4M3)
             nc.vector.tensor_tensor(out=ds_planes[:, t, :], in0=dp[:], in1=weight[t][:], op=ALU.mult)
-        qm0 = prepared("qm0", "scalar", load_rows(qm[0], "slot1"), E4M3, slot="group_qm0", codes_slot="weight0_2")
+        q1_raw = load_rows(qT[1], "slot1")
+        qm0_raw = load_rows(qm[0], "slot2")
+        do1_raw = load_rows(doT[1], "slot3")
+        q1_group = new_group("group_v0")
+        interleave_queries("scalar", q1_group, q1_raw)
+        qm0_group = new_group("group_qm0")
+        interleave("scalar", qm0_group, qm0_raw, 0, 2 * P)
+        interleave("scalar", qm0_group, qm0_raw, 2 * P, 3 * P)
         ds_group = new_group("group_ds0")
         interleave("vector", ds_group, ds_planes)
+        qm0 = new_operand("qm0", "weight0_3")
+        quantize(qm0, qm0_group, E4M3, 0, 2 * P)
         ds0 = new_operand("ds0")
         quantize(ds0, ds_group, E5M2)
 
-        q1 = prepared("q1", "scalar", load_rows(qT[1], "slot2"), E4M3, queries=True, slot="group_v0")
-        do1_raw = load_rows(doT[1], "slot3")
+        q1 = new_operand("q1", "slot5")
+        quantize(q1, q1_group, E4M3)
+        v1 = new_operand("v1", "group_ds0")
+
+        def v1_half(u):
+            interleave("gpsimd", v1_halves[u], values[1][:, :, u * W // 2 : (u + 1) * W // 2], 0, W // 2)
+            cols = slice(u * W // 2, (u + 1) * W // 2)
+            nc.vector.quantize_mx(out=v1[0][:, cols].bitcast(E4M3), scales=v1[1][:, cols], in_=v1_halves[u][:, 0 : W * 2])
+
+        v1_half(0)
+        quantize(qm0, qm0_group, E4M3, 2 * P, 3 * P)
         do1_group = new_group("group_do1")
         interleave_queries("scalar", do1_group, do1_raw)
         do1 = new_operand("do1")
         quantize(do1, do1_group, E5M2)
-        dk0 = [key_gradient(0, 0, qm0, ds0, "dk0_0", 0)]
+        after_do1 = keep.tile([P, PACK, W], F32, name="after_do1", tag="slot3", align_bytes=64)
+        first = product(0, qm0, E4M3, 0, ds0, E5M2)
+        nc.scalar.copy(out=after_do1[:, 0, :], in_=first[:])
+        dk0 = [after_do1[:, 0, :]]
         v1_halves.append(keep.tile([P, W * 2], BF16, name="v1_late", tag="group_do1", align_bytes=64))
-        v1 = new_operand("v1", "weight0_3")
-        for u in range(2):
-            interleave("gpsimd", v1_halves[u], values[1][:, :, u * W // 2 : (u + 1) * W // 2], 0, W // 2)
-            cols = slice(u * W // 2, (u + 1) * W // 2)
-            nc.vector.quantize_mx(out=v1[0][:, cols].bitcast(E4M3), scales=v1[1][:, cols], in_=v1_halves[u][:, 0 : W * 2])
+        v1_half(1)
         sq = keep.tile([P, PACK, W], F32, name="weight1", tag="slot4", align_bytes=64)
         for t in range(PACK):
-            tanh_squared(sq[:, t, :], t, 1 + t, q1, k1)
+            a = product(1 + t, q1, E4M3, t, k1, E4M3)
+            th = after_do1[:, 1 + t % 3, :]
+            nc.scalar.activation(out=th, in_=a[:], func=ACT.Tanh, scale=0.5)
+            nc.scalar.activation(out=sq[:, t, :], in_=th, func=ACT.Square)
             if t == 1:
-                dk0.append(key_gradient(0, 1, qm0, ds0, "tanh0", 1))
+                dk0.append(key_gradient(0, 1, qm0, ds0, "dk0_1", 0)[:])
         factor = keep.tile([P, PACK, W], F32, name="factor1", tag="group_do1", align_bytes=64)
-        for u in range(2):
-            nc.gpsimd.tensor_scalar(out=factor[:, 2 * u : 2 * u + 2, :], in0=sq[:, 2 * u : 2 * u + 2, :], scalar1=-0.25, scalar2=0.25, op0=ALU.mult, op1=ALU.add)
-        gated = keep.tile([P, PACK, W], F32, name="gated", tag="slot5", align_bytes=64)
+        for t in range(PACK):
+            nc.gpsimd.tensor_scalar(out=factor[:, t, :], in0=sq[:, t, :], scalar1=-0.25, scalar2=0.25, op0=ALU.mult, op1=ALU.add)
+        gated = keep.tile([P, PACK, W], F32, name="gated", tag="slot6", align_bytes=64)
         dp1 = [product(bank, do1, E5M2, t, v1, E4M3) for t, bank in enumerate((5, 6, 7, 3))]
         qm1_raw = load_rows(qm[1], "slot8")
         gate1 = keep.tile([P, PACK], F32, name="gate1")
@@ -251,7 +271,12 @@ def tile_attend_gat_sig_k_kernel(tc, qT, kT, vT, doT, rw, qm, offs, out):
                 op=ALU.mult,
             )
 
-        dk0.append(key_gradient(0, 2, qm0, ds0, "tanh2", 2))
+        qm0_last = after_do1[:, 3, 0 : W // 2].bitcast(BF16)
+        interleave("scalar", qm0_last, qm0_raw[:, :, 3 * P : W], 0, P)
+        nc.vector.quantize_mx(out=qm0[0][:, 3 * P : W].bitcast(E4M3), scales=qm0[1][:, 3 * P : W], in_=qm0_last)
+        third = product(2, qm0, E4M3, 2, ds0, E5M2)
+        nc.scalar.copy(out=after_do1[:, 1, :], in_=third[:])
+        dk0.append(after_do1[:, 1, :])
         ds1_half(slice(0, P))
         ds1_half(slice(P, 2 * P))
         ds1_half(halves[1])
@@ -259,16 +284,25 @@ def tile_attend_gat_sig_k_kernel(tc, qT, kT, vT, doT, rw, qm, offs, out):
         last_a = keep.tile([P, W // 2], F32, name="last_a", tag="v1_scales", align_bytes=64)
         nc.scalar.copy(out=last_a[:], in_=last[:, halves[0]])
         qm1 = prepared("qm1", "scalar", qm1_raw, E4M3, slot="do1_codes")
-        ds1 = new_operand("ds1")
+        ds1 = new_operand("ds1", "slot8")
         quantize(ds1, ds_group, E5M2)
-        last_b = keep.tile([P, W // 2], F32, name="last_b", tag="slot5", align_bytes=64)
+        last_b = keep.tile([P, W // 2], F32, name="last_b", tag="slot6", align_bytes=64)
         nc.scalar.copy(out=last_b[:], in_=last[:, halves[1]])
-        dk1 = [key_gradient(1, j, qm1, ds1, "dk1_%d" % j, PACK + j) for j in range(D // P)]
+        opening = product(PACK, qm1, E4M3, 0, ds1, E5M2)
+        opening_halves = [keep.tile([P, W // 2], F32, name="opening%d" % u, align_bytes=64) for u in range(2)]
+        nc.scalar.copy(out=opening_halves[0][:], in_=opening[:, halves[0]])
+        dk1 = [key_gradient(1, 1, qm1, ds1, "dk1_1", PACK + 1)]
+        nc.scalar.copy(out=opening_halves[1][:], in_=opening[:, halves[1]])
+        dk1.extend(key_gradient(1, j, qm1, ds1, "dk1_%d" % j, PACK + j) for j in range(2, D // P))
 
         for j in range(D // P - 1):
-            nc.vector.tensor_copy(out=windows[j][:].indirect(seq_list(0)), in_=dk0[j][:])
+            nc.vector.tensor_copy(out=windows[j][:].indirect(seq_list(0)), in_=dk0[j])
         nc.vector.tensor_copy(out=windows[3][:].indirect(offsets[:, 0 : LIST_COLS // 2]), in_=last_a[:])
         nc.vector.tensor_copy(out=windows[3][:].indirect(offsets[:, LIST_COLS // 2 : LIST_COLS]), in_=last_b[:])
-        for j in range(D // P):
-            nc.vector.tensor_copy(out=windows[j][:].indirect(seq_list(1)), in_=dk1[j][:])
+        nc.vector.tensor_copy(out=windows[0][:].indirect(offsets[:, LIST_COLS : 3 * LIST_COLS // 2]), in_=opening_halves[0][:])
+        for j in range(1, D // P):
+            nc.vector.tensor_copy(out=windows[j][:].indirect(seq_list(1)), in_=dk1[j - 1][:])
             nc.sync.dma_start(out[j * P : (j + 1) * P, :], windows[j][:])
+            if j == 1:
+                nc.vector.tensor_copy(out=windows[0][:].indirect(offsets[:, 3 * LIST_COLS // 2 : 2 * LIST_COLS]), in_=opening_halves[1][:])
+                nc.sync.dma_start(out[0:P, :], windows[0][:])

@@ -20,9 +20,8 @@ PACK = 4
 W = 512
 LIST_COLS = N // 16
 DO0_SPLIT = 64
-TAIL_ON_SCALAR = 256
-K_TAIL_ON_SCALAR = 320
-Q0_ON_VECTOR = 88
+V0_ON_SCALAR = 288
+K0_ON_SCALAR = 416
 
 
 def tile_attend_gat_sig_k_kernel(tc, qT, kT, vT, doT, rw, qm, offs, out):
@@ -67,11 +66,11 @@ def tile_attend_gat_sig_k_kernel(tc, qT, kT, vT, doT, rw, qm, offs, out):
             else:
                 nc.scalar.copy(out=dst, in_=src)
 
-        def interleave(engine, group, src, c0=0, c1=W, j0=0, j1=PACK):
+        def interleave(engine, group, src, c0=0, c1=W):
             copy_on(
                 engine,
-                group[:, c0 * PACK : c1 * PACK].rearrange("p (c i j) -> p c j i", i=4, j=PACK)[:, :, j0:j1],
-                src[:, j0:j1, c0:c1].rearrange("p j (c i) -> p c j i", i=4),
+                group[:, c0 * PACK : c1 * PACK].rearrange("p (c i j) -> p c j i", i=4, j=PACK),
+                src[:, :, c0:c1].rearrange("p j (c i) -> p c j i", i=4),
             )
 
         def interleave_queries(engine, group, src, m0=0, m1=P):
@@ -152,11 +151,9 @@ def tile_attend_gat_sig_k_kernel(tc, qT, kT, vT, doT, rw, qm, offs, out):
 
         kq_group = keep.tile([P, 2 * W * PACK], BF16, name="kq_group", align_bytes=64)
         k_group, q_group = kq_group[:, 0 : W * PACK], kq_group[:, W * PACK : 2 * W * PACK]
-        interleave("scalar", k_group, keys[:, :, 0:N], j1=2)
-        interleave("scalar", k_group, keys[:, :, 0:N], 0, K_TAIL_ON_SCALAR, j0=2)
-        interleave("gpsimd", k_group, keys[:, :, 0:N], K_TAIL_ON_SCALAR, W, j0=2)
-        interleave_queries("vector", q_group, q_raw, 0, Q0_ON_VECTOR)
-        interleave_queries("scalar", q_group, q_raw, Q0_ON_VECTOR, P)
+        interleave("scalar", k_group, keys[:, :, 0:N], 0, K0_ON_SCALAR)
+        interleave("gpsimd", k_group, keys[:, :, 0:N], K0_ON_SCALAR, W)
+        interleave_queries("vector", q_group, q_raw)
         kq_codes = keep.tile([P, 2 * W], U32, name="kq_codes", align_bytes=64)
         kq_scales = keep.tile([P, 2 * W], U8, name="kq_scales", align_bytes=64)
         nc.vector.quantize_mx(out=kq_codes[:].bitcast(E4M3), scales=kq_scales[:], in_=kq_group[:])
@@ -177,15 +174,21 @@ def tile_attend_gat_sig_k_kernel(tc, qT, kT, vT, doT, rw, qm, offs, out):
                 scalar2=gate_pos[:, t : t + 1], op0=ALU.mult, op1=ALU.add,
             )
 
-        for t in range(PACK):
+        for t in range(2):
             plane = load_plane(vT, t, "slot%d" % (PACK + t))
             for b in range(B):
                 nc.vector.tensor_copy(out=values[b][:, t, :], in_=plane[:].indirect(seq_list(b)))
+        v_late = keep.tile([P, 2 * T], F32, name="v_late", tag="slot7", align_bytes=64)
+        for t in range(2):
+            nc.sync.dma_start(v_late[:, t * T : (t + 1) * T], vT.rearrange("(p t) n -> p t n", t=PACK)[:, 2 + t, :])
+        for t in range(2):
+            nc.vector.tensor_copy(out=values[0][:, 2 + t, :], in_=v_late[:, t * T : (t + 1) * T].indirect(seq_list(0)))
+        nc.vector.tensor_copy(out=values[1][:, 2, :], in_=v_late[:].indirect(seq_list(1)))
+        nc.vector.tensor_copy(out=values[1][:, 3, :], in_=v_late[:, T : 2 * T].indirect(seq_list(1)))
         do_raw = load_rows(doT[0], "slot0")
         v_group = new_group("group_v0")
-        interleave("scalar", v_group, values[0], j1=2)
-        interleave("scalar", v_group, values[0], 0, TAIL_ON_SCALAR, j0=2)
-        interleave("gpsimd", v_group, values[0], TAIL_ON_SCALAR, W, j0=2)
+        interleave("scalar", v_group, values[0], 0, V0_ON_SCALAR)
+        interleave("gpsimd", v_group, values[0], V0_ON_SCALAR, W)
         do_halves = [keep.tile([P, W * 2], BF16, name="do_half", tag="do_half%d" % u, align_bytes=64) for u in range(2)]
         for engine, u, m0, m1 in (("scalar", 0, 0, P), ("scalar", 1, 0, DO0_SPLIT), ("vector", 1, DO0_SPLIT, P)):
             copy_on(
@@ -253,7 +256,7 @@ def tile_attend_gat_sig_k_kernel(tc, qT, kT, vT, doT, rw, qm, offs, out):
         factor = keep.tile([P, PACK, W], F32, name="factor1", tag="group_do1", align_bytes=64)
         for t in range(PACK):
             nc.gpsimd.tensor_scalar(out=factor[:, t, :], in0=sq[:, t, :], scalar1=-0.25, scalar2=0.25, op0=ALU.mult, op1=ALU.add)
-        gated = keep.tile([P, PACK, W], F32, name="gated", tag="slot6", align_bytes=64)
+        gated = keep.tile([P, PACK, W], F32, name="gated", tag="slot7", align_bytes=64)
         dp1 = [product(bank, do1, E5M2, t, v1, E4M3) for t, bank in enumerate((5, 6, 7, 3))]
         qm1_raw = load_rows(qm[1], "slot8")
         gate1 = keep.tile([P, PACK], F32, name="gate1")
@@ -286,7 +289,7 @@ def tile_attend_gat_sig_k_kernel(tc, qT, kT, vT, doT, rw, qm, offs, out):
         qm1 = prepared("qm1", "scalar", qm1_raw, E4M3, slot="do1_codes")
         ds1 = new_operand("ds1", "slot8")
         quantize(ds1, ds_group, E5M2)
-        last_b = keep.tile([P, W // 2], F32, name="last_b", tag="slot6", align_bytes=64)
+        last_b = keep.tile([P, W // 2], F32, name="last_b", tag="slot7", align_bytes=64)
         nc.scalar.copy(out=last_b[:], in_=last[:, halves[1]])
         opening = product(PACK, qm1, E4M3, 0, ds1, E5M2)
         opening_halves = [keep.tile([P, W // 2], F32, name="opening%d" % u, align_bytes=64) for u in range(2)]

@@ -22,6 +22,8 @@ LIST_COLS = N // 16
 DO0_SPLIT = 64
 V0_ON_SCALAR = 288
 K0_ON_SCALAR = 416
+RUN = 272
+V1_ON_GPSIMD = 192
 
 
 def tile_attend_gat_sig_k_kernel(tc, qT, kT, vT, doT, rw, qm, offs, out):
@@ -130,7 +132,8 @@ def tile_attend_gat_sig_k_kernel(tc, qT, kT, vT, doT, rw, qm, offs, out):
             return dk
 
         keys = keep.tile([P, PACK, B * N], F32, name="keys")
-        values = [keep.tile([P, PACK, N], F32, name="values%d" % b, align_bytes=64) for b in range(B)]
+        values0 = keep.tile([P, PACK, N], F32, name="values0", align_bytes=64)
+        values1 = keep.tile([P, PACK, 2, RUN], BF16, name="values1", align_bytes=64)
 
         def gather_pool(pool_dram, gathered, first_slot):
             for t in range(PACK - 1):
@@ -176,19 +179,19 @@ def tile_attend_gat_sig_k_kernel(tc, qT, kT, vT, doT, rw, qm, offs, out):
 
         for t in range(2):
             plane = load_plane(vT, t, "slot%d" % (PACK + t))
-            for b in range(B):
-                nc.vector.tensor_copy(out=values[b][:, t, :], in_=plane[:].indirect(seq_list(b)))
+            nc.vector.tensor_copy(out=values0[:, t, :], in_=plane[:].indirect(seq_list(0)))
+            nc.vector.tensor_copy(out=values1[:, t, :, 0 : N // 2], in_=plane[:].indirect(seq_list(1)))
         v_late = keep.tile([P, 2 * T], F32, name="v_late", tag="slot7", align_bytes=64)
         for t in range(2):
             nc.sync.dma_start(v_late[:, t * T : (t + 1) * T], vT.rearrange("(p t) n -> p t n", t=PACK)[:, 2 + t, :])
         for t in range(2):
-            nc.vector.tensor_copy(out=values[0][:, 2 + t, :], in_=v_late[:, t * T : (t + 1) * T].indirect(seq_list(0)))
-        nc.vector.tensor_copy(out=values[1][:, 2, :], in_=v_late[:].indirect(seq_list(1)))
-        nc.vector.tensor_copy(out=values[1][:, 3, :], in_=v_late[:, T : 2 * T].indirect(seq_list(1)))
+            nc.vector.tensor_copy(out=values0[:, 2 + t, :], in_=v_late[:, t * T : (t + 1) * T].indirect(seq_list(0)))
+        nc.vector.tensor_copy(out=values1[:, 2, :, 0 : N // 2], in_=v_late[:].indirect(seq_list(1)))
+        nc.vector.tensor_copy(out=values1[:, 3, :, 0 : N // 2], in_=v_late[:, T : 2 * T].indirect(seq_list(1)))
         do_raw = load_rows(doT[0], "slot0")
         v_group = new_group("group_v0")
-        interleave("scalar", v_group, values[0], 0, V0_ON_SCALAR)
-        interleave("gpsimd", v_group, values[0], V0_ON_SCALAR, W)
+        interleave("scalar", v_group, values0, 0, V0_ON_SCALAR)
+        interleave("gpsimd", v_group, values0, V0_ON_SCALAR, W)
         do_halves = [keep.tile([P, W * 2], BF16, name="do_half", tag="do_half%d" % u, align_bytes=64) for u in range(2)]
         for engine, u, m0, m1 in (("scalar", 0, 0, P), ("scalar", 1, 0, DO0_SPLIT), ("vector", 1, DO0_SPLIT, P)):
             copy_on(
@@ -205,7 +208,10 @@ def tile_attend_gat_sig_k_kernel(tc, qT, kT, vT, doT, rw, qm, offs, out):
         k1 = new_operand("k1", "slot0")
         quantize(k1, k1_group, E4M3)
         ds_planes = keep.tile([P, PACK, W], F32, name="ds_planes", tag="slot5", align_bytes=64)
-        v1_halves = [keep.tile([P, W * 2], BF16, name="v1_early", tag="group_k1", align_bytes=64)]
+        v1_group = new_group("group_k1")
+        v1_dst = v1_group[:].rearrange("p (h c j) -> p h c j", h=2, j=PACK)
+        v1_src = values1[:, :, :, 0 : N // 2].rearrange("p j h c -> p h c j")
+        copy_on("gpsimd", v1_dst[:, :, 0:V1_ON_GPSIMD], v1_src[:, :, 0:V1_ON_GPSIMD])
         for t in range(PACK):
             dp = product(PACK + t, do0, E5M2, t, v0, E4M3)
             nc.vector.tensor_tensor(out=ds_planes[:, t, :], in0=dp[:], in1=weight[t][:], op=ALU.mult)
@@ -214,50 +220,47 @@ def tile_attend_gat_sig_k_kernel(tc, qT, kT, vT, doT, rw, qm, offs, out):
         do1_raw = load_rows(doT[1], "slot3")
         q1_group = new_group("group_v0")
         interleave_queries("scalar", q1_group, q1_raw)
-        qm0_group = new_group("group_qm0")
-        interleave("scalar", qm0_group, qm0_raw, 0, 2 * P)
-        interleave("scalar", qm0_group, qm0_raw, 2 * P, 3 * P)
+        qm0_early = keep.tile([P, W * 2], BF16, name="qm0_early", align_bytes=64)
+        interleave("scalar", qm0_early, qm0_raw, 0, W // 2)
+        copy_on("scalar", v1_dst[:, :, V1_ON_GPSIMD : N // 2], v1_src[:, :, V1_ON_GPSIMD : N // 2])
+        q1 = new_operand("q1", "weight0_2")
+        quantize(q1, q1_group, E4M3)
         ds_group = new_group("group_ds0")
         interleave("vector", ds_group, ds_planes)
-        qm0 = new_operand("qm0", "weight0_3")
-        quantize(qm0, qm0_group, E4M3, 0, 2 * P)
+        qm0 = new_operand("qm0")
+        quantize(qm0, qm0_early, E4M3, 0, W // 2)
         ds0 = new_operand("ds0")
         quantize(ds0, ds_group, E5M2)
 
-        q1 = new_operand("q1", "slot5")
-        quantize(q1, q1_group, E4M3)
-        v1 = new_operand("v1", "group_ds0")
-
-        def v1_half(u):
-            interleave("gpsimd", v1_halves[u], values[1][:, :, u * W // 2 : (u + 1) * W // 2], 0, W // 2)
-            cols = slice(u * W // 2, (u + 1) * W // 2)
-            nc.vector.quantize_mx(out=v1[0][:, cols].bitcast(E4M3), scales=v1[1][:, cols], in_=v1_halves[u][:, 0 : W * 2])
-
-        v1_half(0)
-        quantize(qm0, qm0_group, E4M3, 2 * P, 3 * P)
-        do1_group = new_group("group_do1")
+        v1 = new_operand("v1", "weight0_3")
+        quantize(v1, v1_group, E4M3)
+        factor = keep.tile([P, PACK, W], F32, name="factor1", tag="slot6", align_bytes=64)
+        do1_group = factor[:, 1:3, :].rearrange("p t w -> p (t w)").bitcast(BF16)
         interleave_queries("scalar", do1_group, do1_raw)
         do1 = new_operand("do1")
         quantize(do1, do1_group, E5M2)
         after_do1 = keep.tile([P, PACK, W], F32, name="after_do1", tag="slot3", align_bytes=64)
-        first = product(0, qm0, E4M3, 0, ds0, E5M2)
+        scores1 = [product(t, q1, E4M3, t, k1, E4M3) for t in range(PACK)]
+        tanh1 = [after_do1[:, row, :] for row in (1, 2, 3, 2)]
+        nc.scalar.activation(out=tanh1[0], in_=scores1[0][:], func=ACT.Tanh, scale=0.5)
+        first = product(4, qm0, E4M3, 0, ds0, E5M2)
         nc.scalar.copy(out=after_do1[:, 0, :], in_=first[:])
+        second = product(5, qm0, E4M3, 1, ds0, E5M2)
         dk0 = [after_do1[:, 0, :]]
-        v1_halves.append(keep.tile([P, W * 2], BF16, name="v1_late", tag="group_do1", align_bytes=64))
-        v1_half(1)
+        qm0_late = factor[:, 1, :].bitcast(BF16)
+        interleave("gpsimd", qm0_late, qm0_raw[:, :, W // 2 : W], 0, W // 2)
+        nc.vector.quantize_mx(out=qm0[0][:, W // 2 : W].bitcast(E4M3), scales=qm0[1][:, W // 2 : W], in_=qm0_late)
         sq = keep.tile([P, PACK, W], F32, name="weight1", tag="slot4", align_bytes=64)
         for t in range(PACK):
-            a = product(1 + t, q1, E4M3, t, k1, E4M3)
-            th = after_do1[:, 1 + t % 3, :]
-            nc.scalar.activation(out=th, in_=a[:], func=ACT.Tanh, scale=0.5)
-            nc.scalar.activation(out=sq[:, t, :], in_=th, func=ACT.Square)
-            if t == 1:
-                dk0.append(key_gradient(0, 1, qm0, ds0, "dk0_1", 0)[:])
-        factor = keep.tile([P, PACK, W], F32, name="factor1", tag="group_do1", align_bytes=64)
-        for t in range(PACK):
+            if t > 0:
+                nc.scalar.activation(out=tanh1[t], in_=scores1[t][:], func=ACT.Tanh, scale=0.5)
+            nc.scalar.activation(out=sq[:, t, :], in_=tanh1[t], func=ACT.Square)
             nc.gpsimd.tensor_scalar(out=factor[:, t, :], in0=sq[:, t, :], scalar1=-0.25, scalar2=0.25, op0=ALU.mult, op1=ALU.add)
+            if t == 1:
+                nc.scalar.copy(out=tanh1[0], in_=second[:])
+                dk0.append(tanh1[0])
         gated = keep.tile([P, PACK, W], F32, name="gated", tag="slot7", align_bytes=64)
-        dp1 = [product(bank, do1, E5M2, t, v1, E4M3) for t, bank in enumerate((5, 6, 7, 3))]
+        dp1 = [product(bank, do1, E5M2, t, v1, E4M3) for t, bank in enumerate((6, 7, 4, 0))]
         qm1_raw = load_rows(qm[1], "slot8")
         gate1 = keep.tile([P, PACK], F32, name="gate1")
         nc.sync.dma_start(gate1[:], rw[1].rearrange("(p t) o -> p (t o)", t=PACK))
@@ -274,16 +277,12 @@ def tile_attend_gat_sig_k_kernel(tc, qT, kT, vT, doT, rw, qm, offs, out):
                 op=ALU.mult,
             )
 
-        qm0_last = after_do1[:, 3, 0 : W // 2].bitcast(BF16)
-        interleave("scalar", qm0_last, qm0_raw[:, :, 3 * P : W], 0, P)
-        nc.vector.quantize_mx(out=qm0[0][:, 3 * P : W].bitcast(E4M3), scales=qm0[1][:, 3 * P : W], in_=qm0_last)
-        third = product(2, qm0, E4M3, 2, ds0, E5M2)
-        nc.scalar.copy(out=after_do1[:, 1, :], in_=third[:])
-        dk0.append(after_do1[:, 1, :])
-        ds1_half(slice(0, P))
-        ds1_half(slice(P, 2 * P))
-        ds1_half(halves[1])
-        last = product(0, qm0, E4M3, 3, ds0, E5M2)
+        ds1_half(slice(0, 192))
+        third = product(1, qm0, E4M3, 2, ds0, E5M2)
+        nc.scalar.copy(out=tanh1[3], in_=third[:])
+        dk0.append(tanh1[3])
+        ds1_half(slice(192, W))
+        last = product(2, qm0, E4M3, 3, ds0, E5M2)
         last_a = keep.tile([P, W // 2], F32, name="last_a", tag="v1_scales", align_bytes=64)
         nc.scalar.copy(out=last_a[:], in_=last[:, halves[0]])
         qm1 = prepared("qm1", "scalar", qm1_raw, E4M3, slot="do1_codes")
@@ -291,21 +290,12 @@ def tile_attend_gat_sig_k_kernel(tc, qT, kT, vT, doT, rw, qm, offs, out):
         quantize(ds1, ds_group, E5M2)
         last_b = keep.tile([P, W // 2], F32, name="last_b", tag="slot7", align_bytes=64)
         nc.scalar.copy(out=last_b[:], in_=last[:, halves[1]])
-        opening = product(PACK, qm1, E4M3, 0, ds1, E5M2)
-        opening_halves = [keep.tile([P, W // 2], F32, name="opening%d" % u, align_bytes=64) for u in range(2)]
-        nc.scalar.copy(out=opening_halves[0][:], in_=opening[:, halves[0]])
-        dk1 = [key_gradient(1, 1, qm1, ds1, "dk1_1", PACK + 1)]
-        nc.scalar.copy(out=opening_halves[1][:], in_=opening[:, halves[1]])
-        dk1.extend(key_gradient(1, j, qm1, ds1, "dk1_%d" % j, PACK + j) for j in range(2, D // P))
+        dk1 = [key_gradient(1, j, qm1, ds1, "dk1_%d" % j, PACK + j) for j in range(D // P)]
 
         for j in range(D // P - 1):
             nc.vector.tensor_copy(out=windows[j][:].indirect(seq_list(0)), in_=dk0[j])
         nc.vector.tensor_copy(out=windows[3][:].indirect(offsets[:, 0 : LIST_COLS // 2]), in_=last_a[:])
         nc.vector.tensor_copy(out=windows[3][:].indirect(offsets[:, LIST_COLS // 2 : LIST_COLS]), in_=last_b[:])
-        nc.vector.tensor_copy(out=windows[0][:].indirect(offsets[:, LIST_COLS : 3 * LIST_COLS // 2]), in_=opening_halves[0][:])
-        for j in range(1, D // P):
-            nc.vector.tensor_copy(out=windows[j][:].indirect(seq_list(1)), in_=dk1[j - 1][:])
+        for j in range(D // P):
+            nc.vector.tensor_copy(out=windows[j][:].indirect(seq_list(1)), in_=dk1[j][:])
             nc.sync.dma_start(out[j * P : (j + 1) * P, :], windows[j][:])
-            if j == 1:
-                nc.vector.tensor_copy(out=windows[0][:].indirect(offsets[:, 3 * LIST_COLS // 2 : 2 * LIST_COLS]), in_=opening_halves[1][:])
-                nc.sync.dma_start(out[0:P, :], windows[0][:])

@@ -132,8 +132,8 @@ def tile_attend_gat_sig_k_kernel(tc, qT, kT, vT, doT, rw, qm, offs, out):
             return dk
 
         keys = keep.tile([P, PACK, B * N], F32, name="keys")
-        values0 = keep.tile([P, PACK, N], F32, name="values0", align_bytes=64)
-        values1 = keep.tile([P, PACK, 2, RUN], BF16, name="values1", align_bytes=64)
+        values = keep.tile([P, B, PACK, 2, RUN], BF16, name="values", align_bytes=64)
+        values0, values1 = values[:, 0], values[:, 1]
 
         def gather_pool(pool_dram, gathered, first_slot):
             for t in range(PACK - 1):
@@ -179,19 +179,22 @@ def tile_attend_gat_sig_k_kernel(tc, qT, kT, vT, doT, rw, qm, offs, out):
 
         for t in range(2):
             plane = load_plane(vT, t, "slot%d" % (PACK + t))
-            nc.vector.tensor_copy(out=values0[:, t, :], in_=plane[:].indirect(seq_list(0)))
-            nc.vector.tensor_copy(out=values1[:, t, :, 0 : N // 2], in_=plane[:].indirect(seq_list(1)))
+            nc.vector.tensor_copy(out=values[:, :, t, :, 0 : N // 2], in_=plane[:].indirect(offsets[:]))
         v_late = keep.tile([P, 2 * T], F32, name="v_late", tag="slot7", align_bytes=64)
         for t in range(2):
             nc.sync.dma_start(v_late[:, t * T : (t + 1) * T], vT.rearrange("(p t) n -> p t n", t=PACK)[:, 2 + t, :])
         for t in range(2):
-            nc.vector.tensor_copy(out=values0[:, 2 + t, :], in_=v_late[:, t * T : (t + 1) * T].indirect(seq_list(0)))
+            nc.vector.tensor_copy(out=values0[:, 2 + t, :, 0 : N // 2], in_=v_late[:, t * T : (t + 1) * T].indirect(seq_list(0)))
         nc.vector.tensor_copy(out=values1[:, 2, :, 0 : N // 2], in_=v_late[:].indirect(seq_list(1)))
         nc.vector.tensor_copy(out=values1[:, 3, :, 0 : N // 2], in_=v_late[:, T : 2 * T].indirect(seq_list(1)))
         do_raw = load_rows(doT[0], "slot0")
         v_group = new_group("group_v0")
-        interleave("scalar", v_group, values0, 0, V0_ON_SCALAR)
-        interleave("gpsimd", v_group, values0, V0_ON_SCALAR, W)
+        interleave("scalar", v_group, values0[:, :, 0, :], 0, N // 2)
+        copy_on(
+            "gpsimd",
+            v_group[:, W * 2 : W * 4].rearrange("p (c j) -> p c j", j=PACK),
+            values0[:, :, 1, 0 : N // 2].rearrange("p j c -> p c j"),
+        )
         do_halves = [keep.tile([P, W * 2], BF16, name="do_half", tag="do_half%d" % u, align_bytes=64) for u in range(2)]
         for engine, u, m0, m1 in (("scalar", 0, 0, P), ("scalar", 1, 0, DO0_SPLIT), ("vector", 1, DO0_SPLIT, P)):
             copy_on(

@@ -20,10 +20,10 @@ PACK = 4
 W = 512
 LIST_COLS = N // 16
 DO0_SPLIT = 64
-V0_ON_SCALAR = 288
 K0_ON_SCALAR = 416
-RUN = 272
-V1_ON_GPSIMD = 192
+RUNS = 4
+RUN = N // RUNS
+RUN_PITCH = RUN + 16
 
 
 def tile_attend_gat_sig_k_kernel(tc, qT, kT, vT, doT, rw, qm, offs, out):
@@ -132,7 +132,7 @@ def tile_attend_gat_sig_k_kernel(tc, qT, kT, vT, doT, rw, qm, offs, out):
             return dk
 
         keys = keep.tile([P, PACK, B * N], F32, name="keys")
-        values = keep.tile([P, B, PACK, 2, RUN], BF16, name="values", align_bytes=64)
+        values = keep.tile([P, B, PACK, RUNS, RUN_PITCH], BF16, name="values", align_bytes=64)
         values0, values1 = values[:, 0], values[:, 1]
 
         def gather_pool(pool_dram, gathered, first_slot):
@@ -166,7 +166,8 @@ def tile_attend_gat_sig_k_kernel(tc, qT, kT, vT, doT, rw, qm, offs, out):
         gate_neg = keep.tile([P, PACK], F32, name="gate_neg")
         nc.scalar.activation(out=gate_pos[:], in_=gate[:], func=ACT.Copy, scale=0.25)
         nc.scalar.activation(out=gate_neg[:], in_=gate[:], func=ACT.Copy, scale=-0.25)
-        k1_group = new_group("group_k1")
+        shared = keep.tile([P, 7 * W], BF16, name="shared", tag="group_k1", align_bytes=64)
+        k1_group, v1_group = shared[:, 3 * W : 7 * W], shared[:, 0 : 4 * W]
         interleave("scalar", k1_group, keys[:, :, N : 2 * N])
         weight = [keep.tile([P, W], F32, name="weight0_%d" % t, tag="weight0_%d" % t, align_bytes=64) for t in range(PACK)]
         for t in range(PACK):
@@ -179,27 +180,34 @@ def tile_attend_gat_sig_k_kernel(tc, qT, kT, vT, doT, rw, qm, offs, out):
 
         for t in range(2):
             plane = load_plane(vT, t, "slot%d" % (PACK + t))
-            nc.vector.tensor_copy(out=values[:, :, t, :, 0 : N // 2], in_=plane[:].indirect(offsets[:]))
+            nc.vector.tensor_copy(out=values[:, :, t, :, 0:RUN], in_=plane[:].indirect(offsets[:]))
         v_late = keep.tile([P, 2 * T], F32, name="v_late", tag="slot7", align_bytes=64)
         for t in range(2):
             nc.sync.dma_start(v_late[:, t * T : (t + 1) * T], vT.rearrange("(p t) n -> p t n", t=PACK)[:, 2 + t, :])
         for t in range(2):
-            nc.vector.tensor_copy(out=values0[:, 2 + t, :, 0 : N // 2], in_=v_late[:, t * T : (t + 1) * T].indirect(seq_list(0)))
-        nc.vector.tensor_copy(out=values1[:, 2, :, 0 : N // 2], in_=v_late[:].indirect(seq_list(1)))
-        nc.vector.tensor_copy(out=values1[:, 3, :, 0 : N // 2], in_=v_late[:, T : 2 * T].indirect(seq_list(1)))
+            nc.vector.tensor_copy(out=values0[:, 2 + t, :, 0:RUN], in_=v_late[:, t * T : (t + 1) * T].indirect(seq_list(0)))
+        nc.vector.tensor_copy(out=values1[:, 2, :, 0:RUN], in_=v_late[:].indirect(seq_list(1)))
+        nc.vector.tensor_copy(out=values1[:, 3, :, 0:RUN], in_=v_late[:, T : 2 * T].indirect(seq_list(1)))
         do_raw = load_rows(doT[0], "slot0")
         v_group = new_group("group_v0")
-        interleave("scalar", v_group, values0[:, :, 0, :], 0, N // 2)
-        copy_on(
-            "gpsimd",
-            v_group[:, W * 2 : W * 4].rearrange("p (c j) -> p c j", j=PACK),
-            values0[:, :, 1, 0 : N // 2].rearrange("p j c -> p c j"),
+        nc.scalar.copy(
+            out=v_group[:, 0 : 2 * W].rearrange("p (h c i j) -> p h c j i", h=2, i=4, j=PACK),
+            in_=values0[:, :, 0:2, 0:RUN].rearrange("p j h (c i) -> p h c j i", i=4),
         )
-        do_halves = [keep.tile([P, W * 2], BF16, name="do_half", tag="do_half%d" % u, align_bytes=64) for u in range(2)]
+
+        def weave_runs(engine, group, planes, h0, h1):
+            copy_on(
+                engine,
+                group.rearrange("p (h c j) -> p h c j", h=RUNS, j=PACK)[:, h0:h1],
+                planes[:, :, h0:h1, 0:RUN].rearrange("p j h c -> p h c j"),
+            )
+
+        weave_runs("gpsimd", v_group[:], values0, 2, RUNS)
+        do_halves = [keep.tile([P, W * 2], BF16, name="do_half0", align_bytes=64)[:], shared[:, 0 : 2 * W]]
         for engine, u, m0, m1 in (("scalar", 0, 0, P), ("scalar", 1, 0, DO0_SPLIT), ("vector", 1, DO0_SPLIT, P)):
             copy_on(
                 engine,
-                do_halves[u][:].rearrange("p (e m j) -> p m j e", e=2, j=PACK)[:, m0:m1],
+                do_halves[u].rearrange("p (e m j) -> p m j e", e=2, j=PACK)[:, m0:m1],
                 do_raw[:].rearrange("p j (m u e) -> p u m j e", u=2, e=2)[:, u, m0:m1],
             )
         v0 = new_operand("v0")
@@ -207,14 +215,11 @@ def tile_attend_gat_sig_k_kernel(tc, qT, kT, vT, doT, rw, qm, offs, out):
         do0 = new_operand("do0")
         for u in range(2):
             cols = slice(u * W // 2, (u + 1) * W // 2)
-            nc.vector.quantize_mx(out=do0[0][:, cols].bitcast(E5M2), scales=do0[1][:, cols], in_=do_halves[u][:])
+            nc.vector.quantize_mx(out=do0[0][:, cols].bitcast(E5M2), scales=do0[1][:, cols], in_=do_halves[u])
         k1 = new_operand("k1", "slot0")
         quantize(k1, k1_group, E4M3)
         ds_planes = keep.tile([P, PACK, W], F32, name="ds_planes", tag="slot5", align_bytes=64)
-        v1_group = new_group("group_k1")
-        v1_dst = v1_group[:].rearrange("p (h c j) -> p h c j", h=2, j=PACK)
-        v1_src = values1[:, :, :, 0 : N // 2].rearrange("p j h c -> p h c j")
-        copy_on("gpsimd", v1_dst[:, :, 0:V1_ON_GPSIMD], v1_src[:, :, 0:V1_ON_GPSIMD])
+        weave_runs("gpsimd", v1_group, values1, 0, RUNS - 1)
         for t in range(PACK):
             dp = product(PACK + t, do0, E5M2, t, v0, E4M3)
             nc.vector.tensor_tensor(out=ds_planes[:, t, :], in0=dp[:], in1=weight[t][:], op=ALU.mult)
@@ -225,7 +230,7 @@ def tile_attend_gat_sig_k_kernel(tc, qT, kT, vT, doT, rw, qm, offs, out):
         interleave_queries("scalar", q1_group, q1_raw)
         qm0_early = keep.tile([P, W * 2], BF16, name="qm0_early", align_bytes=64)
         interleave("scalar", qm0_early, qm0_raw, 0, W // 2)
-        copy_on("scalar", v1_dst[:, :, V1_ON_GPSIMD : N // 2], v1_src[:, :, V1_ON_GPSIMD : N // 2])
+        weave_runs("scalar", v1_group, values1, RUNS - 1, RUNS)
         q1 = new_operand("q1", "weight0_2")
         quantize(q1, q1_group, E4M3)
         ds_group = new_group("group_ds0")
@@ -239,29 +244,29 @@ def tile_attend_gat_sig_k_kernel(tc, qT, kT, vT, doT, rw, qm, offs, out):
         quantize(v1, v1_group, E4M3)
         factor = keep.tile([P, PACK, W], F32, name="factor1", tag="slot6", align_bytes=64)
         do1_group = factor[:, 1:3, :].rearrange("p t w -> p (t w)").bitcast(BF16)
-        interleave_queries("scalar", do1_group, do1_raw)
+        for h in range(2):
+            interleave_queries("scalar", do1_group, do1_raw, h * P // 2, (h + 1) * P // 2)
         do1 = new_operand("do1")
         quantize(do1, do1_group, E5M2)
-        after_do1 = keep.tile([P, PACK, W], F32, name="after_do1", tag="slot3", align_bytes=64)
         scores1 = [product(t, q1, E4M3, t, k1, E4M3) for t in range(PACK)]
-        tanh1 = [after_do1[:, row, :] for row in (1, 2, 3, 2)]
-        nc.scalar.activation(out=tanh1[0], in_=scores1[0][:], func=ACT.Tanh, scale=0.5)
+        tanh1 = [do1_raw[:, 0:2, 0 : W // 2]] + [do1_raw[:, row, :].rearrange("p (h c) -> p h c", h=2) for row in (2, 0, 2)]
+        nc.scalar.activation(out=tanh1[0], in_=scores1[0][:].rearrange("p (h c) -> p h c", h=2), func=ACT.Tanh, scale=0.5)
         first = product(4, qm0, E4M3, 0, ds0, E5M2)
-        nc.scalar.copy(out=after_do1[:, 0, :], in_=first[:])
+        nc.scalar.copy(out=do1_raw[:, 3, :], in_=first[:])
         second = product(5, qm0, E4M3, 1, ds0, E5M2)
-        dk0 = [after_do1[:, 0, :]]
+        dk0 = [do1_raw[:, 3, :]]
         qm0_late = factor[:, 1, :].bitcast(BF16)
         interleave("gpsimd", qm0_late, qm0_raw[:, :, W // 2 : W], 0, W // 2)
         nc.vector.quantize_mx(out=qm0[0][:, W // 2 : W].bitcast(E4M3), scales=qm0[1][:, W // 2 : W], in_=qm0_late)
         sq = keep.tile([P, PACK, W], F32, name="weight1", tag="slot4", align_bytes=64)
         for t in range(PACK):
             if t > 0:
-                nc.scalar.activation(out=tanh1[t], in_=scores1[t][:], func=ACT.Tanh, scale=0.5)
-            nc.scalar.activation(out=sq[:, t, :], in_=tanh1[t], func=ACT.Square)
+                nc.scalar.activation(out=tanh1[t], in_=scores1[t][:].rearrange("p (h c) -> p h c", h=2), func=ACT.Tanh, scale=0.5)
+            nc.scalar.activation(out=sq[:, t, :].rearrange("p (h c) -> p h c", h=2), in_=tanh1[t], func=ACT.Square)
             nc.gpsimd.tensor_scalar(out=factor[:, t, :], in0=sq[:, t, :], scalar1=-0.25, scalar2=0.25, op0=ALU.mult, op1=ALU.add)
             if t == 1:
-                nc.scalar.copy(out=tanh1[0], in_=second[:])
-                dk0.append(tanh1[0])
+                nc.scalar.copy(out=do1_raw[:, 1, :], in_=second[:])
+                dk0.append(do1_raw[:, 1, :])
         gated = keep.tile([P, PACK, W], F32, name="gated", tag="slot7", align_bytes=64)
         dp1 = [product(bank, do1, E5M2, t, v1, E4M3) for t, bank in enumerate((6, 7, 4, 0))]
         qm1_raw = load_rows(qm[1], "slot8")
@@ -282,8 +287,8 @@ def tile_attend_gat_sig_k_kernel(tc, qT, kT, vT, doT, rw, qm, offs, out):
 
         ds1_half(slice(0, 192))
         third = product(1, qm0, E4M3, 2, ds0, E5M2)
-        nc.scalar.copy(out=tanh1[3], in_=third[:])
-        dk0.append(tanh1[3])
+        nc.scalar.copy(out=do1_raw[:, 2, :], in_=third[:])
+        dk0.append(do1_raw[:, 2, :])
         ds1_half(slice(192, W))
         last = product(2, qm0, E4M3, 3, ds0, E5M2)
         last_a = keep.tile([P, W // 2], F32, name="last_a", tag="v1_scales", align_bytes=64)

@@ -20,7 +20,8 @@ PACK = 4
 W = 512
 LIST_COLS = N // 16
 DO0_SPLIT = 64
-K0_ON_SCALAR = 416
+KEY_PLANES_ON_SCALAR = 2
+Q0_ON_VECTOR = 112
 RUNS = 4
 RUN = N // RUNS
 RUN_PITCH = RUN + 16
@@ -131,32 +132,45 @@ def tile_attend_gat_sig_k_kernel(tc, qT, kT, vT, doT, rw, qm, offs, out):
             nc.scalar.copy(out=dk[:], in_=acc[:])
             return dk
 
-        keys = keep.tile([P, PACK, B * N], F32, name="keys")
+        keys = keep.tile([P, B, PACK, RUNS, RUN_PITCH], BF16, name="keys", align_bytes=64)
         values = keep.tile([P, B, PACK, RUNS, RUN_PITCH], BF16, name="values", align_bytes=64)
         values0, values1 = values[:, 0], values[:, 1]
 
-        def gather_pool(pool_dram, gathered, first_slot):
-            for t in range(PACK - 1):
-                plane = first_plane if t == 0 else load_plane(pool_dram, t, "slot%d" % (first_slot + t))
-                nc.vector.tensor_copy(out=gathered[:, t, :], in_=plane[:].indirect(offsets[:]))
-            plane = load_plane(pool_dram, PACK - 1, "slot%d" % (first_slot + PACK - 1))
-            nc.vector.tensor_copy(out=gathered[:, PACK - 1, 0:N], in_=plane[:].indirect(seq_list(0)))
-            return plane
+        def weave_runs(engine, group, planes, h0, h1):
+            copy_on(
+                engine,
+                group.rearrange("p (h c j) -> p h c j", h=RUNS, j=PACK)[:, h0:h1],
+                planes[:, :, h0:h1, 0:RUN].rearrange("p j h c -> p h c j"),
+            )
 
-        def gather_rest(plane, gathered):
-            nc.vector.tensor_copy(out=gathered[:, PACK - 1, N : 2 * N], in_=plane[:].indirect(seq_list(1)))
+        def weave_lines(group, planes, h0, h1):
+            nc.scalar.copy(
+                out=group.rearrange("p (h c i j) -> p h c j i", h=RUNS, i=4, j=PACK)[:, h0:h1],
+                in_=planes[:, :, h0:h1, 0:RUN].rearrange("p j h (c i) -> p h c j i", i=4),
+            )
 
-        k_last = gather_pool(kT, keys, 0)
-        gather_rest(k_last, keys)
+        for t in range(PACK):
+            plane = first_plane if t == 0 else load_plane(kT, t, "slot%d" % t)
+            if t < KEY_PLANES_ON_SCALAR:
+                nc.vector.tensor_copy(out=keys[:, 0, t, :, 0:RUN], in_=plane[:].indirect(seq_list(0)))
+                rounded = keep.tile([P, T], BF16, name="rounded%d" % t, align_bytes=64)
+                nc.scalar.activation(out=rounded[:], in_=plane[:], func=ACT.Copy)
+                nc.scalar.activation(out=keys[:, 1, t, :, 0:RUN], in_=rounded[:].indirect(seq_list(1)), func=ACT.Copy)
+            elif t < PACK - 1:
+                nc.vector.tensor_copy(out=keys[:, :, t, :, 0:RUN], in_=plane[:].indirect(offsets[:]))
+            else:
+                for b in range(B):
+                    nc.vector.tensor_copy(out=keys[:, b, t, :, 0:RUN], in_=plane[:].indirect(seq_list(b)))
         q_raw = load_rows(qT[0], "slot8")
         gate = keep.tile([P, PACK], F32, name="gate", tag="group_k1", align_bytes=64)
         nc.sync.dma_start(gate[:], rw[0].rearrange("(p t) o -> p (t o)", t=PACK))
 
         kq_group = keep.tile([P, 2 * W * PACK], BF16, name="kq_group", align_bytes=64)
         k_group, q_group = kq_group[:, 0 : W * PACK], kq_group[:, W * PACK : 2 * W * PACK]
-        interleave("scalar", k_group, keys[:, :, 0:N], 0, K0_ON_SCALAR)
-        interleave("gpsimd", k_group, keys[:, :, 0:N], K0_ON_SCALAR, W)
-        interleave_queries("vector", q_group, q_raw)
+        weave_lines(k_group, keys[:, 0], 0, RUNS - 1)
+        weave_runs("gpsimd", k_group, keys[:, 0], RUNS - 1, RUNS)
+        interleave_queries("vector", q_group, q_raw, 0, Q0_ON_VECTOR)
+        interleave_queries("scalar", q_group, q_raw, Q0_ON_VECTOR, P)
         kq_codes = keep.tile([P, 2 * W], U32, name="kq_codes", align_bytes=64)
         kq_scales = keep.tile([P, 2 * W], U8, name="kq_scales", align_bytes=64)
         nc.vector.quantize_mx(out=kq_codes[:].bitcast(E4M3), scales=kq_scales[:], in_=kq_group[:])
@@ -168,7 +182,7 @@ def tile_attend_gat_sig_k_kernel(tc, qT, kT, vT, doT, rw, qm, offs, out):
         nc.scalar.activation(out=gate_neg[:], in_=gate[:], func=ACT.Copy, scale=-0.25)
         shared = keep.tile([P, 7 * W], BF16, name="shared", tag="group_k1", align_bytes=64)
         k1_group, v1_group = shared[:, 3 * W : 7 * W], shared[:, 0 : 4 * W]
-        interleave("scalar", k1_group, keys[:, :, N : 2 * N])
+        weave_lines(k1_group, keys[:, 1], 0, RUNS)
         weight = [keep.tile([P, W], F32, name="weight0_%d" % t, tag="weight0_%d" % t, align_bytes=64) for t in range(PACK)]
         for t in range(PACK):
             tanh_squared(weight[t][:], t, t, q0, k0)
@@ -190,18 +204,7 @@ def tile_attend_gat_sig_k_kernel(tc, qT, kT, vT, doT, rw, qm, offs, out):
         nc.vector.tensor_copy(out=values1[:, 3, :, 0:RUN], in_=v_late[:, T : 2 * T].indirect(seq_list(1)))
         do_raw = load_rows(doT[0], "slot0")
         v_group = new_group("group_v0")
-        nc.scalar.copy(
-            out=v_group[:, 0 : 2 * W].rearrange("p (h c i j) -> p h c j i", h=2, i=4, j=PACK),
-            in_=values0[:, :, 0:2, 0:RUN].rearrange("p j h (c i) -> p h c j i", i=4),
-        )
-
-        def weave_runs(engine, group, planes, h0, h1):
-            copy_on(
-                engine,
-                group.rearrange("p (h c j) -> p h c j", h=RUNS, j=PACK)[:, h0:h1],
-                planes[:, :, h0:h1, 0:RUN].rearrange("p j h c -> p h c j"),
-            )
-
+        weave_lines(v_group[:], values0, 0, 2)
         weave_runs("gpsimd", v_group[:], values0, 2, RUNS)
         do_halves = [keep.tile([P, W * 2], BF16, name="do_half0", align_bytes=64)[:], shared[:, 0 : 2 * W]]
         for engine, u, m0, m1 in (("scalar", 0, 0, P), ("scalar", 1, 0, DO0_SPLIT), ("vector", 1, DO0_SPLIT, P)):

@@ -19,12 +19,12 @@ P = 128
 PACK = 4
 W = 512
 LIST_COLS = N // 16
-DO0_SPLIT = 64
+DO0_SPLIT = 96
 KEY_PLANES_ON_SCALAR = 2
-Q0_ON_VECTOR = 112
-RUNS = 4
-RUN = N // RUNS
-RUN_PITCH = RUN + 16
+Q0_ON_VECTOR = 88
+K0_ON_SCALAR = 352
+V0_ON_SCALAR = 320
+V1_ON_GPSIMD = 384
 
 
 def tile_attend_gat_sig_k_kernel(tc, qT, kT, vT, doT, rw, qm, offs, out):
@@ -132,43 +132,44 @@ def tile_attend_gat_sig_k_kernel(tc, qT, kT, vT, doT, rw, qm, offs, out):
             nc.scalar.copy(out=dk[:], in_=acc[:])
             return dk
 
-        keys = keep.tile([P, B, PACK, RUNS, RUN_PITCH], BF16, name="keys", align_bytes=64)
-        values = keep.tile([P, B, PACK, RUNS, RUN_PITCH], BF16, name="values", align_bytes=64)
-        values0, values1 = values[:, 0], values[:, 1]
+        keys_tile = keep.tile([P, B * PACK * N], BF16, name="keys", align_bytes=64)
+        values_tile = keep.tile([P, B * PACK * N], BF16, name="values", align_bytes=64)
+        keys = keys_tile[:].rearrange("p (b u n e) -> p b u e n", b=B, u=2, e=2)
+        values = values_tile[:].rearrange("p (b u n e) -> p b u e n", b=B, u=2, e=2)
 
-        def weave_runs(engine, group, planes, h0, h1):
+        def weave_values(group, pairs, b, n0, n1):
             copy_on(
-                engine,
-                group.rearrange("p (h c j) -> p h c j", h=RUNS, j=PACK)[:, h0:h1],
-                planes[:, :, h0:h1, 0:RUN].rearrange("p j h c -> p h c j"),
+                "gpsimd",
+                group.rearrange("p (n u e) -> p n u e", u=2, e=2)[:, n0:n1],
+                pairs[:].rearrange("p (b u n e) -> p b n u e", b=B, u=2, e=2)[:, b, n0:n1],
             )
 
-        def weave_lines(group, planes, h0, h1):
+        def weave_words(group, pairs, b, n0, n1):
             nc.scalar.copy(
-                out=group.rearrange("p (h c i j) -> p h c j i", h=RUNS, i=4, j=PACK)[:, h0:h1],
-                in_=planes[:, :, h0:h1, 0:RUN].rearrange("p j h (c i) -> p h c j i", i=4),
+                out=group.bitcast(U32).rearrange("p (n u) -> p n u", u=2)[:, n0:n1],
+                in_=pairs[:].bitcast(U32).rearrange("p (b u n) -> p b n u", b=B, u=2)[:, b, n0:n1],
             )
 
         for t in range(PACK):
             plane = first_plane if t == 0 else load_plane(kT, t, "slot%d" % t)
             if t < KEY_PLANES_ON_SCALAR:
-                nc.vector.tensor_copy(out=keys[:, 0, t, :, 0:RUN], in_=plane[:].indirect(seq_list(0)))
+                nc.vector.tensor_copy(out=keys[:, 0, t // 2, t % 2, :], in_=plane[:].indirect(seq_list(0)))
                 rounded = keep.tile([P, T], BF16, name="rounded%d" % t, align_bytes=64)
                 nc.scalar.activation(out=rounded[:], in_=plane[:], func=ACT.Copy)
-                nc.scalar.activation(out=keys[:, 1, t, :, 0:RUN], in_=rounded[:].indirect(seq_list(1)), func=ACT.Copy)
+                nc.scalar.activation(out=keys[:, 1, t // 2, t % 2, :], in_=rounded[:].indirect(seq_list(1)), func=ACT.Copy)
             elif t < PACK - 1:
-                nc.vector.tensor_copy(out=keys[:, :, t, :, 0:RUN], in_=plane[:].indirect(offsets[:]))
+                nc.vector.tensor_copy(out=keys[:, :, t // 2, t % 2, :], in_=plane[:].indirect(offsets[:]))
             else:
                 for b in range(B):
-                    nc.vector.tensor_copy(out=keys[:, b, t, :, 0:RUN], in_=plane[:].indirect(seq_list(b)))
+                    nc.vector.tensor_copy(out=keys[:, b, t // 2, t % 2, :], in_=plane[:].indirect(seq_list(b)))
         q_raw = load_rows(qT[0], "slot8")
         gate = keep.tile([P, PACK], F32, name="gate", tag="group_k1", align_bytes=64)
         nc.sync.dma_start(gate[:], rw[0].rearrange("(p t) o -> p (t o)", t=PACK))
 
         kq_group = keep.tile([P, 2 * W * PACK], BF16, name="kq_group", align_bytes=64)
         k_group, q_group = kq_group[:, 0 : W * PACK], kq_group[:, W * PACK : 2 * W * PACK]
-        weave_lines(k_group, keys[:, 0], 0, RUNS - 1)
-        weave_runs("gpsimd", k_group, keys[:, 0], RUNS - 1, RUNS)
+        weave_words(k_group, keys_tile, 0, 0, K0_ON_SCALAR)
+        weave_values(k_group, keys_tile, 0, K0_ON_SCALAR, N)
         interleave_queries("vector", q_group, q_raw, 0, Q0_ON_VECTOR)
         interleave_queries("scalar", q_group, q_raw, Q0_ON_VECTOR, P)
         kq_codes = keep.tile([P, 2 * W], U32, name="kq_codes", align_bytes=64)
@@ -180,9 +181,9 @@ def tile_attend_gat_sig_k_kernel(tc, qT, kT, vT, doT, rw, qm, offs, out):
         gate_neg = keep.tile([P, PACK], F32, name="gate_neg")
         nc.scalar.activation(out=gate_pos[:], in_=gate[:], func=ACT.Copy, scale=0.25)
         nc.scalar.activation(out=gate_neg[:], in_=gate[:], func=ACT.Copy, scale=-0.25)
-        shared = keep.tile([P, 7 * W], BF16, name="shared", tag="group_k1", align_bytes=64)
-        k1_group, v1_group = shared[:, 3 * W : 7 * W], shared[:, 0 : 4 * W]
-        weave_lines(k1_group, keys[:, 1], 0, RUNS)
+        shared = keep.tile([P, 9 * W], BF16, name="shared", tag="group_k1", align_bytes=64)
+        do_group, v1_group, k1_group = shared[:, 0 : 4 * W], shared[:, 2 * W : 6 * W], shared[:, 5 * W : 9 * W]
+        weave_words(k1_group, keys_tile, 1, 0, N)
         weight = [keep.tile([P, W], F32, name="weight0_%d" % t, tag="weight0_%d" % t, align_bytes=64) for t in range(PACK)]
         for t in range(PACK):
             tanh_squared(weight[t][:], t, t, q0, k0)
@@ -194,35 +195,29 @@ def tile_attend_gat_sig_k_kernel(tc, qT, kT, vT, doT, rw, qm, offs, out):
 
         for t in range(2):
             plane = load_plane(vT, t, "slot%d" % (PACK + t))
-            nc.vector.tensor_copy(out=values[:, :, t, :, 0:RUN], in_=plane[:].indirect(offsets[:]))
+            nc.vector.tensor_copy(out=values[:, :, 0, t, :], in_=plane[:].indirect(offsets[:]))
         v_late = keep.tile([P, 2 * T], F32, name="v_late", tag="slot7", align_bytes=64)
         for t in range(2):
             nc.sync.dma_start(v_late[:, t * T : (t + 1) * T], vT.rearrange("(p t) n -> p t n", t=PACK)[:, 2 + t, :])
         for t in range(2):
-            nc.vector.tensor_copy(out=values0[:, 2 + t, :, 0:RUN], in_=v_late[:, t * T : (t + 1) * T].indirect(seq_list(0)))
-        nc.vector.tensor_copy(out=values1[:, 2, :, 0:RUN], in_=v_late[:].indirect(seq_list(1)))
-        nc.vector.tensor_copy(out=values1[:, 3, :, 0:RUN], in_=v_late[:, T : 2 * T].indirect(seq_list(1)))
+            nc.vector.tensor_copy(out=values[:, 0, 1, t, :], in_=v_late[:, t * T : (t + 1) * T].indirect(seq_list(0)))
+        nc.vector.tensor_copy(out=values[:, 1, 1, 0, :], in_=v_late[:].indirect(seq_list(1)))
+        nc.vector.tensor_copy(out=values[:, 1, 1, 1, :], in_=v_late[:, T : 2 * T].indirect(seq_list(1)))
         do_raw = load_rows(doT[0], "slot0")
         v_group = new_group("group_v0")
-        weave_lines(v_group[:], values0, 0, 2)
-        weave_runs("gpsimd", v_group[:], values0, 2, RUNS)
-        do_halves = [keep.tile([P, W * 2], BF16, name="do_half0", align_bytes=64)[:], shared[:, 0 : 2 * W]]
-        for engine, u, m0, m1 in (("scalar", 0, 0, P), ("scalar", 1, 0, DO0_SPLIT), ("vector", 1, DO0_SPLIT, P)):
-            copy_on(
-                engine,
-                do_halves[u].rearrange("p (e m j) -> p m j e", e=2, j=PACK)[:, m0:m1],
-                do_raw[:].rearrange("p j (m u e) -> p u m j e", u=2, e=2)[:, u, m0:m1],
-            )
+        weave_words(v_group[:], values_tile, 0, 0, V0_ON_SCALAR)
+        weave_values(v_group[:], values_tile, 0, V0_ON_SCALAR, N)
+        interleave_queries("scalar", do_group, do_raw, 0, DO0_SPLIT)
+        interleave_queries("gpsimd", do_group, do_raw, DO0_SPLIT, P)
         v0 = new_operand("v0")
         quantize(v0, v_group, E4M3)
         do0 = new_operand("do0")
         for u in range(2):
-            cols = slice(u * W // 2, (u + 1) * W // 2)
-            nc.vector.quantize_mx(out=do0[0][:, cols].bitcast(E5M2), scales=do0[1][:, cols], in_=do_halves[u])
+            quantize(do0, do_group, E5M2, u * W // 2, (u + 1) * W // 2)
         k1 = new_operand("k1", "slot0")
         quantize(k1, k1_group, E4M3)
         ds_planes = keep.tile([P, PACK, W], F32, name="ds_planes", tag="slot5", align_bytes=64)
-        weave_runs("gpsimd", v1_group, values1, 0, RUNS - 1)
+        weave_values(v1_group, values_tile, 1, 0, V1_ON_GPSIMD)
         for t in range(PACK):
             dp = product(PACK + t, do0, E5M2, t, v0, E4M3)
             nc.vector.tensor_tensor(out=ds_planes[:, t, :], in0=dp[:], in1=weight[t][:], op=ALU.mult)
@@ -233,7 +228,7 @@ def tile_attend_gat_sig_k_kernel(tc, qT, kT, vT, doT, rw, qm, offs, out):
         interleave_queries("scalar", q1_group, q1_raw)
         qm0_early = keep.tile([P, W * 2], BF16, name="qm0_early", align_bytes=64)
         interleave("scalar", qm0_early, qm0_raw, 0, W // 2)
-        weave_runs("scalar", v1_group, values1, RUNS - 1, RUNS)
+        weave_words(v1_group, values_tile, 1, V1_ON_GPSIMD, N)
         q1 = new_operand("q1", "weight0_2")
         quantize(q1, q1_group, E4M3)
         ds_group = new_group("group_ds0")

@@ -19,12 +19,13 @@ P = 128
 PACK = 4
 W = 512
 LIST_COLS = N // 16
-DO0_SPLIT = 96
+DO0_SPLIT = 100
 KEY_PLANES_ON_SCALAR = 2
-Q0_ON_VECTOR = 88
-K0_ON_SCALAR = 352
-V0_ON_SCALAR = 320
-V1_ON_GPSIMD = 384
+Q0_ON_VECTOR = 80
+K0_ON_SCALAR = 192
+V0_ON_SCALAR = 224
+QM0_ON_GPSIMD = 64
+DS0_ON_SCALAR = 112
 
 
 def tile_attend_gat_sig_k_kernel(tc, qT, kT, vT, doT, rw, qm, offs, out):
@@ -137,18 +138,13 @@ def tile_attend_gat_sig_k_kernel(tc, qT, kT, vT, doT, rw, qm, offs, out):
         keys = keys_tile[:].rearrange("p (b u n e) -> p b u e n", b=B, u=2, e=2)
         values = values_tile[:].rearrange("p (b u n e) -> p b u e n", b=B, u=2, e=2)
 
-        def weave_values(group, pairs, b, n0, n1):
-            copy_on(
-                "gpsimd",
-                group.rearrange("p (n u e) -> p n u e", u=2, e=2)[:, n0:n1],
-                pairs[:].rearrange("p (b u n e) -> p b n u e", b=B, u=2, e=2)[:, b, n0:n1],
-            )
-
-        def weave_words(group, pairs, b, n0, n1):
-            nc.scalar.copy(
-                out=group.bitcast(U32).rearrange("p (n u) -> p n u", u=2)[:, n0:n1],
-                in_=pairs[:].bitcast(U32).rearrange("p (b u n) -> p b n u", b=B, u=2)[:, b, n0:n1],
-            )
+        def weave_words(engine, group, pairs, b, n0, n1):
+            dst = group.bitcast(U32).rearrange("p (n u) -> p n u", u=2)[:, n0:n1]
+            src = pairs[:].bitcast(U32).rearrange("p (b u n) -> p b n u", b=B, u=2)[:, b, n0:n1]
+            if engine == "scalar":
+                nc.scalar.copy(out=dst, in_=src)
+            else:
+                nc.gpsimd.tensor_copy(out=dst, in_=src)
 
         for t in range(PACK):
             plane = first_plane if t == 0 else load_plane(kT, t, "slot%d" % t)
@@ -168,8 +164,8 @@ def tile_attend_gat_sig_k_kernel(tc, qT, kT, vT, doT, rw, qm, offs, out):
 
         kq_group = keep.tile([P, 2 * W * PACK], BF16, name="kq_group", align_bytes=64)
         k_group, q_group = kq_group[:, 0 : W * PACK], kq_group[:, W * PACK : 2 * W * PACK]
-        weave_words(k_group, keys_tile, 0, 0, K0_ON_SCALAR)
-        weave_values(k_group, keys_tile, 0, K0_ON_SCALAR, N)
+        weave_words("scalar", k_group, keys_tile, 0, 0, K0_ON_SCALAR)
+        weave_words("gpsimd", k_group, keys_tile, 0, K0_ON_SCALAR, N)
         interleave_queries("vector", q_group, q_raw, 0, Q0_ON_VECTOR)
         interleave_queries("scalar", q_group, q_raw, Q0_ON_VECTOR, P)
         kq_codes = keep.tile([P, 2 * W], U32, name="kq_codes", align_bytes=64)
@@ -181,9 +177,9 @@ def tile_attend_gat_sig_k_kernel(tc, qT, kT, vT, doT, rw, qm, offs, out):
         gate_neg = keep.tile([P, PACK], F32, name="gate_neg")
         nc.scalar.activation(out=gate_pos[:], in_=gate[:], func=ACT.Copy, scale=0.25)
         nc.scalar.activation(out=gate_neg[:], in_=gate[:], func=ACT.Copy, scale=-0.25)
-        shared = keep.tile([P, 9 * W], BF16, name="shared", tag="group_k1", align_bytes=64)
-        do_group, v1_group, k1_group = shared[:, 0 : 4 * W], shared[:, 2 * W : 6 * W], shared[:, 5 * W : 9 * W]
-        weave_words(k1_group, keys_tile, 1, 0, N)
+        shared = keep.tile([P, 10 * W], BF16, name="shared", tag="group_k1", align_bytes=64)
+        do_group, v1_group, k1_group = shared[:, 0 : 4 * W], shared[:, 2 * W : 6 * W], shared[:, 6 * W : 10 * W]
+        weave_words("scalar", k1_group, keys_tile, 1, 0, N)
         weight = [keep.tile([P, W], F32, name="weight0_%d" % t, tag="weight0_%d" % t, align_bytes=64) for t in range(PACK)]
         for t in range(PACK):
             tanh_squared(weight[t][:], t, t, q0, k0)
@@ -205,8 +201,8 @@ def tile_attend_gat_sig_k_kernel(tc, qT, kT, vT, doT, rw, qm, offs, out):
         nc.vector.tensor_copy(out=values[:, 1, 1, 1, :], in_=v_late[:, T : 2 * T].indirect(seq_list(1)))
         do_raw = load_rows(doT[0], "slot0")
         v_group = new_group("group_v0")
-        weave_words(v_group[:], values_tile, 0, 0, V0_ON_SCALAR)
-        weave_values(v_group[:], values_tile, 0, V0_ON_SCALAR, N)
+        weave_words("scalar", v_group[:], values_tile, 0, 0, V0_ON_SCALAR)
+        weave_words("gpsimd", v_group[:], values_tile, 0, V0_ON_SCALAR, N)
         interleave_queries("scalar", do_group, do_raw, 0, DO0_SPLIT)
         interleave_queries("gpsimd", do_group, do_raw, DO0_SPLIT, P)
         v0 = new_operand("v0")
@@ -217,28 +213,30 @@ def tile_attend_gat_sig_k_kernel(tc, qT, kT, vT, doT, rw, qm, offs, out):
         k1 = new_operand("k1", "slot0")
         quantize(k1, k1_group, E4M3)
         ds_planes = keep.tile([P, PACK, W], F32, name="ds_planes", tag="slot5", align_bytes=64)
-        weave_values(v1_group, values_tile, 1, 0, V1_ON_GPSIMD)
+        weave_words("gpsimd", v1_group, values_tile, 1, 0, N)
         for t in range(PACK):
             dp = product(PACK + t, do0, E5M2, t, v0, E4M3)
-            nc.vector.tensor_tensor(out=ds_planes[:, t, :], in0=dp[:], in1=weight[t][:], op=ALU.mult)
+            for cols in [slice(0, W)] if t < PACK - 1 else [slice(0, DS0_ON_SCALAR), slice(DS0_ON_SCALAR, W)]:
+                nc.vector.tensor_tensor(out=ds_planes[:, t, cols], in0=dp[:, cols], in1=weight[t][:, cols], op=ALU.mult)
         q1_raw = load_rows(qT[1], "slot1")
         qm0_raw = load_rows(qm[0], "slot2")
         do1_raw = load_rows(doT[1], "slot3")
-        q1_group = new_group("group_v0")
+        q1_group = new_group("group_q1")
         interleave_queries("scalar", q1_group, q1_raw)
         qm0_early = keep.tile([P, W * 2], BF16, name="qm0_early", align_bytes=64)
-        interleave("scalar", qm0_early, qm0_raw, 0, W // 2)
-        weave_words(v1_group, values_tile, 1, V1_ON_GPSIMD, N)
+        interleave("gpsimd", qm0_early, qm0_raw, 0, QM0_ON_GPSIMD)
+        interleave("scalar", qm0_early, qm0_raw, QM0_ON_GPSIMD, W // 2)
         q1 = new_operand("q1", "weight0_2")
         quantize(q1, q1_group, E4M3)
         ds_group = new_group("group_ds0")
-        interleave("vector", ds_group, ds_planes)
+        interleave("vector", ds_group, ds_planes, DS0_ON_SCALAR, W)
+        interleave("scalar", ds_group, ds_planes, 0, DS0_ON_SCALAR)
         qm0 = new_operand("qm0")
         quantize(qm0, qm0_early, E4M3, 0, W // 2)
         ds0 = new_operand("ds0")
         quantize(ds0, ds_group, E5M2)
 
-        v1 = new_operand("v1", "weight0_3")
+        v1 = new_operand("v1", "slot5")
         quantize(v1, v1_group, E4M3)
         factor = keep.tile([P, PACK, W], F32, name="factor1", tag="slot6", align_bytes=64)
         do1_group = factor[:, 1:3, :].rearrange("p t w -> p (t w)").bitcast(BF16)

@@ -66,7 +66,7 @@ def tile_attend_gat_sig_k_kernel(tc, qT, kT, vT, doT, rw, qm, offs, out):
             if engine == "vector":
                 nc.vector.tensor_copy(out=dst, in_=src)
             elif engine == "gpsimd":
-                nc.gpsimd.tensor_scalar(out=dst, in0=src, scalar1=1.0, scalar2=0.0, op0=ALU.mult, op1=ALU.add)
+                nc.gpsimd.tensor_copy(out=dst, in_=src)
             else:
                 nc.scalar.copy(out=dst, in_=src)
 

@@ -19,13 +19,14 @@ P = 128
 PACK = 4
 W = 512
 LIST_COLS = N // 16
-DO0_SPLIT = 100
+DO0_SPLIT = 76
 KEY_PLANES_ON_SCALAR = 2
 Q0_ON_VECTOR = 80
 K0_ON_SCALAR = 192
 V0_ON_SCALAR = 224
-QM0_ON_GPSIMD = 64
-DS0_ON_SCALAR = 112
+QM0_ON_GPSIMD = 128
+DS0_ON_SCALAR = 144
+SQUARES_ON_GPSIMD = 2
 
 
 def tile_attend_gat_sig_k_kernel(tc, qT, kT, vT, doT, rw, qm, offs, out):
@@ -121,12 +122,6 @@ def tile_attend_gat_sig_k_kernel(tc, qT, kT, vT, doT, rw, qm, offs, out):
             quantize(operand, group, fmt)
             return operand
 
-        def tanh_squared(sq, t, bank, q_op, k_op):
-            a = product(bank, q_op, E4M3, t, k_op, E4M3)
-            th = keep.tile([P, W], F32, name="tanh%d" % t, tag="tanh%d" % t, align_bytes=64)
-            nc.scalar.activation(out=th[:], in_=a[:], func=ACT.Tanh, scale=0.5)
-            nc.scalar.activation(out=sq, in_=th[:], func=ACT.Square)
-
         def key_gradient(b, j, qm_op, ds_op, slot, bank):
             acc = product(bank, qm_op, E4M3, j, ds_op, E5M2)
             dk = keep.tile([P, W], F32, name="dk%d_%d" % (b, j), tag=slot, align_bytes=64)
@@ -181,30 +176,37 @@ def tile_attend_gat_sig_k_kernel(tc, qT, kT, vT, doT, rw, qm, offs, out):
         do_group, v1_group, k1_group = shared[:, 0 : 4 * W], shared[:, 2 * W : 6 * W], shared[:, 6 * W : 10 * W]
         weave_words("scalar", k1_group, keys_tile, 1, 0, N)
         weight = [keep.tile([P, W], F32, name="weight0_%d" % t, tag="weight0_%d" % t, align_bytes=64) for t in range(PACK)]
+        tanh0 = [keep.tile([P, W], F32, name="tanh%d" % t, align_bytes=64) for t in range(PACK)]
         for t in range(PACK):
-            tanh_squared(weight[t][:], t, t, q0, k0)
+            nc.scalar.activation(out=tanh0[t][:], in_=product(t, q0, E4M3, t, k0, E4M3)[:], func=ACT.Tanh, scale=0.5)
+        for t in range(PACK):
+            if t < SQUARES_ON_GPSIMD:
+                nc.gpsimd.tensor_tensor(out=weight[t][:], in0=tanh0[t][:], in1=tanh0[t][:], op=ALU.mult)
+            else:
+                nc.scalar.activation(out=weight[t][:], in_=tanh0[t][:], func=ACT.Square)
         for t in range(PACK):
             nc.gpsimd.tensor_scalar(
                 out=weight[t][:], in0=weight[t][:], scalar1=gate_neg[:, t : t + 1],
                 scalar2=gate_pos[:, t : t + 1], op0=ALU.mult, op1=ALU.add,
             )
 
-        for t in range(2):
-            plane = load_plane(vT, t, "slot%d" % (PACK + t))
-            nc.vector.tensor_copy(out=values[:, :, 0, t, :], in_=plane[:].indirect(offsets[:]))
-        v_late = keep.tile([P, 2 * T], F32, name="v_late", tag="slot7", align_bytes=64)
-        for t in range(2):
-            nc.sync.dma_start(v_late[:, t * T : (t + 1) * T], vT.rearrange("(p t) n -> p t n", t=PACK)[:, 2 + t, :])
-        for t in range(2):
-            nc.vector.tensor_copy(out=values[:, 0, 1, t, :], in_=v_late[:, t * T : (t + 1) * T].indirect(seq_list(0)))
-        nc.vector.tensor_copy(out=values[:, 1, 1, 0, :], in_=v_late[:].indirect(seq_list(1)))
-        nc.vector.tensor_copy(out=values[:, 1, 1, 1, :], in_=v_late[:, T : 2 * T].indirect(seq_list(1)))
+        for t, slot in ((0, "slot4"), (2, "slot5")):
+            plane = load_plane(vT, t, slot)
+            nc.vector.tensor_copy(out=values[:, :, t // 2, 0, :], in_=plane[:].indirect(offsets[:]))
+        plane = load_plane(vT, 1, "slot7")
+        nc.vector.tensor_copy(out=values[:, 0, 0, 1, :], in_=plane[:].indirect(seq_list(0)))
+        rounded = keep.tile([P, T], BF16, name="rounded_v1", tag="slot4", align_bytes=64)
+        nc.scalar.activation(out=rounded[:], in_=plane[:], func=ACT.Copy)
+        nc.scalar.activation(out=values[:, 1, 0, 1, :], in_=rounded[:].indirect(seq_list(1)), func=ACT.Copy)
+        plane = load_plane(vT, 3, "slot6")
+        for b in range(B):
+            nc.vector.tensor_copy(out=values[:, b, 1, 1, :], in_=plane[:].indirect(seq_list(b)))
         do_raw = load_rows(doT[0], "slot0")
-        v_group = new_group("group_v0")
+        v_group = new_group("slot7")
         weave_words("scalar", v_group[:], values_tile, 0, 0, V0_ON_SCALAR)
         weave_words("gpsimd", v_group[:], values_tile, 0, V0_ON_SCALAR, N)
         interleave_queries("scalar", do_group, do_raw, 0, DO0_SPLIT)
-        interleave_queries("gpsimd", do_group, do_raw, DO0_SPLIT, P)
+        interleave_queries("vector", do_group, do_raw, DO0_SPLIT, P)
         v0 = new_operand("v0")
         quantize(v0, v_group, E4M3)
         do0 = new_operand("do0")
@@ -213,14 +215,19 @@ def tile_attend_gat_sig_k_kernel(tc, qT, kT, vT, doT, rw, qm, offs, out):
         k1 = new_operand("k1", "slot0")
         quantize(k1, k1_group, E4M3)
         ds_planes = keep.tile([P, PACK, W], F32, name="ds_planes", tag="slot5", align_bytes=64)
+        ds_cut = W - DS0_ON_SCALAR
         weave_words("gpsimd", v1_group, values_tile, 1, 0, N)
         for t in range(PACK):
             dp = product(PACK + t, do0, E5M2, t, v0, E4M3)
-            for cols in [slice(0, W)] if t < PACK - 1 else [slice(0, DS0_ON_SCALAR), slice(DS0_ON_SCALAR, W)]:
+            for cols in [slice(0, W)] if t < PACK - 1 else [slice(ds_cut, W), slice(0, ds_cut)]:
                 nc.vector.tensor_tensor(out=ds_planes[:, t, cols], in0=dp[:, cols], in1=weight[t][:, cols], op=ALU.mult)
         q1_raw = load_rows(qT[1], "slot1")
-        qm0_raw = load_rows(qm[0], "slot2")
+        qm0_rows = qm[0].rearrange("(p j) w -> p j w", j=PACK)
+        qm0_raw = keep.tile([P, PACK, W // 2], F32, name="qm0_raw", tag="slot2", align_bytes=64)
+        nc.sync.dma_start(qm0_raw[:], qm0_rows[:, :, 0 : W // 2])
         do1_raw = load_rows(doT[1], "slot3")
+        qm0_rest = keep.tile([P, PACK, W // 2], F32, name="qm0_rest", tag="rounded0", align_bytes=64)
+        nc.sync.dma_start(qm0_rest[:], qm0_rows[:, :, W // 2 : W])
         q1_group = new_group("group_q1")
         interleave_queries("scalar", q1_group, q1_raw)
         qm0_early = keep.tile([P, W * 2], BF16, name="qm0_early", align_bytes=64)
@@ -229,8 +236,8 @@ def tile_attend_gat_sig_k_kernel(tc, qT, kT, vT, doT, rw, qm, offs, out):
         q1 = new_operand("q1", "weight0_2")
         quantize(q1, q1_group, E4M3)
         ds_group = new_group("group_ds0")
-        interleave("vector", ds_group, ds_planes, DS0_ON_SCALAR, W)
-        interleave("scalar", ds_group, ds_planes, 0, DS0_ON_SCALAR)
+        interleave("vector", ds_group, ds_planes, 0, ds_cut)
+        interleave("scalar", ds_group, ds_planes, ds_cut, W)
         qm0 = new_operand("qm0")
         quantize(qm0, qm0_early, E4M3, 0, W // 2)
         ds0 = new_operand("ds0")
@@ -238,21 +245,22 @@ def tile_attend_gat_sig_k_kernel(tc, qT, kT, vT, doT, rw, qm, offs, out):
 
         v1 = new_operand("v1", "slot5")
         quantize(v1, v1_group, E4M3)
-        factor = keep.tile([P, PACK, W], F32, name="factor1", tag="slot6", align_bytes=64)
+        factor = keep.tile([P, PACK, W], F32, name="factor1", tag="weight0_3", align_bytes=64)
         do1_group = factor[:, 1:3, :].rearrange("p t w -> p (t w)").bitcast(BF16)
         for h in range(2):
             interleave_queries("scalar", do1_group, do1_raw, h * P // 2, (h + 1) * P // 2)
         do1 = new_operand("do1")
         quantize(do1, do1_group, E5M2)
         scores1 = [product(t, q1, E4M3, t, k1, E4M3) for t in range(PACK)]
-        tanh1 = [do1_raw[:, 0:2, 0 : W // 2]] + [do1_raw[:, row, :].rearrange("p (h c) -> p h c", h=2) for row in (2, 0, 2)]
+        tanh1 = [do1_raw[:, 0:2, 0 : W // 2], do1_raw[:, 1:3, W // 2 : W]]
+        tanh1 = tanh1 + [do1_raw[:, row, :].rearrange("p (h c) -> p h c", h=2) for row in (0, 2)]
         nc.scalar.activation(out=tanh1[0], in_=scores1[0][:].rearrange("p (h c) -> p h c", h=2), func=ACT.Tanh, scale=0.5)
         first = product(4, qm0, E4M3, 0, ds0, E5M2)
         nc.scalar.copy(out=do1_raw[:, 3, :], in_=first[:])
         second = product(5, qm0, E4M3, 1, ds0, E5M2)
         dk0 = [do1_raw[:, 3, :]]
         qm0_late = factor[:, 1, :].bitcast(BF16)
-        interleave("gpsimd", qm0_late, qm0_raw[:, :, W // 2 : W], 0, W // 2)
+        interleave("gpsimd", qm0_late, qm0_rest, 0, W // 2)
         nc.vector.quantize_mx(out=qm0[0][:, W // 2 : W].bitcast(E4M3), scales=qm0[1][:, W // 2 : W], in_=qm0_late)
         sq = keep.tile([P, PACK, W], F32, name="weight1", tag="slot4", align_bytes=64)
         for t in range(PACK):

@@ -18,50 +18,47 @@ ALU = mybir.AluOpType
 P = 128
 PACK = 4
 W = 512
+HALF = W // 2
 LIST_COLS = N // 16
-DO0_SPLIT = 76
-KEY_PLANES_ON_SCALAR = 2
-Q0_ON_VECTOR = 80
-K0_ON_SCALAR = 192
-V0_ON_SCALAR = 224
-QM0_ON_GPSIMD = 128
-DS0_ON_SCALAR = 144
-SQUARES_ON_GPSIMD = 2
+Q_ON_VECTOR = 80
+DO0_ON_VECTOR = 56
 
 
 def tile_attend_gat_sig_k_kernel(tc, qT, kT, vT, doT, rw, qm, offs, out):
     nc = tc.nc
     with ExitStack() as ctx:
         keep = ctx.enter_context(tc.tile_pool(name="keep", bufs=1))
-        groups = ctx.enter_context(tc.tile_pool(name="groups", bufs=1))
         psum = ctx.enter_context(tc.psum_pool(name="psum", bufs=1))
 
-        first_plane = keep.tile([P, T], F32, name="plane", tag="slot0", align_bytes=64)
-        nc.sync.dma_start(first_plane[:], kT.rearrange("(p t) n -> p t n", t=PACK)[:, 0, :])
-        offsets = keep.tile([P, B * LIST_COLS], U16, name="offsets")
-        nc.sync.dma_start(offsets[:], offs)
+        def new_tile(shape, dtype, name, tag=None):
+            return keep.tile(shape, dtype, name=name, tag=tag or name, align_bytes=64)
 
-        windows = [keep.tile([P, T], F32, name="window%d" % j) for j in range(D // P)]
-        for window in windows:
-            nc.vector.memset(window[:], 0.0)
-
-        def seq_list(b):
-            return offsets[:, b * LIST_COLS : (b + 1) * LIST_COLS]
-
-        def load_plane(pool_dram, t, slot):
-            plane = keep.tile([P, T], F32, name="plane", tag=slot, align_bytes=64)
+        def load_plane(pool_dram, t, tag):
+            plane = new_tile([P, T], F32, "plane", tag)
             nc.sync.dma_start(plane[:], pool_dram.rearrange("(p t) n -> p t n", t=PACK)[:, t, :])
             return plane
 
-        def load_rows(rows, slot):
-            raw = keep.tile([P, PACK, W], F32, name="raw", tag=slot, align_bytes=64)
-            nc.sync.dma_start(raw[:], rows.rearrange("(p j) w -> p j w", j=PACK))
+        def load_rows(rows, tag, c0=0, c1=W):
+            raw = new_tile([P, PACK, c1 - c0], F32, "raw", tag)
+            nc.sync.dma_start(raw[:], rows.rearrange("(p j) w -> p j w", j=PACK)[:, :, c0:c1])
             return raw
 
-        def new_group(slot=None):
-            if slot is not None:
-                return keep.tile([P, W * PACK], BF16, name="group", tag=slot, align_bytes=64)
-            return groups.tile([P, W * PACK], BF16, name="group", align_bytes=64)
+        key_planes = [load_plane(kT, 0, "a0")]
+        offsets = keep.tile([P, B * LIST_COLS], U16, name="offsets")
+        nc.sync.dma_start(offsets[:], offs)
+        key_planes = key_planes + [load_plane(kT, t, "a%d" % t) for t in range(1, PACK)]
+        q_raw = [load_rows(qT[0], "q0")]
+        gate = new_tile([P, B, PACK], F32, "gate")
+        nc.sync.dma_start(gate[:], rw.rearrange("b (p t) o -> p b (t o)", t=PACK))
+        q_raw.append(load_rows(qT[1], "q1"))
+        value_planes = [load_plane(vT, t, "b%d" % t) for t in range(PACK)]
+
+        windows = [new_tile([P, T], F32, "window%d" % j) for j in range(D // P)]
+        for window in windows:
+            nc.gpsimd.memset(window[:], 0.0)
+
+        def entries(e0, e1):
+            return offsets[:, e0 // 16 : e1 // 16]
 
         def copy_on(engine, dst, src):
             if engine == "vector":
@@ -71,243 +68,203 @@ def tile_attend_gat_sig_k_kernel(tc, qT, kT, vT, doT, rw, qm, offs, out):
             else:
                 nc.scalar.copy(out=dst, in_=src)
 
-        def interleave(engine, group, src, c0=0, c1=W):
+        def indirect_copy(engine, dst, src):
+            if engine == "vector":
+                nc.vector.tensor_copy(out=dst, in_=src)
+            else:
+                nc.scalar.activation(out=dst, in_=src, func=ACT.Copy)
+
+        def interleave(engine, group, src):
             copy_on(
                 engine,
-                group[:, c0 * PACK : c1 * PACK].rearrange("p (c i j) -> p c j i", i=4, j=PACK),
-                src[:, :, c0:c1].rearrange("p j (c i) -> p c j i", i=4),
+                group.rearrange("p (c i j) -> p c j i", i=4, j=PACK),
+                src.rearrange("p j (c i) -> p c j i", i=4),
             )
 
-        def interleave_queries(engine, group, src, m0=0, m1=P):
+        def deal_queries(engine, group, src, m0, m1):
             copy_on(
                 engine,
-                group[:].rearrange("p (t m j) -> p m j t", t=PACK, j=PACK)[:, m0:m1],
+                group.rearrange("p (t m j) -> p m j t", t=PACK, j=PACK)[:, m0:m1],
                 src[:].rearrange("p j (m t) -> p m j t", t=PACK)[:, m0:m1],
             )
 
-        def new_operand(name, slot=None, codes=None):
-            if codes is None:
-                codes = keep.tile([P, W], U32, name=name + "_codes", tag=slot or name + "_codes", align_bytes=64)
-            scales = keep.tile([P, W], U8, name=name + "_scales", tag=name + "_scales", align_bytes=64)
-            return codes, scales
+        def weave_words(engine, group, pairs, b, n0, n1):
+            dst = group[:].bitcast(U32).rearrange("p (n u) -> p n u", u=2)[:, n0:n1]
+            src = pairs[:].bitcast(U32).rearrange("p (b u n) -> p b n u", u=2, n=N)[:, b, n0:n1]
+            copy_on(engine, dst, src)
 
-        def quantize(operand, group, fmt, c0=0, c1=W):
-            codes, scales = operand
-            nc.vector.quantize_mx(
-                out=codes[:, c0:c1].bitcast(fmt), scales=scales[:, c0:c1], in_=group[:, c0 * PACK : c1 * PACK]
-            )
+        def quantize(name, group, fmt, tag=None):
+            words = group.shape[1] // PACK
+            codes = new_tile([P, words], U32, name + "_codes", tag)
+            scales = new_tile([P, words], U8, name + "_scales")
+            nc.vector.quantize_mx(out=codes[:].bitcast(fmt), scales=scales[:], in_=group)
+            return codes, scales, fmt
 
-        def product(bank, stationary, fmt_s, block, moving, fmt_m):
-            acc = psum.tile([P, W], F32, name="acc", tag="bank%d" % bank)
+        def product(acc, stationary, block, moving, n0, n1):
             cols = slice(block * P, (block + 1) * P)
             nc.tensor.matmul_mx(
-                out=acc[:],
-                lhsT=stationary[0][:, cols].bitcast(fmt_s),
+                out=acc,
+                lhsT=stationary[0][:, cols].bitcast(stationary[2]),
                 lhsT_scale=stationary[1][:, cols],
-                rhs=moving[0][:, 0:W].bitcast(fmt_m),
-                rhs_scale=moving[1][:],
+                rhs=moving[0][:, n0:n1].bitcast(moving[2]),
+                rhs_scale=moving[1][:, n0:n1],
                 start=True,
                 stop=True,
             )
+
+        def new_bank(bank):
+            return psum.tile([P, W], F32, name="acc", tag="bank%d" % bank)
+
+        def pair_view(pairs):
+            return pairs[:].rearrange("p (b u n e) -> p b u e n", u=2, e=2, n=N)
+
+        def gather_whole(pairs, plane, t):
+            indirect_copy("vector", pair_view(pairs)[:, :, t // 2, t % 2, :], plane[:].indirect(offsets[:]))
+
+        def gather_one(pairs, plane, t, b):
+            indirect_copy("vector", pair_view(pairs)[:, b, t // 2, t % 2, :], plane[:].indirect(entries(b * N, (b + 1) * N)))
+
+        k_pairs = new_tile([P, B * PACK * N], BF16, "k_pairs")
+        k_rows = new_tile([P, 2, N], BF16, "k_rows")
+        for t in range(2):
+            gather_one(k_pairs, key_planes[t], t, 0)
+            indirect_copy("scalar", k_rows[:, t, :], key_planes[t][:].indirect(entries(N, 2 * N)))
+        copy_on(
+            "scalar",
+            k_pairs[:, 4 * N : 6 * N].rearrange("p (n e) -> p n e", e=2),
+            k_rows[:].rearrange("p e n -> p n e"),
+        )
+        gather_whole(k_pairs, key_planes[2], 2)
+        for b in range(B):
+            gather_one(k_pairs, key_planes[3], 3, b)
+        k_group = [new_tile([P, W * PACK], BF16, "k_group0")]
+        gate_pos = new_tile([P, B * PACK], F32, "gate_pos")
+        gate_neg = new_tile([P, B * PACK], F32, "gate_neg")
+        gate_flat = gate[:].rearrange("p b t -> p (b t)")
+        nc.gpsimd.tensor_scalar(out=gate_pos[:], in0=gate_flat, scalar1=0.25, scalar2=0.0, op0=ALU.mult, op1=ALU.add)
+        nc.gpsimd.tensor_scalar(out=gate_neg[:], in0=gate_flat, scalar1=-0.25, scalar2=0.0, op0=ALU.mult, op1=ALU.add)
+        scores = []
+        for b in range(B):
+            q_group = new_tile([P, W * PACK], BF16, "q_group%d" % b)
+            if b == 0:
+                weave_words("scalar", k_group[0], k_pairs, 0, 0, N)
+            deal_queries("vector", q_group[:], q_raw[b], 0, Q_ON_VECTOR)
+            deal_queries("scalar", q_group[:], q_raw[b], Q_ON_VECTOR, P)
+            if b == 0:
+                k_group.append(new_tile([P, W * PACK], BF16, "k_group1", "q0"))
+                weave_words("scalar", k_group[1], k_pairs, 1, 0, N)
+            k_op = quantize("k%d" % b, k_group[b][:], E4M3)
+            q_op = quantize("q%d" % b, q_group[:], E4M3)
+            banks = [new_bank(b * PACK + t) for t in range(PACK)]
+            for t in range(PACK):
+                product(banks[t][:], q_op, t, k_op, 0, N)
+            scores.append(banks)
+
+        v_pairs = new_tile([P, B * PACK * N], BF16, "v_pairs")
+        for t in range(PACK - 1):
+            gather_whole(v_pairs, value_planes[t], t)
+        for b in range(B):
+            gather_one(v_pairs, value_planes[PACK - 1], PACK - 1, b)
+        do_raw = [load_rows(doT[0], "a0")]
+        qm_raw = {(0, 0): load_rows(qm[0], "a1", 0, HALF)}
+        do_raw.append(load_rows(doT[1], "a2"))
+        qm_raw[(1, 0)] = load_rows(qm[1], "a3", 0, HALF)
+        qm_raw[(0, 1)] = load_rows(qm[0], "q_group0", HALF, W)
+        qm_raw[(1, 1)] = load_rows(qm[1], "q_group1", HALF, W)
+        weights = []
+        for b in range(B):
+            weight = new_tile([P, PACK, N], F32, "weight%d" % b, ("q1", "weight1")[b])
+            for t in range(PACK):
+                nc.scalar.activation(out=weight[:, t, :], in_=scores[b][t][:], func=ACT.Tanh, scale=0.5)
+            for t in range(PACK):
+                nc.scalar.activation(out=weight[:, t, :], in_=weight[:, t, :], func=ACT.Square)
+            for t in range(PACK):
+                col = slice(b * PACK + t, b * PACK + t + 1)
+                nc.gpsimd.tensor_scalar(
+                    out=weight[:, t, :], in0=weight[:, t, :], scalar1=gate_neg[:, col], scalar2=gate_pos[:, col],
+                    op0=ALU.mult, op1=ALU.add,
+                )
+            weights.append(weight)
+
+        def weighted_gradient(b, do_op, v_op, ds_group):
+            for c in range(N // P):
+                acc = new_bank(b * PACK + c)
+                for t in range(PACK):
+                    product(acc[:, t * P : (t + 1) * P], do_op, t, v_op, c * P, (c + 1) * P)
+                nc.vector.tensor_tensor(
+                    out=ds_group[:, c * W : (c + 1) * W].rearrange("p (n i t) -> p n t i", i=2, t=PACK),
+                    in0=acc[:].rearrange("p (t n i) -> p n t i", i=2, t=PACK),
+                    in1=weights[b][:, :, c * P : (c + 1) * P].rearrange("p t (n i) -> p n t i", i=2),
+                    op=ALU.mult,
+                )
+
+        v0_group = new_tile([P, W * PACK], BF16, "v0_group")
+        weave_words("scalar", v0_group, v_pairs, 0, 0, N)
+        v0 = quantize("v0", v0_group[:], E4M3)
+        do0_group = new_tile([P, W * PACK], BF16, "do0_group")
+        deal_queries("vector", do0_group[:], do_raw[0], 0, DO0_ON_VECTOR)
+        deal_queries("scalar", do0_group[:], do_raw[0], DO0_ON_VECTOR, P)
+        do0 = quantize("do0", do0_group[:], E5M2)
+        ds0_group = new_tile([P, W * PACK], BF16, "ds0_group", "k_group0")
+        weighted_gradient(0, do0, v0, ds0_group)
+        v1_group = new_tile([P, W * PACK], BF16, "v1_group", "do0_group")
+        weave_words("gpsimd", v1_group, v_pairs, 1, 0, N)
+        qm_group = new_tile([P, HALF * PACK], BF16, "qm00_group")
+        interleave("scalar", qm_group[:], qm_raw[(0, 0)][:])
+        qm_op = {(0, 0): quantize("qm00", qm_group[:], E4M3, "q1")}
+        ds = [quantize("ds0", ds0_group[:], E5M2)]
+
+        late = new_tile([P, 2 * W * PACK], BF16, "late")
+        do1_group, ds1_group = late[:, 0 : W * PACK], late[:, W * PACK : 2 * W * PACK]
+        deal_queries("scalar", do1_group, do_raw[1], 0, P)
+        qm10_group = new_tile([P, HALF * PACK], BF16, "qm10_group")
+        interleave("scalar", qm10_group[:], qm_raw[(1, 0)][:])
+        v1 = quantize("v1", v1_group[:], E4M3)
+        do1 = quantize("do1", do1_group, E5M2)
+
+        def key_gradient(b, j):
+            acc = new_bank(b * PACK + j)
+            product(acc[:], qm_op[(b, j // 2)], j % 2, ds[b], 0, N)
             return acc
 
-        def prepared(name, engine, src, fmt, queries=False, slot=None, codes_slot=None):
-            group = new_group(slot)
-            for h in range(2):
-                if queries:
-                    interleave_queries(engine, group, src, h * P // 2, (h + 1) * P // 2)
-                else:
-                    interleave(engine, group, src, h * W // 2, (h + 1) * W // 2)
-            operand = new_operand(name, codes_slot)
-            quantize(operand, group, fmt)
-            return operand
+        def scatter(engine, j, dk, e0, e1):
+            step = e1 - e0 if engine == "vector" else HALF
+            for e in range(e0, e1, step):
+                indirect_copy(engine, windows[j][:].indirect(entries(e, e + step)), dk[:, e : e + step])
 
-        def key_gradient(b, j, qm_op, ds_op, slot, bank):
-            acc = product(bank, qm_op, E4M3, j, ds_op, E5M2)
-            dk = keep.tile([P, W], F32, name="dk%d_%d" % (b, j), tag=slot, align_bytes=64)
-            nc.scalar.copy(out=dk[:], in_=acc[:])
-            return dk
+        dk_s = new_tile([P, B * N], F32, "dk_scalar")
+        copy_on("scalar", dk_s[:, 0:N], key_gradient(0, 0)[:])
+        scatter("scalar", 0, dk_s, 0, N)
+        acc01 = key_gradient(0, 1)
 
-        keys_tile = keep.tile([P, B * PACK * N], BF16, name="keys", align_bytes=64)
-        values_tile = keep.tile([P, B * PACK * N], BF16, name="values", align_bytes=64)
-        keys = keys_tile[:].rearrange("p (b u n e) -> p b u e n", b=B, u=2, e=2)
-        values = values_tile[:].rearrange("p (b u n e) -> p b u e n", b=B, u=2, e=2)
+        weighted_gradient(1, do1, v1, ds1_group)
+        interleave("gpsimd", do1_group[:, 0 : HALF * PACK], qm_raw[(0, 1)][:])
+        qm_op[(1, 0)] = quantize("qm10", qm10_group[:], E4M3, "weight1")
+        ds.append(quantize("ds1", ds1_group, E5M2))
+        qm_op[(0, 1)] = quantize("qm01", do1_group[:, 0 : HALF * PACK], E4M3)
 
-        def weave_words(engine, group, pairs, b, n0, n1):
-            dst = group.bitcast(U32).rearrange("p (n u) -> p n u", u=2)[:, n0:n1]
-            src = pairs[:].bitcast(U32).rearrange("p (b u n) -> p b n u", b=B, u=2)[:, b, n0:n1]
-            if engine == "scalar":
-                nc.scalar.copy(out=dst, in_=src)
-            else:
-                nc.gpsimd.tensor_copy(out=dst, in_=src)
+        dk_v = new_tile([P, B * N], F32, "dk_vector", "late")
+        copy_on("scalar", dk_v[:, 0:N], acc01[:])
+        qm11_group = dk_v[:, N : 2 * N].bitcast(BF16)
+        interleave("gpsimd", qm11_group, qm_raw[(1, 1)][:])
+        copy_on("scalar", dk_s[:, N : 2 * N], key_gradient(1, 0)[:])
+        scatter("vector", 1, dk_v, 0, N)
+        scatter("scalar", 0, dk_s, N, 2 * N)
+        nc.sync.dma_start(out[0:P, :], windows[0][:])
+        qm_op[(1, 1)] = quantize("qm11", qm11_group, E4M3)
+        copy_on("vector", dk_v[:, N : 2 * N], key_gradient(1, 1)[:])
+        scatter("vector", 1, dk_v, N, 2 * N)
+        nc.sync.dma_start(out[P : 2 * P, :], windows[1][:])
 
-        for t in range(PACK):
-            plane = first_plane if t == 0 else load_plane(kT, t, "slot%d" % t)
-            if t < KEY_PLANES_ON_SCALAR:
-                nc.vector.tensor_copy(out=keys[:, 0, t // 2, t % 2, :], in_=plane[:].indirect(seq_list(0)))
-                rounded = keep.tile([P, T], BF16, name="rounded%d" % t, align_bytes=64)
-                nc.scalar.activation(out=rounded[:], in_=plane[:], func=ACT.Copy)
-                nc.scalar.activation(out=keys[:, 1, t // 2, t % 2, :], in_=rounded[:].indirect(seq_list(1)), func=ACT.Copy)
-            elif t < PACK - 1:
-                nc.vector.tensor_copy(out=keys[:, :, t // 2, t % 2, :], in_=plane[:].indirect(offsets[:]))
-            else:
-                for b in range(B):
-                    nc.vector.tensor_copy(out=keys[:, b, t // 2, t % 2, :], in_=plane[:].indirect(seq_list(b)))
-        q_raw = load_rows(qT[0], "slot8")
-        gate = keep.tile([P, PACK], F32, name="gate", tag="group_k1", align_bytes=64)
-        nc.sync.dma_start(gate[:], rw[0].rearrange("(p t) o -> p (t o)", t=PACK))
-
-        kq_group = keep.tile([P, 2 * W * PACK], BF16, name="kq_group", align_bytes=64)
-        k_group, q_group = kq_group[:, 0 : W * PACK], kq_group[:, W * PACK : 2 * W * PACK]
-        weave_words("scalar", k_group, keys_tile, 0, 0, K0_ON_SCALAR)
-        weave_words("gpsimd", k_group, keys_tile, 0, K0_ON_SCALAR, N)
-        interleave_queries("vector", q_group, q_raw, 0, Q0_ON_VECTOR)
-        interleave_queries("scalar", q_group, q_raw, Q0_ON_VECTOR, P)
-        kq_codes = keep.tile([P, 2 * W], U32, name="kq_codes", align_bytes=64)
-        kq_scales = keep.tile([P, 2 * W], U8, name="kq_scales", align_bytes=64)
-        nc.vector.quantize_mx(out=kq_codes[:].bitcast(E4M3), scales=kq_scales[:], in_=kq_group[:])
-        k0 = (kq_codes[:, 0:W], kq_scales[:, 0:W])
-        q0 = (kq_codes[:, W : 2 * W], kq_scales[:, W : 2 * W])
-        gate_pos = keep.tile([P, PACK], F32, name="gate_pos")
-        gate_neg = keep.tile([P, PACK], F32, name="gate_neg")
-        nc.scalar.activation(out=gate_pos[:], in_=gate[:], func=ACT.Copy, scale=0.25)
-        nc.scalar.activation(out=gate_neg[:], in_=gate[:], func=ACT.Copy, scale=-0.25)
-        shared = keep.tile([P, 10 * W], BF16, name="shared", tag="group_k1", align_bytes=64)
-        do_group, v1_group, k1_group = shared[:, 0 : 4 * W], shared[:, 2 * W : 6 * W], shared[:, 6 * W : 10 * W]
-        weave_words("scalar", k1_group, keys_tile, 1, 0, N)
-        weight = [keep.tile([P, W], F32, name="weight0_%d" % t, tag="weight0_%d" % t, align_bytes=64) for t in range(PACK)]
-        tanh0 = [keep.tile([P, W], F32, name="tanh%d" % t, align_bytes=64) for t in range(PACK)]
-        for t in range(PACK):
-            nc.scalar.activation(out=tanh0[t][:], in_=product(t, q0, E4M3, t, k0, E4M3)[:], func=ACT.Tanh, scale=0.5)
-        for t in range(PACK):
-            if t < SQUARES_ON_GPSIMD:
-                nc.gpsimd.tensor_tensor(out=weight[t][:], in0=tanh0[t][:], in1=tanh0[t][:], op=ALU.mult)
-            else:
-                nc.scalar.activation(out=weight[t][:], in_=tanh0[t][:], func=ACT.Square)
-        for t in range(PACK):
-            nc.gpsimd.tensor_scalar(
-                out=weight[t][:], in0=weight[t][:], scalar1=gate_neg[:, t : t + 1],
-                scalar2=gate_pos[:, t : t + 1], op0=ALU.mult, op1=ALU.add,
-            )
-
-        for t, slot in ((0, "slot4"), (2, "slot5")):
-            plane = load_plane(vT, t, slot)
-            nc.vector.tensor_copy(out=values[:, :, t // 2, 0, :], in_=plane[:].indirect(offsets[:]))
-        plane = load_plane(vT, 1, "slot7")
-        nc.vector.tensor_copy(out=values[:, 0, 0, 1, :], in_=plane[:].indirect(seq_list(0)))
-        rounded = keep.tile([P, T], BF16, name="rounded_v1", tag="slot4", align_bytes=64)
-        nc.scalar.activation(out=rounded[:], in_=plane[:], func=ACT.Copy)
-        nc.scalar.activation(out=values[:, 1, 0, 1, :], in_=rounded[:].indirect(seq_list(1)), func=ACT.Copy)
-        plane = load_plane(vT, 3, "slot6")
-        for b in range(B):
-            nc.vector.tensor_copy(out=values[:, b, 1, 1, :], in_=plane[:].indirect(seq_list(b)))
-        do_raw = load_rows(doT[0], "slot0")
-        v_group = new_group("slot7")
-        weave_words("scalar", v_group[:], values_tile, 0, 0, V0_ON_SCALAR)
-        weave_words("gpsimd", v_group[:], values_tile, 0, V0_ON_SCALAR, N)
-        interleave_queries("scalar", do_group, do_raw, 0, DO0_SPLIT)
-        interleave_queries("vector", do_group, do_raw, DO0_SPLIT, P)
-        v0 = new_operand("v0")
-        quantize(v0, v_group, E4M3)
-        do0 = new_operand("do0")
-        for u in range(2):
-            quantize(do0, do_group, E5M2, u * W // 2, (u + 1) * W // 2)
-        k1 = new_operand("k1", "slot0")
-        quantize(k1, k1_group, E4M3)
-        ds_planes = keep.tile([P, PACK, W], F32, name="ds_planes", tag="slot5", align_bytes=64)
-        ds_cut = W - DS0_ON_SCALAR
-        weave_words("gpsimd", v1_group, values_tile, 1, 0, N)
-        for t in range(PACK):
-            dp = product(PACK + t, do0, E5M2, t, v0, E4M3)
-            for cols in [slice(0, W)] if t < PACK - 1 else [slice(ds_cut, W), slice(0, ds_cut)]:
-                nc.vector.tensor_tensor(out=ds_planes[:, t, cols], in0=dp[:, cols], in1=weight[t][:, cols], op=ALU.mult)
-        q1_raw = load_rows(qT[1], "slot1")
-        qm0_rows = qm[0].rearrange("(p j) w -> p j w", j=PACK)
-        qm0_raw = keep.tile([P, PACK, W // 2], F32, name="qm0_raw", tag="slot2", align_bytes=64)
-        nc.sync.dma_start(qm0_raw[:], qm0_rows[:, :, 0 : W // 2])
-        do1_raw = load_rows(doT[1], "slot3")
-        qm0_rest = keep.tile([P, PACK, W // 2], F32, name="qm0_rest", tag="rounded0", align_bytes=64)
-        nc.sync.dma_start(qm0_rest[:], qm0_rows[:, :, W // 2 : W])
-        q1_group = new_group("group_q1")
-        interleave_queries("scalar", q1_group, q1_raw)
-        qm0_early = keep.tile([P, W * 2], BF16, name="qm0_early", align_bytes=64)
-        interleave("gpsimd", qm0_early, qm0_raw, 0, QM0_ON_GPSIMD)
-        interleave("scalar", qm0_early, qm0_raw, QM0_ON_GPSIMD, W // 2)
-        q1 = new_operand("q1", "weight0_2")
-        quantize(q1, q1_group, E4M3)
-        ds_group = new_group("group_ds0")
-        interleave("vector", ds_group, ds_planes, 0, ds_cut)
-        interleave("scalar", ds_group, ds_planes, ds_cut, W)
-        qm0 = new_operand("qm0")
-        quantize(qm0, qm0_early, E4M3, 0, W // 2)
-        ds0 = new_operand("ds0")
-        quantize(ds0, ds_group, E5M2)
-
-        v1 = new_operand("v1", "slot5")
-        quantize(v1, v1_group, E4M3)
-        factor = keep.tile([P, PACK, W], F32, name="factor1", tag="weight0_3", align_bytes=64)
-        do1_group = factor[:, 1:3, :].rearrange("p t w -> p (t w)").bitcast(BF16)
-        for h in range(2):
-            interleave_queries("scalar", do1_group, do1_raw, h * P // 2, (h + 1) * P // 2)
-        do1 = new_operand("do1")
-        quantize(do1, do1_group, E5M2)
-        scores1 = [product(t, q1, E4M3, t, k1, E4M3) for t in range(PACK)]
-        tanh1 = [do1_raw[:, 0:2, 0 : W // 2], do1_raw[:, 1:3, W // 2 : W]]
-        tanh1 = tanh1 + [do1_raw[:, row, :].rearrange("p (h c) -> p h c", h=2) for row in (0, 2)]
-        nc.scalar.activation(out=tanh1[0], in_=scores1[0][:].rearrange("p (h c) -> p h c", h=2), func=ACT.Tanh, scale=0.5)
-        first = product(4, qm0, E4M3, 0, ds0, E5M2)
-        nc.scalar.copy(out=do1_raw[:, 3, :], in_=first[:])
-        second = product(5, qm0, E4M3, 1, ds0, E5M2)
-        dk0 = [do1_raw[:, 3, :]]
-        qm0_late = factor[:, 1, :].bitcast(BF16)
-        interleave("gpsimd", qm0_late, qm0_rest, 0, W // 2)
-        nc.vector.quantize_mx(out=qm0[0][:, W // 2 : W].bitcast(E4M3), scales=qm0[1][:, W // 2 : W], in_=qm0_late)
-        sq = keep.tile([P, PACK, W], F32, name="weight1", tag="slot4", align_bytes=64)
-        for t in range(PACK):
-            if t > 0:
-                nc.scalar.activation(out=tanh1[t], in_=scores1[t][:].rearrange("p (h c) -> p h c", h=2), func=ACT.Tanh, scale=0.5)
-            nc.scalar.activation(out=sq[:, t, :].rearrange("p (h c) -> p h c", h=2), in_=tanh1[t], func=ACT.Square)
-            nc.gpsimd.tensor_scalar(out=factor[:, t, :], in0=sq[:, t, :], scalar1=-0.25, scalar2=0.25, op0=ALU.mult, op1=ALU.add)
-            if t == 1:
-                nc.scalar.copy(out=do1_raw[:, 1, :], in_=second[:])
-                dk0.append(do1_raw[:, 1, :])
-        gated = keep.tile([P, PACK, W], F32, name="gated", tag="slot7", align_bytes=64)
-        dp1 = [product(bank, do1, E5M2, t, v1, E4M3) for t, bank in enumerate((6, 7, 4, 0))]
-        qm1_raw = load_rows(qm[1], "slot8")
-        gate1 = keep.tile([P, PACK], F32, name="gate1")
-        nc.sync.dma_start(gate1[:], rw[1].rearrange("(p t) o -> p (t o)", t=PACK))
-        ds_group = new_group()
-        halves = (slice(0, W // 2), slice(W // 2, W))
-
-        def ds1_half(cols):
-            for t in range(PACK):
-                nc.scalar.activation(out=gated[:, t, cols], in_=dp1[t][:, cols], func=ACT.Copy, scale=gate1[:, t : t + 1])
-            nc.gpsimd.tensor_tensor(
-                out=ds_group[:, cols.start * PACK : cols.stop * PACK].rearrange("p (c i t) -> p c t i", i=4, t=PACK),
-                in0=factor[:, :, cols].rearrange("p t (c i) -> p c t i", i=4),
-                in1=gated[:, :, cols].rearrange("p t (c i) -> p c t i", i=4),
-                op=ALU.mult,
-            )
-
-        ds1_half(slice(0, 192))
-        third = product(1, qm0, E4M3, 2, ds0, E5M2)
-        nc.scalar.copy(out=do1_raw[:, 2, :], in_=third[:])
-        dk0.append(do1_raw[:, 2, :])
-        ds1_half(slice(192, W))
-        last = product(2, qm0, E4M3, 3, ds0, E5M2)
-        last_a = keep.tile([P, W // 2], F32, name="last_a", tag="v1_scales", align_bytes=64)
-        nc.scalar.copy(out=last_a[:], in_=last[:, halves[0]])
-        qm1 = prepared("qm1", "scalar", qm1_raw, E4M3, slot="do1_codes")
-        ds1 = new_operand("ds1", "slot8")
-        quantize(ds1, ds_group, E5M2)
-        last_b = keep.tile([P, W // 2], F32, name="last_b", tag="slot7", align_bytes=64)
-        nc.scalar.copy(out=last_b[:], in_=last[:, halves[1]])
-        dk1 = [key_gradient(1, j, qm1, ds1, "dk1_%d" % j, PACK + j) for j in range(D // P)]
-
-        for j in range(D // P - 1):
-            nc.vector.tensor_copy(out=windows[j][:].indirect(seq_list(0)), in_=dk0[j])
-        nc.vector.tensor_copy(out=windows[3][:].indirect(offsets[:, 0 : LIST_COLS // 2]), in_=last_a[:])
-        nc.vector.tensor_copy(out=windows[3][:].indirect(offsets[:, LIST_COLS // 2 : LIST_COLS]), in_=last_b[:])
-        for j in range(D // P):
-            nc.vector.tensor_copy(out=windows[j][:].indirect(seq_list(1)), in_=dk1[j][:])
-            nc.sync.dma_start(out[j * P : (j + 1) * P, :], windows[j][:])
+        dk_s = new_tile([P, B * N], F32, "dk_scalar")
+        dk_v = new_tile([P, B * N], F32, "dk_vector", "late")
+        copy_on("scalar", dk_s[:, 0:N], key_gradient(0, 2)[:])
+        scatter("scalar", 2, dk_s, 0, N)
+        copy_on("vector", dk_v[:, 0:N], key_gradient(0, 3)[:])
+        scatter("vector", 3, dk_v, 0, N)
+        copy_on("scalar", dk_s[:, N : 2 * N], key_gradient(1, 2)[:])
+        copy_on("scalar", dk_v[:, N : 2 * N], key_gradient(1, 3)[:])
+        scatter("scalar", 2, dk_s, N, 2 * N)
+        nc.scalar.dma_start(out[2 * P : 3 * P, :], windows[2][:])
+        scatter("vector", 3, dk_v, N, 2 * N)
+        nc.sync.dma_start(out[3 * P : 4 * P, :], windows[3][:])

@@ -8,6 +8,7 @@ FLOPS = 3 * 2 * B * N * D * R
 F32 = mybir.dt.float32
 BF16 = mybir.dt.bfloat16
 U32 = mybir.dt.uint32
+I32 = mybir.dt.int32
 U16 = mybir.dt.uint16
 U8 = mybir.dt.uint8
 E4M3 = mybir.dt.float8_e4m3fn_x4
@@ -20,8 +21,9 @@ PACK = 4
 W = 512
 HALF = W // 2
 LIST_COLS = N // 16
-Q_ON_VECTOR = 80
-DO0_ON_VECTOR = 56
+Q_ON_VECTOR = (88, 88)
+DO0_ON_VECTOR = 88
+SCALAR_PIECE = 384
 
 
 def tile_attend_gat_sig_k_kernel(tc, qT, kT, vT, doT, rw, qm, offs, out):
@@ -46,16 +48,16 @@ def tile_attend_gat_sig_k_kernel(tc, qT, kT, vT, doT, rw, qm, offs, out):
         key_planes = [load_plane(kT, 0, "a0")]
         offsets = keep.tile([P, B * LIST_COLS], U16, name="offsets")
         nc.sync.dma_start(offsets[:], offs)
-        key_planes = key_planes + [load_plane(kT, t, "a%d" % t) for t in range(1, PACK)]
-        q_raw = [load_rows(qT[0], "q0")]
         gate = new_tile([P, B, PACK], F32, "gate")
         nc.sync.dma_start(gate[:], rw.rearrange("b (p t) o -> p b (t o)", t=PACK))
+        key_planes = key_planes + [load_plane(kT, t, "a%d" % t) for t in range(1, PACK)]
+        q_raw = [load_rows(qT[0], "q0")]
         q_raw.append(load_rows(qT[1], "q1"))
         value_planes = [load_plane(vT, t, "b%d" % t) for t in range(PACK)]
 
         windows = [new_tile([P, T], F32, "window%d" % j) for j in range(D // P)]
         for window in windows:
-            nc.gpsimd.memset(window[:], 0.0)
+            nc.vector.memset(window[:], 0.0)
 
         def entries(e0, e1):
             return offsets[:, e0 // 16 : e1 // 16]
@@ -89,13 +91,15 @@ def tile_attend_gat_sig_k_kernel(tc, qT, kT, vT, doT, rw, qm, offs, out):
             )
 
         def weave_words(engine, group, pairs, b, n0, n1):
-            dst = group[:].bitcast(U32).rearrange("p (n u) -> p n u", u=2)[:, n0:n1]
-            src = pairs[:].bitcast(U32).rearrange("p (b u n) -> p b n u", u=2, n=N)[:, b, n0:n1]
+            word = I32 if engine == "vector" else U32
+            dst = group[:].bitcast(word).rearrange("p (n u) -> p n u", u=2)[:, n0:n1]
+            src = pairs[:].bitcast(word).rearrange("p (b u n) -> p b n u", u=2, n=N)[:, b, n0:n1]
             copy_on(engine, dst, src)
 
-        def quantize(name, group, fmt, tag=None):
+        def quantize(name, group, fmt, tag=None, codes=None):
             words = group.shape[1] // PACK
-            codes = new_tile([P, words], U32, name + "_codes", tag)
+            if codes is None:
+                codes = new_tile([P, words], U32, name + "_codes", tag)
             scales = new_tile([P, words], U8, name + "_scales")
             nc.vector.quantize_mx(out=codes[:].bitcast(fmt), scales=scales[:], in_=group)
             return codes, scales, fmt
@@ -125,18 +129,16 @@ def tile_attend_gat_sig_k_kernel(tc, qT, kT, vT, doT, rw, qm, offs, out):
             indirect_copy("vector", pair_view(pairs)[:, b, t // 2, t % 2, :], plane[:].indirect(entries(b * N, (b + 1) * N)))
 
         k_pairs = new_tile([P, B * PACK * N], BF16, "k_pairs")
-        k_rows = new_tile([P, 2, N], BF16, "k_rows")
-        for t in range(2):
+        k_rows = new_tile([P, PACK, N], BF16, "k_rows")
+        for t in range(PACK):
             gather_one(k_pairs, key_planes[t], t, 0)
             indirect_copy("scalar", k_rows[:, t, :], key_planes[t][:].indirect(entries(N, 2 * N)))
-        copy_on(
-            "scalar",
-            k_pairs[:, 4 * N : 6 * N].rearrange("p (n e) -> p n e", e=2),
-            k_rows[:].rearrange("p e n -> p n e"),
-        )
-        gather_whole(k_pairs, key_planes[2], 2)
-        for b in range(B):
-            gather_one(k_pairs, key_planes[3], 3, b)
+            if t % 2 == 1:
+                copy_on(
+                    "scalar",
+                    k_pairs[:, (PACK + t - 1) * N : (PACK + t + 1) * N].rearrange("p (n e) -> p n e", e=2),
+                    k_rows[:, t - 1 : t + 1, :].rearrange("p e n -> p n e"),
+                )
         k_group = [new_tile([P, W * PACK], BF16, "k_group0")]
         gate_pos = new_tile([P, B * PACK], F32, "gate_pos")
         gate_neg = new_tile([P, B * PACK], F32, "gate_neg")
@@ -147,13 +149,15 @@ def tile_attend_gat_sig_k_kernel(tc, qT, kT, vT, doT, rw, qm, offs, out):
         for b in range(B):
             q_group = new_tile([P, W * PACK], BF16, "q_group%d" % b)
             if b == 0:
-                weave_words("scalar", k_group[0], k_pairs, 0, 0, N)
-            deal_queries("vector", q_group[:], q_raw[b], 0, Q_ON_VECTOR)
-            deal_queries("scalar", q_group[:], q_raw[b], Q_ON_VECTOR, P)
+                weave_words("vector", k_group[0], k_pairs, 0, 0, N)
+                k_op = quantize("k0", k_group[0][:], E4M3)
+            deal_queries("vector", q_group[:], q_raw[b], 0, Q_ON_VECTOR[b])
+            deal_queries("scalar", q_group[:], q_raw[b], Q_ON_VECTOR[b], P)
             if b == 0:
                 k_group.append(new_tile([P, W * PACK], BF16, "k_group1", "q0"))
                 weave_words("scalar", k_group[1], k_pairs, 1, 0, N)
-            k_op = quantize("k%d" % b, k_group[b][:], E4M3)
+            else:
+                k_op = quantize("k1", k_group[1][:], E4M3)
             q_op = quantize("q%d" % b, q_group[:], E4M3)
             banks = [new_bank(b * PACK + t) for t in range(PACK)]
             for t in range(PACK):
@@ -176,7 +180,9 @@ def tile_attend_gat_sig_k_kernel(tc, qT, kT, vT, doT, rw, qm, offs, out):
             weight = new_tile([P, PACK, N], F32, "weight%d" % b, ("q1", "weight1")[b])
             for t in range(PACK):
                 nc.scalar.activation(out=weight[:, t, :], in_=scores[b][t][:], func=ACT.Tanh, scale=0.5)
-            for t in range(PACK):
+                if t == 2:
+                    nc.scalar.activation(out=weight[:, 0:2, :], in_=weight[:, 0:2, :], func=ACT.Square)
+            for t in range(2, PACK):
                 nc.scalar.activation(out=weight[:, t, :], in_=weight[:, t, :], func=ACT.Square)
             for t in range(PACK):
                 col = slice(b * PACK + t, b * PACK + t + 1)
@@ -186,85 +192,104 @@ def tile_attend_gat_sig_k_kernel(tc, qT, kT, vT, doT, rw, qm, offs, out):
                 )
             weights.append(weight)
 
-        def weighted_gradient(b, do_op, v_op, ds_group):
-            for c in range(N // P):
+        def weighted_gradient(b, do_op, v_op, ds_group, blocks):
+            for c in blocks:
                 acc = new_bank(b * PACK + c)
                 for t in range(PACK):
                     product(acc[:, t * P : (t + 1) * P], do_op, t, v_op, c * P, (c + 1) * P)
                 nc.vector.tensor_tensor(
-                    out=ds_group[:, c * W : (c + 1) * W].rearrange("p (n i t) -> p n t i", i=2, t=PACK),
-                    in0=acc[:].rearrange("p (t n i) -> p n t i", i=2, t=PACK),
-                    in1=weights[b][:, :, c * P : (c + 1) * P].rearrange("p t (n i) -> p n t i", i=2),
+                    out=ds_group[:, c * W : (c + 1) * W].rearrange("p (n i t) -> p n t i", i=4, t=PACK),
+                    in0=acc[:].rearrange("p (t n i) -> p n t i", i=4, t=PACK),
+                    in1=weights[b][:, :, c * P : (c + 1) * P].rearrange("p t (n i) -> p n t i", i=4),
                     op=ALU.mult,
                 )
 
         v0_group = new_tile([P, W * PACK], BF16, "v0_group")
         weave_words("scalar", v0_group, v_pairs, 0, 0, N)
-        v0 = quantize("v0", v0_group[:], E4M3)
         do0_group = new_tile([P, W * PACK], BF16, "do0_group")
         deal_queries("vector", do0_group[:], do_raw[0], 0, DO0_ON_VECTOR)
         deal_queries("scalar", do0_group[:], do_raw[0], DO0_ON_VECTOR, P)
+        v0 = quantize("v0", v0_group[:], E4M3)
         do0 = quantize("do0", do0_group[:], E5M2)
-        ds0_group = new_tile([P, W * PACK], BF16, "ds0_group", "k_group0")
-        weighted_gradient(0, do0, v0, ds0_group)
-        v1_group = new_tile([P, W * PACK], BF16, "v1_group", "do0_group")
-        weave_words("gpsimd", v1_group, v_pairs, 1, 0, N)
         qm_group = new_tile([P, HALF * PACK], BF16, "qm00_group")
         interleave("scalar", qm_group[:], qm_raw[(0, 0)][:])
-        qm_op = {(0, 0): quantize("qm00", qm_group[:], E4M3, "q1")}
-        ds = [quantize("ds0", ds0_group[:], E5M2)]
-
+        qm_op = {(0, 0): quantize("qm00", qm_group[:], E4M3, "do0_group")}
+        v1_group = new_tile([P, W * PACK], BF16, "v1_group", "qm00_group")
+        weave_words("gpsimd", v1_group, v_pairs, 1, 0, N)
         late = new_tile([P, 2 * W * PACK], BF16, "late")
         do1_group, ds1_group = late[:, 0 : W * PACK], late[:, W * PACK : 2 * W * PACK]
         deal_queries("scalar", do1_group, do_raw[1], 0, P)
+
+        def scatter(engine, j, e0, src):
+            indirect_copy(engine, windows[j][:].indirect(entries(e0, e0 + src.shape[1])), src)
+
+        def store(queue, j):
+            queue.dma_start(out[j * P : (j + 1) * P, :], windows[j][:])
+
+        halves = (slice(0, HALF), slice(HALF, W))
+        ds0_group = new_tile([P, W * PACK], BF16, "ds0_group", "k_group0")
+        ds0 = (new_tile([P, W], U32, "ds0_codes"), new_tile([P, W], U8, "ds0_scales"), E5M2)
+        for h, cols in enumerate(halves):
+            weighted_gradient(0, do0, v0, ds0_group, range(2 * h, 2 * h + 2))
+            nc.vector.quantize_mx(
+                out=ds0[0][:, cols].bitcast(E5M2), scales=ds0[1][:, cols],
+                in_=ds0_group[:, cols.start * PACK : cols.stop * PACK],
+            )
+            acc = new_bank(2 * h)
+            for j in range(2):
+                product(acc[:, halves[j]], qm_op[(0, 0)], j, ds0, cols.start, cols.stop)
+            if h == 0:
+                early = new_tile([P, W], F32, "early")
+                copy_on("scalar", early[:], acc[:])
+                for j in range(2):
+                    scatter("scalar", j, cols.start, early[:, halves[j]])
+        ds = [ds0]
+
         qm10_group = new_tile([P, HALF * PACK], BF16, "qm10_group")
         interleave("scalar", qm10_group[:], qm_raw[(1, 0)][:])
-        v1 = quantize("v1", v1_group[:], E4M3)
-        do1 = quantize("do1", do1_group, E5M2)
+        codes = new_tile([P, 2 * W], U32, "v1_do1_codes", "k_group0")
+        v1 = quantize("v1", v1_group[:], E4M3, codes=codes[:, 0:W])
+        do1 = quantize("do1", do1_group, E5M2, codes=codes[:, W : 2 * W])
+        qm_op[(1, 0)] = quantize("qm10", qm10_group[:], E4M3)
+        early = do1_group[:, 0 : HALF * PACK].bitcast(F32)
+        copy_on("vector", early, acc[:])
+        for j in range(2):
+            scatter("scalar", j, HALF, early[:, halves[j]])
 
         def key_gradient(b, j):
-            acc = new_bank(b * PACK + j)
+            acc = new_bank((PACK, 1)[j - 2] if b == 0 else (PACK, PACK + 1, 3, PACK + 2)[j])
             product(acc[:], qm_op[(b, j // 2)], j % 2, ds[b], 0, N)
             return acc
 
-        def scatter(engine, j, dk, e0, e1):
-            step = e1 - e0 if engine == "vector" else HALF
-            for e in range(e0, e1, step):
-                indirect_copy(engine, windows[j][:].indirect(entries(e, e + step)), dk[:, e : e + step])
-
-        dk_s = new_tile([P, B * N], F32, "dk_scalar")
-        copy_on("scalar", dk_s[:, 0:N], key_gradient(0, 0)[:])
-        scatter("scalar", 0, dk_s, 0, N)
-        acc01 = key_gradient(0, 1)
-
-        weighted_gradient(1, do1, v1, ds1_group)
-        interleave("gpsimd", do1_group[:, 0 : HALF * PACK], qm_raw[(0, 1)][:])
-        qm_op[(1, 0)] = quantize("qm10", qm10_group[:], E4M3, "weight1")
+        weighted_gradient(1, do1, v1, ds1_group, range(N // P))
+        interleave("gpsimd", do1_group[:, HALF * PACK : W * PACK], qm_raw[(0, 1)][:])
+        qm_op[(0, 1)] = quantize("qm01", do1_group[:, HALF * PACK : W * PACK], E4M3)
         ds.append(quantize("ds1", ds1_group, E5M2))
-        qm_op[(0, 1)] = quantize("qm01", do1_group[:, 0 : HALF * PACK], E4M3)
 
-        dk_v = new_tile([P, B * N], F32, "dk_vector", "late")
-        copy_on("scalar", dk_v[:, 0:N], acc01[:])
-        qm11_group = dk_v[:, N : 2 * N].bitcast(BF16)
+        qm11_group = late[:, 3 * W : 5 * W]
         interleave("gpsimd", qm11_group, qm_raw[(1, 1)][:])
-        copy_on("scalar", dk_s[:, N : 2 * N], key_gradient(1, 0)[:])
-        scatter("vector", 1, dk_v, 0, N)
-        scatter("scalar", 0, dk_s, N, 2 * N)
-        nc.sync.dma_start(out[0:P, :], windows[0][:])
+        dk2 = new_tile([P, B * N], F32, "dk2")
+        dk3 = new_tile([P, B * N], F32, "dk3")
+        copy_on("vector", dk3[:, 0:N], key_gradient(0, 3)[:])
+        dk10 = new_tile([P, N], F32, "dk10")
+        copy_on("vector", dk10[:], key_gradient(1, 0)[:])
+        scatter("vector", 0, N, dk10[:])
+        store(nc.sync, 0)
         qm_op[(1, 1)] = quantize("qm11", qm11_group, E4M3)
-        copy_on("vector", dk_v[:, N : 2 * N], key_gradient(1, 1)[:])
-        scatter("vector", 1, dk_v, N, 2 * N)
-        nc.sync.dma_start(out[P : 2 * P, :], windows[1][:])
 
-        dk_s = new_tile([P, B * N], F32, "dk_scalar")
-        dk_v = new_tile([P, B * N], F32, "dk_vector", "late")
-        copy_on("scalar", dk_s[:, 0:N], key_gradient(0, 2)[:])
-        scatter("scalar", 2, dk_s, 0, N)
-        copy_on("vector", dk_v[:, 0:N], key_gradient(0, 3)[:])
-        scatter("vector", 3, dk_v, 0, N)
-        copy_on("scalar", dk_s[:, N : 2 * N], key_gradient(1, 2)[:])
-        copy_on("scalar", dk_v[:, N : 2 * N], key_gradient(1, 3)[:])
-        scatter("scalar", 2, dk_s, N, 2 * N)
-        nc.scalar.dma_start(out[2 * P : 3 * P, :], windows[2][:])
-        scatter("vector", 3, dk_v, N, 2 * N)
-        nc.sync.dma_start(out[3 * P : 4 * P, :], windows[3][:])
+        dk11 = new_tile([P, N], F32, "dk11")
+        copy_on("scalar", dk11[:], key_gradient(1, 1)[:])
+        scatter("scalar", 1, N, dk11[:, halves[0]])
+        copy_on("scalar", dk2[:, 0:N], key_gradient(0, 2)[:])
+        scatter("scalar", 1, N + HALF, dk11[:, halves[1]])
+        store(nc.sync, 1)
+        scatter("scalar", 2, 0, dk2[:, 0:HALF])
+
+        copy_on("vector", dk2[:, N : 2 * N], key_gradient(1, 2)[:])
+        copy_on("vector", dk3[:, N : 2 * N], key_gradient(1, 3)[:])
+        scatter("vector", 2, HALF, dk2[:, HALF : 2 * N])
+        store(nc.sync, 2)
+
+        for e0, e1 in ((HALF, HALF + SCALAR_PIECE), (HALF + SCALAR_PIECE, 2 * N), (0, HALF)):
+            scatter("scalar", 3, e0, dk3[:, e0:e1])
+        store(nc.scalar, 3)

@@ -21,9 +21,10 @@ PACK = 4
 W = 512
 HALF = W // 2
 LIST_COLS = N // 16
-Q_ON_VECTOR = (88, 88)
-DO0_ON_VECTOR = 88
+Q1_ON_VECTOR = 72
+DO0_ON_VECTOR = 96
 SCALAR_PIECE = 384
+LAST_ON_SCALAR = 256
 
 
 def tile_attend_gat_sig_k_kernel(tc, qT, kT, vT, doT, rw, qm, offs, out):
@@ -129,36 +130,36 @@ def tile_attend_gat_sig_k_kernel(tc, qT, kT, vT, doT, rw, qm, offs, out):
             indirect_copy("vector", pair_view(pairs)[:, b, t // 2, t % 2, :], plane[:].indirect(entries(b * N, (b + 1) * N)))
 
         k_pairs = new_tile([P, B * PACK * N], BF16, "k_pairs")
-        k_rows = new_tile([P, PACK, N], BF16, "k_rows")
-        for t in range(PACK):
+        k_rows = new_tile([P, 2, N], BF16, "k_rows")
+        for t in range(2):
             gather_one(k_pairs, key_planes[t], t, 0)
             indirect_copy("scalar", k_rows[:, t, :], key_planes[t][:].indirect(entries(N, 2 * N)))
-            if t % 2 == 1:
-                copy_on(
-                    "scalar",
-                    k_pairs[:, (PACK + t - 1) * N : (PACK + t + 1) * N].rearrange("p (n e) -> p n e", e=2),
-                    k_rows[:, t - 1 : t + 1, :].rearrange("p e n -> p n e"),
-                )
-        k_group = [new_tile([P, W * PACK], BF16, "k_group0")]
+        copy_on(
+            "scalar",
+            k_pairs[:, PACK * N : (PACK + 2) * N].rearrange("p (n e) -> p n e", e=2),
+            k_rows[:].rearrange("p e n -> p n e"),
+        )
+        gather_whole(k_pairs, key_planes[2], 2)
+        for b in range(B):
+            gather_one(k_pairs, key_planes[3], 3, b)
         gate_pos = new_tile([P, B * PACK], F32, "gate_pos")
         gate_neg = new_tile([P, B * PACK], F32, "gate_neg")
         gate_flat = gate[:].rearrange("p b t -> p (b t)")
         nc.gpsimd.tensor_scalar(out=gate_pos[:], in0=gate_flat, scalar1=0.25, scalar2=0.0, op0=ALU.mult, op1=ALU.add)
         nc.gpsimd.tensor_scalar(out=gate_neg[:], in0=gate_flat, scalar1=-0.25, scalar2=0.0, op0=ALU.mult, op1=ALU.add)
+        q_group = [new_tile([P, W * PACK], BF16, "q_group%d" % b) for b in range(B)]
+        k0_group = new_tile([P, W * PACK], BF16, "k_group0")
+        weave_words("scalar", k0_group, k_pairs, 0, 0, N)
+        deal_queries("vector", q_group[0][:], q_raw[0], 0, P)
+        k_group = [k0_group, new_tile([P, W * PACK], BF16, "k_group1")]
+        weave_words("scalar", k_group[1], k_pairs, 1, 0, N)
         scores = []
         for b in range(B):
-            q_group = new_tile([P, W * PACK], BF16, "q_group%d" % b)
-            if b == 0:
-                weave_words("vector", k_group[0], k_pairs, 0, 0, N)
-                k_op = quantize("k0", k_group[0][:], E4M3)
-            deal_queries("vector", q_group[:], q_raw[b], 0, Q_ON_VECTOR[b])
-            deal_queries("scalar", q_group[:], q_raw[b], Q_ON_VECTOR[b], P)
-            if b == 0:
-                k_group.append(new_tile([P, W * PACK], BF16, "k_group1", "q0"))
-                weave_words("scalar", k_group[1], k_pairs, 1, 0, N)
-            else:
-                k_op = quantize("k1", k_group[1][:], E4M3)
-            q_op = quantize("q%d" % b, q_group[:], E4M3)
+            if b == 1:
+                deal_queries("vector", q_group[1][:], q_raw[1], 0, Q1_ON_VECTOR)
+                deal_queries("scalar", q_group[1][:], q_raw[1], Q1_ON_VECTOR, P)
+            k_op = quantize("k%d" % b, k_group[b][:], E4M3, ("q0", "q_group0")[b])
+            q_op = quantize("q%d" % b, q_group[b][:], E4M3)
             banks = [new_bank(b * PACK + t) for t in range(PACK)]
             for t in range(PACK):
                 product(banks[t][:], q_op, t, k_op, 0, N)
@@ -170,10 +171,10 @@ def tile_attend_gat_sig_k_kernel(tc, qT, kT, vT, doT, rw, qm, offs, out):
         for b in range(B):
             gather_one(v_pairs, value_planes[PACK - 1], PACK - 1, b)
         do_raw = [load_rows(doT[0], "a0")]
-        qm_raw = {(0, 0): load_rows(qm[0], "a1", 0, HALF)}
-        do_raw.append(load_rows(doT[1], "a2"))
+        do_raw.append(load_rows(doT[1], "a1"))
+        qm_raw = {(0, 0): load_rows(qm[0], "a2", 0, HALF)}
         qm_raw[(1, 0)] = load_rows(qm[1], "a3", 0, HALF)
-        qm_raw[(0, 1)] = load_rows(qm[0], "q_group0", HALF, W)
+        qm_raw[(0, 1)] = load_rows(qm[0], "k_group1", HALF, W)
         qm_raw[(1, 1)] = load_rows(qm[1], "q_group1", HALF, W)
         weights = []
         for b in range(B):
@@ -211,11 +212,9 @@ def tile_attend_gat_sig_k_kernel(tc, qT, kT, vT, doT, rw, qm, offs, out):
         deal_queries("scalar", do0_group[:], do_raw[0], DO0_ON_VECTOR, P)
         v0 = quantize("v0", v0_group[:], E4M3)
         do0 = quantize("do0", do0_group[:], E5M2)
-        qm_group = new_tile([P, HALF * PACK], BF16, "qm00_group")
-        interleave("scalar", qm_group[:], qm_raw[(0, 0)][:])
-        qm_op = {(0, 0): quantize("qm00", qm_group[:], E4M3, "do0_group")}
-        v1_group = new_tile([P, W * PACK], BF16, "v1_group", "qm00_group")
-        weave_words("gpsimd", v1_group, v_pairs, 1, 0, N)
+        qm_group = new_tile([P, HALF * PACK], BF16, "qm00_group", "do0_group")
+        interleave("vector", qm_group[:], qm_raw[(0, 0)][:])
+        qm_op = {}
         late = new_tile([P, 2 * W * PACK], BF16, "late")
         do1_group, ds1_group = late[:, 0 : W * PACK], late[:, W * PACK : 2 * W * PACK]
         deal_queries("scalar", do1_group, do_raw[1], 0, P)
@@ -231,6 +230,10 @@ def tile_attend_gat_sig_k_kernel(tc, qT, kT, vT, doT, rw, qm, offs, out):
         ds0 = (new_tile([P, W], U32, "ds0_codes"), new_tile([P, W], U8, "ds0_scales"), E5M2)
         for h, cols in enumerate(halves):
             weighted_gradient(0, do0, v0, ds0_group, range(2 * h, 2 * h + 2))
+            if h == 0:
+                qm_op[(0, 0)] = quantize("qm00", qm_group[:], E4M3, "do0_codes")
+                v1_group = new_tile([P, W * PACK], BF16, "v1_group", "a2")
+                weave_words("gpsimd", v1_group, v_pairs, 1, 0, N)
             nc.vector.quantize_mx(
                 out=ds0[0][:, cols].bitcast(E5M2), scales=ds0[1][:, cols],
                 in_=ds0_group[:, cols.start * PACK : cols.stop * PACK],
@@ -257,7 +260,7 @@ def tile_attend_gat_sig_k_kernel(tc, qT, kT, vT, doT, rw, qm, offs, out):
             scatter("scalar", j, HALF, early[:, halves[j]])
 
         def key_gradient(b, j):
-            acc = new_bank((PACK, 1)[j - 2] if b == 0 else (PACK, PACK + 1, 3, PACK + 2)[j])
+            acc = new_bank((1, 3)[j - 2] if b == 0 else PACK + j)
             product(acc[:], qm_op[(b, j // 2)], j % 2, ds[b], 0, N)
             return acc
 
@@ -268,28 +271,27 @@ def tile_attend_gat_sig_k_kernel(tc, qT, kT, vT, doT, rw, qm, offs, out):
 
         qm11_group = late[:, 3 * W : 5 * W]
         interleave("gpsimd", qm11_group, qm_raw[(1, 1)][:])
+        dk10 = new_tile([P, N], F32, "dk10")
         dk2 = new_tile([P, B * N], F32, "dk2")
         dk3 = new_tile([P, B * N], F32, "dk3")
-        copy_on("vector", dk3[:, 0:N], key_gradient(0, 3)[:])
-        dk10 = new_tile([P, N], F32, "dk10")
         copy_on("vector", dk10[:], key_gradient(1, 0)[:])
+        copy_on("vector", dk3[:, 0:N], key_gradient(0, 3)[:])
+        copy_on("scalar", dk2[:, 0:N], key_gradient(0, 2)[:])
+        acc11 = key_gradient(1, 1)
         scatter("vector", 0, N, dk10[:])
         store(nc.sync, 0)
         qm_op[(1, 1)] = quantize("qm11", qm11_group, E4M3)
-
-        dk11 = new_tile([P, N], F32, "dk11")
-        copy_on("scalar", dk11[:], key_gradient(1, 1)[:])
-        scatter("scalar", 1, N, dk11[:, halves[0]])
-        copy_on("scalar", dk2[:, 0:N], key_gradient(0, 2)[:])
-        scatter("scalar", 1, N + HALF, dk11[:, halves[1]])
-        store(nc.sync, 1)
-        scatter("scalar", 2, 0, dk2[:, 0:HALF])
-
-        copy_on("vector", dk2[:, N : 2 * N], key_gradient(1, 2)[:])
+        dk11 = qm11_group.bitcast(F32)
+        copy_on("vector", dk11, acc11[:])
         copy_on("vector", dk3[:, N : 2 * N], key_gradient(1, 3)[:])
-        scatter("vector", 2, HALF, dk2[:, HALF : 2 * N])
-        store(nc.sync, 2)
+        scatter("vector", 1, N, dk11)
+        store(nc.sync, 1)
 
-        for e0, e1 in ((HALF, HALF + SCALAR_PIECE), (HALF + SCALAR_PIECE, 2 * N), (0, HALF)):
-            scatter("scalar", 3, e0, dk3[:, e0:e1])
-        store(nc.scalar, 3)
+        scatter("scalar", 2, 0, dk2[:, 0:SCALAR_PIECE])
+        scatter("scalar", 3, 0, dk3[:, 0:LAST_ON_SCALAR])
+        copy_on("scalar", dk2[:, N : 2 * N], key_gradient(1, 2)[:])
+        scatter("scalar", 2, SCALAR_PIECE, dk2[:, SCALAR_PIECE : 2 * SCALAR_PIECE])
+        scatter("scalar", 2, 2 * SCALAR_PIECE, dk2[:, 2 * SCALAR_PIECE : 2 * N])
+        store(nc.scalar, 2)
+        scatter("vector", 3, LAST_ON_SCALAR, dk3[:, LAST_ON_SCALAR : 2 * N])
+        store(nc.sync, 3)

@@ -21,10 +21,9 @@ PACK = 4
 W = 512
 HALF = W // 2
 LIST_COLS = N // 16
-Q1_ON_VECTOR = 72
-DO0_ON_VECTOR = 96
+Q_ON_VECTOR = (88, 48)
+DO0_ON_VECTOR = 64
 SCALAR_PIECE = 384
-LAST_ON_SCALAR = 256
 
 
 def tile_attend_gat_sig_k_kernel(tc, qT, kT, vT, doT, rw, qm, offs, out):
@@ -97,10 +96,9 @@ def tile_attend_gat_sig_k_kernel(tc, qT, kT, vT, doT, rw, qm, offs, out):
             src = pairs[:].bitcast(word).rearrange("p (b u n) -> p b n u", u=2, n=N)[:, b, n0:n1]
             copy_on(engine, dst, src)
 
-        def quantize(name, group, fmt, tag=None, codes=None):
+        def quantize(name, group, fmt, tag=None):
             words = group.shape[1] // PACK
-            if codes is None:
-                codes = new_tile([P, words], U32, name + "_codes", tag)
+            codes = new_tile([P, words], U32, name + "_codes", tag)
             scales = new_tile([P, words], U8, name + "_scales")
             nc.vector.quantize_mx(out=codes[:].bitcast(fmt), scales=scales[:], in_=group)
             return codes, scales, fmt
@@ -150,16 +148,19 @@ def tile_attend_gat_sig_k_kernel(tc, qT, kT, vT, doT, rw, qm, offs, out):
         q_group = [new_tile([P, W * PACK], BF16, "q_group%d" % b) for b in range(B)]
         k0_group = new_tile([P, W * PACK], BF16, "k_group0")
         weave_words("scalar", k0_group, k_pairs, 0, 0, N)
-        deal_queries("vector", q_group[0][:], q_raw[0], 0, P)
+        deal_queries("vector", q_group[0][:], q_raw[0], 0, Q_ON_VECTOR[0])
+        deal_queries("scalar", q_group[0][:], q_raw[0], Q_ON_VECTOR[0], P)
         k_group = [k0_group, new_tile([P, W * PACK], BF16, "k_group1")]
         weave_words("scalar", k_group[1], k_pairs, 1, 0, N)
         scores = []
         for b in range(B):
             if b == 1:
-                deal_queries("vector", q_group[1][:], q_raw[1], 0, Q1_ON_VECTOR)
-                deal_queries("scalar", q_group[1][:], q_raw[1], Q1_ON_VECTOR, P)
-            k_op = quantize("k%d" % b, k_group[b][:], E4M3, ("q0", "q_group0")[b])
+                deal_queries("vector", q_group[1][:], q_raw[1], 0, Q_ON_VECTOR[1])
+                deal_queries("scalar", q_group[1][:], q_raw[1], Q_ON_VECTOR[1], P)
+            k_op = quantize("k%d" % b, k_group[b][:], E4M3) if b == 0 else None
             q_op = quantize("q%d" % b, q_group[b][:], E4M3)
+            if b == 1:
+                k_op = quantize("k1", k_group[1][:], E4M3, "q_group1")
             banks = [new_bank(b * PACK + t) for t in range(PACK)]
             for t in range(PACK):
                 product(banks[t][:], q_op, t, k_op, 0, N)
@@ -171,11 +172,11 @@ def tile_attend_gat_sig_k_kernel(tc, qT, kT, vT, doT, rw, qm, offs, out):
         for b in range(B):
             gather_one(v_pairs, value_planes[PACK - 1], PACK - 1, b)
         do_raw = [load_rows(doT[0], "a0")]
-        do_raw.append(load_rows(doT[1], "a1"))
-        qm_raw = {(0, 0): load_rows(qm[0], "a2", 0, HALF)}
+        qm_raw = {(0, 0): load_rows(qm[0], "a1", 0, HALF)}
+        do_raw.append(load_rows(doT[1], "a2"))
         qm_raw[(1, 0)] = load_rows(qm[1], "a3", 0, HALF)
-        qm_raw[(0, 1)] = load_rows(qm[0], "k_group1", HALF, W)
-        qm_raw[(1, 1)] = load_rows(qm[1], "q_group1", HALF, W)
+        qm_raw[(0, 1)] = load_rows(qm[0], "q0", HALF, W)
+        qm_raw[(1, 1)] = load_rows(qm[1], "q_group0", HALF, W)
         weights = []
         for b in range(B):
             weight = new_tile([P, PACK, N], F32, "weight%d" % b, ("q1", "weight1")[b])
@@ -199,7 +200,7 @@ def tile_attend_gat_sig_k_kernel(tc, qT, kT, vT, doT, rw, qm, offs, out):
                 for t in range(PACK):
                     product(acc[:, t * P : (t + 1) * P], do_op, t, v_op, c * P, (c + 1) * P)
                 nc.vector.tensor_tensor(
-                    out=ds_group[:, c * W : (c + 1) * W].rearrange("p (n i t) -> p n t i", i=4, t=PACK),
+                    out=ds_group[:, (c - blocks[0]) * W : (c - blocks[0] + 1) * W].rearrange("p (n i t) -> p n t i", i=4, t=PACK),
                     in0=acc[:].rearrange("p (t n i) -> p n t i", i=4, t=PACK),
                     in1=weights[b][:, :, c * P : (c + 1) * P].rearrange("p t (n i) -> p n t i", i=4),
                     op=ALU.mult,
@@ -212,11 +213,13 @@ def tile_attend_gat_sig_k_kernel(tc, qT, kT, vT, doT, rw, qm, offs, out):
         deal_queries("scalar", do0_group[:], do_raw[0], DO0_ON_VECTOR, P)
         v0 = quantize("v0", v0_group[:], E4M3)
         do0 = quantize("do0", do0_group[:], E5M2)
-        qm_group = new_tile([P, HALF * PACK], BF16, "qm00_group", "do0_group")
-        interleave("vector", qm_group[:], qm_raw[(0, 0)][:])
-        qm_op = {}
-        late = new_tile([P, 2 * W * PACK], BF16, "late")
-        do1_group, ds1_group = late[:, 0 : W * PACK], late[:, W * PACK : 2 * W * PACK]
+        middle = new_tile([P, 6 * W], BF16, "middle")
+        v1_group, qm00_group, ds0_first = middle[:, 0 : 4 * W], middle[:, 7 * HALF : 11 * HALF], middle[:, 4 * W : 6 * W]
+        interleave("scalar", qm00_group, qm_raw[(0, 0)][:])
+        qm_op = {(0, 0): quantize("qm00", qm00_group, E4M3, "do0_group")}
+        weave_words("gpsimd", v1_group, v_pairs, 1, 0, N)
+        late = new_tile([P, 6 * W], BF16, "late")
+        do1_group = late[:, 0 : 4 * W]
         deal_queries("scalar", do1_group, do_raw[1], 0, P)
 
         def scatter(engine, j, e0, src):
@@ -226,59 +229,52 @@ def tile_attend_gat_sig_k_kernel(tc, qT, kT, vT, doT, rw, qm, offs, out):
             queue.dma_start(out[j * P : (j + 1) * P, :], windows[j][:])
 
         halves = (slice(0, HALF), slice(HALF, W))
-        ds0_group = new_tile([P, W * PACK], BF16, "ds0_group", "k_group0")
         ds0 = (new_tile([P, W], U32, "ds0_codes"), new_tile([P, W], U8, "ds0_scales"), E5M2)
+        first = []
         for h, cols in enumerate(halves):
-            weighted_gradient(0, do0, v0, ds0_group, range(2 * h, 2 * h + 2))
-            if h == 0:
-                qm_op[(0, 0)] = quantize("qm00", qm_group[:], E4M3, "do0_codes")
-                v1_group = new_tile([P, W * PACK], BF16, "v1_group", "a2")
-                weave_words("gpsimd", v1_group, v_pairs, 1, 0, N)
-            nc.vector.quantize_mx(
-                out=ds0[0][:, cols].bitcast(E5M2), scales=ds0[1][:, cols],
-                in_=ds0_group[:, cols.start * PACK : cols.stop * PACK],
-            )
-            acc = new_bank(2 * h)
+            ds_half = (ds0_first, late[:, 2 * W : 4 * W])[h]
+            weighted_gradient(0, do0, v0, ds_half, range(2 * h, 2 * h + 2))
+            nc.vector.quantize_mx(out=ds0[0][:, cols].bitcast(E5M2), scales=ds0[1][:, cols], in_=ds_half)
+            first.append(new_bank(2 * h))
             for j in range(2):
-                product(acc[:, halves[j]], qm_op[(0, 0)], j, ds0, cols.start, cols.stop)
+                product(first[h][:, halves[j]], qm_op[(0, 0)], (j + h) % 2, ds0, cols.start, cols.stop)
             if h == 0:
                 early = new_tile([P, W], F32, "early")
-                copy_on("scalar", early[:], acc[:])
+                copy_on("scalar", early[:], first[0][:])
                 for j in range(2):
-                    scatter("scalar", j, cols.start, early[:, halves[j]])
+                    scatter("scalar", j, 0, early[:, halves[j]])
+                v1 = quantize("v1", v1_group, E4M3)
+                do1 = quantize("do1", do1_group, E5M2)
         ds = [ds0]
 
-        qm10_group = new_tile([P, HALF * PACK], BF16, "qm10_group")
-        interleave("scalar", qm10_group[:], qm_raw[(1, 0)][:])
-        codes = new_tile([P, 2 * W], U32, "v1_do1_codes", "k_group0")
-        v1 = quantize("v1", v1_group[:], E4M3, codes=codes[:, 0:W])
-        do1 = quantize("do1", do1_group, E5M2, codes=codes[:, W : 2 * W])
-        qm_op[(1, 0)] = quantize("qm10", qm10_group[:], E4M3)
-        early = do1_group[:, 0 : HALF * PACK].bitcast(F32)
-        copy_on("vector", early, acc[:])
-        for j in range(2):
-            scatter("scalar", j, HALF, early[:, halves[j]])
+        qm10_group = late[:, 4 * W : 6 * W]
+        interleave("scalar", qm10_group, qm_raw[(1, 0)][:])
+        qm_op[(1, 0)] = quantize("qm10", qm10_group, E4M3)
+        dk0 = new_tile([P, B * N], F32, "dk0")
+        copy_on("scalar", dk0[:, 0:N], first[1][:])
+        scatter("scalar", 1, HALF, dk0[:, 0:HALF])
 
         def key_gradient(b, j):
             acc = new_bank((1, 3)[j - 2] if b == 0 else PACK + j)
             product(acc[:], qm_op[(b, j // 2)], j % 2, ds[b], 0, N)
             return acc
 
-        weighted_gradient(1, do1, v1, ds1_group, range(N // P))
-        interleave("gpsimd", do1_group[:, HALF * PACK : W * PACK], qm_raw[(0, 1)][:])
-        qm_op[(0, 1)] = quantize("qm01", do1_group[:, HALF * PACK : W * PACK], E4M3)
-        ds.append(quantize("ds1", ds1_group, E5M2))
+        ds1_group = new_tile([P, W * PACK], BF16, "ds1_group", "k_group0")
+        weighted_gradient(1, do1, v1, ds1_group[:], range(N // P))
+        qm01_group = late[:, 3 * W : 5 * W]
+        interleave("gpsimd", qm01_group, qm_raw[(0, 1)][:])
+        ds.append(quantize("ds1", ds1_group[:], E5M2))
+        qm_op[(0, 1)] = quantize("qm01", qm01_group, E4M3, "k_group0")
 
-        qm11_group = late[:, 3 * W : 5 * W]
+        qm11_group = qm01_group
         interleave("gpsimd", qm11_group, qm_raw[(1, 1)][:])
-        dk10 = new_tile([P, N], F32, "dk10")
         dk2 = new_tile([P, B * N], F32, "dk2")
         dk3 = new_tile([P, B * N], F32, "dk3")
-        copy_on("vector", dk10[:], key_gradient(1, 0)[:])
-        copy_on("vector", dk3[:, 0:N], key_gradient(0, 3)[:])
+        copy_on("vector", dk0[:, N : 2 * N], key_gradient(1, 0)[:])
+        copy_on("scalar", dk3[:, 0:N], key_gradient(0, 3)[:])
         copy_on("scalar", dk2[:, 0:N], key_gradient(0, 2)[:])
         acc11 = key_gradient(1, 1)
-        scatter("vector", 0, N, dk10[:])
+        scatter("vector", 0, HALF, dk0[:, HALF : 2 * N])
         store(nc.sync, 0)
         qm_op[(1, 1)] = quantize("qm11", qm11_group, E4M3)
         dk11 = qm11_group.bitcast(F32)
@@ -287,11 +283,11 @@ def tile_attend_gat_sig_k_kernel(tc, qT, kT, vT, doT, rw, qm, offs, out):
         scatter("vector", 1, N, dk11)
         store(nc.sync, 1)
 
+        scatter("scalar", 3, 0, dk3[:, 0:HALF])
         scatter("scalar", 2, 0, dk2[:, 0:SCALAR_PIECE])
-        scatter("scalar", 3, 0, dk3[:, 0:LAST_ON_SCALAR])
         copy_on("scalar", dk2[:, N : 2 * N], key_gradient(1, 2)[:])
         scatter("scalar", 2, SCALAR_PIECE, dk2[:, SCALAR_PIECE : 2 * SCALAR_PIECE])
         scatter("scalar", 2, 2 * SCALAR_PIECE, dk2[:, 2 * SCALAR_PIECE : 2 * N])
         store(nc.scalar, 2)
-        scatter("vector", 3, LAST_ON_SCALAR, dk3[:, LAST_ON_SCALAR : 2 * N])
+        scatter("vector", 3, HALF, dk3[:, HALF : 2 * N])
         store(nc.sync, 3)

@@ -21,9 +21,10 @@ PACK = 4
 W = 512
 HALF = W // 2
 LIST_COLS = N // 16
-Q_ON_VECTOR = (88, 48)
-DO0_ON_VECTOR = 64
+Q_ON_VECTOR = (88, 64)
+DO0_ON_VECTOR = 24
 SCALAR_PIECE = 384
+EARLY_FACTORS = 2
 
 
 def tile_attend_gat_sig_k_kernel(tc, qT, kT, vT, doT, rw, qm, offs, out):
@@ -157,16 +158,14 @@ def tile_attend_gat_sig_k_kernel(tc, qT, kT, vT, doT, rw, qm, offs, out):
             if b == 1:
                 deal_queries("vector", q_group[1][:], q_raw[1], 0, Q_ON_VECTOR[1])
                 deal_queries("scalar", q_group[1][:], q_raw[1], Q_ON_VECTOR[1], P)
-            k_op = quantize("k%d" % b, k_group[b][:], E4M3) if b == 0 else None
+            k_op = quantize("k%d" % b, k_group[b][:], E4M3)
             q_op = quantize("q%d" % b, q_group[b][:], E4M3)
-            if b == 1:
-                k_op = quantize("k1", k_group[1][:], E4M3, "q_group1")
             banks = [new_bank(b * PACK + t) for t in range(PACK)]
             for t in range(PACK):
                 product(banks[t][:], q_op, t, k_op, 0, N)
             scores.append(banks)
 
-        v_pairs = new_tile([P, B * PACK * N], BF16, "v_pairs")
+        v_pairs = new_tile([P, B * PACK * N], BF16, "v_pairs", "q_group1")
         for t in range(PACK - 1):
             gather_whole(v_pairs, value_planes[t], t)
         for b in range(B):
@@ -186,7 +185,7 @@ def tile_attend_gat_sig_k_kernel(tc, qT, kT, vT, doT, rw, qm, offs, out):
                     nc.scalar.activation(out=weight[:, 0:2, :], in_=weight[:, 0:2, :], func=ACT.Square)
             for t in range(2, PACK):
                 nc.scalar.activation(out=weight[:, t, :], in_=weight[:, t, :], func=ACT.Square)
-            for t in range(PACK):
+            for t in range(PACK if b == 0 else EARLY_FACTORS):
                 col = slice(b * PACK + t, b * PACK + t + 1)
                 nc.gpsimd.tensor_scalar(
                     out=weight[:, t, :], in0=weight[:, t, :], scalar1=gate_neg[:, col], scalar2=gate_pos[:, col],
@@ -206,8 +205,8 @@ def tile_attend_gat_sig_k_kernel(tc, qT, kT, vT, doT, rw, qm, offs, out):
                     op=ALU.mult,
                 )
 
-        v0_group = new_tile([P, W * PACK], BF16, "v0_group")
-        weave_words("scalar", v0_group, v_pairs, 0, 0, N)
+        v0_group = new_tile([P, W * PACK], BF16, "v0_group", "gate_neg")
+        weave_words("gpsimd", v0_group, v_pairs, 0, 0, N)
         do0_group = new_tile([P, W * PACK], BF16, "do0_group")
         deal_queries("vector", do0_group[:], do_raw[0], 0, DO0_ON_VECTOR)
         deal_queries("scalar", do0_group[:], do_raw[0], DO0_ON_VECTOR, P)
@@ -237,7 +236,7 @@ def tile_attend_gat_sig_k_kernel(tc, qT, kT, vT, doT, rw, qm, offs, out):
             nc.vector.quantize_mx(out=ds0[0][:, cols].bitcast(E5M2), scales=ds0[1][:, cols], in_=ds_half)
             first.append(new_bank(2 * h))
             for j in range(2):
-                product(first[h][:, halves[j]], qm_op[(0, 0)], (j + h) % 2, ds0, cols.start, cols.stop)
+                product(first[h][:, halves[j]], qm_op[(0, 0)], j, ds0, cols.start, cols.stop)
             if h == 0:
                 early = new_tile([P, W], F32, "early")
                 copy_on("scalar", early[:], first[0][:])
@@ -245,17 +244,25 @@ def tile_attend_gat_sig_k_kernel(tc, qT, kT, vT, doT, rw, qm, offs, out):
                     scatter("scalar", j, 0, early[:, halves[j]])
                 v1 = quantize("v1", v1_group, E4M3)
                 do1 = quantize("do1", do1_group, E5M2)
+                late_gate = late[:, 0 : 2 * PACK].bitcast(F32)
+                nc.gpsimd.tensor_scalar(out=late_gate, in0=gate[:, 1, :], scalar1=-0.25, scalar2=0.0, op0=ALU.mult, op1=ALU.add)
+                for t in range(EARLY_FACTORS, PACK):
+                    nc.gpsimd.tensor_scalar(
+                        out=weights[1][:, t, :], in0=weights[1][:, t, :], scalar1=late_gate[:, t : t + 1],
+                        scalar2=gate_pos[:, PACK + t : PACK + t + 1], op0=ALU.mult, op1=ALU.add,
+                    )
         ds = [ds0]
 
         qm10_group = late[:, 4 * W : 6 * W]
         interleave("scalar", qm10_group, qm_raw[(1, 0)][:])
         qm_op[(1, 0)] = quantize("qm10", qm10_group, E4M3)
-        dk0 = new_tile([P, B * N], F32, "dk0")
-        copy_on("scalar", dk0[:, 0:N], first[1][:])
-        scatter("scalar", 1, HALF, dk0[:, 0:HALF])
+        early1 = new_tile([P, W], F32, "early1")
+        copy_on("scalar", early1[:], first[1][:])
+        for j in range(2):
+            scatter("scalar", j, HALF, early1[:, halves[j]])
 
         def key_gradient(b, j):
-            acc = new_bank((1, 3)[j - 2] if b == 0 else PACK + j)
+            acc = new_bank((1, 3)[j - 2] if b == 0 else PACK + j - (j == 1))
             product(acc[:], qm_op[(b, j // 2)], j % 2, ds[b], 0, N)
             return acc
 
@@ -270,11 +277,12 @@ def tile_attend_gat_sig_k_kernel(tc, qT, kT, vT, doT, rw, qm, offs, out):
         interleave("gpsimd", qm11_group, qm_raw[(1, 1)][:])
         dk2 = new_tile([P, B * N], F32, "dk2")
         dk3 = new_tile([P, B * N], F32, "dk3")
-        copy_on("vector", dk0[:, N : 2 * N], key_gradient(1, 0)[:])
+        dk10 = new_tile([P, N], F32, "dk10")
+        copy_on("vector", dk10[:], key_gradient(1, 0)[:])
         copy_on("scalar", dk3[:, 0:N], key_gradient(0, 3)[:])
         copy_on("scalar", dk2[:, 0:N], key_gradient(0, 2)[:])
         acc11 = key_gradient(1, 1)
-        scatter("vector", 0, HALF, dk0[:, HALF : 2 * N])
+        scatter("vector", 0, N, dk10[:])
         store(nc.sync, 0)
         qm_op[(1, 1)] = quantize("qm11", qm11_group, E4M3)
         dk11 = qm11_group.bitcast(F32)

from contextlib import ExitStack

import concourse.mybir as mybir

B, N, T, D, R = 2, 512, 2048, 512, 512
FLOPS = 3 * 2 * B * N * D * R

F32 = mybir.dt.float32
BF16 = mybir.dt.bfloat16
U32 = mybir.dt.uint32
I32 = mybir.dt.int32
U16 = mybir.dt.uint16
U8 = mybir.dt.uint8
E4M3 = mybir.dt.float8_e4m3fn_x4
E5M2 = mybir.dt.float8_e5m2_x4
ACT = mybir.ActivationFunctionType
ALU = mybir.AluOpType

P = 128
PACK = 4
W = 512
HALF = W // 2
LIST_COLS = N // 16
Q_ON_VECTOR = (88, 64)
DO0_ON_VECTOR = 24
SCALAR_PIECE = 384
EARLY_FACTORS = 2


def tile_attend_gat_sig_k_kernel(tc, qT, kT, vT, doT, rw, qm, offs, out):
    nc = tc.nc
    with ExitStack() as ctx:
        keep = ctx.enter_context(tc.tile_pool(name="keep", bufs=1))
        psum = ctx.enter_context(tc.psum_pool(name="psum", bufs=1))

        def new_tile(shape, dtype, name, tag=None):
            return keep.tile(shape, dtype, name=name, tag=tag or name, align_bytes=64)

        def load_plane(pool_dram, t, tag):
            plane = new_tile([P, T], F32, "plane", tag)
            nc.sync.dma_start(plane[:], pool_dram.rearrange("(p t) n -> p t n", t=PACK)[:, t, :])
            return plane

        def load_rows(rows, tag, c0=0, c1=W):
            raw = new_tile([P, PACK, c1 - c0], F32, "raw", tag)
            nc.sync.dma_start(raw[:], rows.rearrange("(p j) w -> p j w", j=PACK)[:, :, c0:c1])
            return raw

        key_planes = [load_plane(kT, 0, "a0")]
        offsets = keep.tile([P, B * LIST_COLS], U16, name="offsets")
        nc.sync.dma_start(offsets[:], offs)
        gate = new_tile([P, B, PACK], F32, "gate")
        nc.sync.dma_start(gate[:], rw.rearrange("b (p t) o -> p b (t o)", t=PACK))
        key_planes = key_planes + [load_plane(kT, t, "a%d" % t) for t in range(1, PACK)]
        q_raw = [load_rows(qT[0], "q0")]
        q_raw.append(load_rows(qT[1], "q1"))
        value_planes = [load_plane(vT, t, "b%d" % t) for t in range(PACK)]

        windows = [new_tile([P, T], F32, "window%d" % j) for j in range(D // P)]
        for window in windows:
            nc.vector.memset(window[:], 0.0)

        def entries(e0, e1):
            return offsets[:, e0 // 16 : e1 // 16]

        def copy_on(engine, dst, src):
            if engine == "vector":
                nc.vector.tensor_copy(out=dst, in_=src)
            elif engine == "gpsimd":
                nc.gpsimd.tensor_copy(out=dst, in_=src)
            else:
                nc.scalar.copy(out=dst, in_=src)

        def indirect_copy(engine, dst, src):
            if engine == "vector":
                nc.vector.tensor_copy(out=dst, in_=src)
            else:
                nc.scalar.activation(out=dst, in_=src, func=ACT.Copy)

        def interleave(engine, group, src):
            copy_on(
                engine,
                group.rearrange("p (c i j) -> p c j i", i=4, j=PACK),
                src.rearrange("p j (c i) -> p c j i", i=4),
            )

        def deal_queries(engine, group, src, m0, m1):
            copy_on(
                engine,
                group.rearrange("p (t m j) -> p m j t", t=PACK, j=PACK)[:, m0:m1],
                src[:].rearrange("p j (m t) -> p m j t", t=PACK)[:, m0:m1],
            )

        def weave_words(engine, group, pairs, b, n0, n1):
            word = I32 if engine == "vector" else U32
            dst = group[:].bitcast(word).rearrange("p (n u) -> p n u", u=2)[:, n0:n1]
            src = pairs[:].bitcast(word).rearrange("p (b u n) -> p b n u", u=2, n=N)[:, b, n0:n1]
            copy_on(engine, dst, src)

        def quantize(name, group, fmt, tag=None):
            words = group.shape[1] // PACK
            codes = new_tile([P, words], U32, name + "_codes", tag)
            scales = new_tile([P, words], U8, name + "_scales")
            nc.vector.quantize_mx(out=codes[:].bitcast(fmt), scales=scales[:], in_=group)
            return codes, scales, fmt

        def product(acc, stationary, block, moving, n0, n1):
            cols = slice(block * P, (block + 1) * P)
            nc.tensor.matmul_mx(
                out=acc,
                lhsT=stationary[0][:, cols].bitcast(stationary[2]),
                lhsT_scale=stationary[1][:, cols],
                rhs=moving[0][:, n0:n1].bitcast(moving[2]),
                rhs_scale=moving[1][:, n0:n1],
                start=True,
                stop=True,
            )

        def new_bank(bank):
            return psum.tile([P, W], F32, name="acc", tag="bank%d" % bank)

        def pair_view(pairs):
            return pairs[:].rearrange("p (b u n e) -> p b u e n", u=2, e=2, n=N)

        def gather_whole(pairs, plane, t):
            indirect_copy("vector", pair_view(pairs)[:, :, t // 2, t % 2, :], plane[:].indirect(offsets[:]))

        def gather_one(pairs, plane, t, b):
            indirect_copy("vector", pair_view(pairs)[:, b, t // 2, t % 2, :], plane[:].indirect(entries(b * N, (b + 1) * N)))

        k_pairs = new_tile([P, B * PACK * N], BF16, "k_pairs")
        k_rows = new_tile([P, 2, N], BF16, "k_rows")
        for t in range(2):
            gather_one(k_pairs, key_planes[t], t, 0)
            indirect_copy("scalar", k_rows[:, t, :], key_planes[t][:].indirect(entries(N, 2 * N)))
        copy_on(
            "scalar",
            k_pairs[:, PACK * N : (PACK + 2) * N].rearrange("p (n e) -> p n e", e=2),
            k_rows[:].rearrange("p e n -> p n e"),
        )
        gather_whole(k_pairs, key_planes[2], 2)
        for b in range(B):
            gather_one(k_pairs, key_planes[3], 3, b)
        gate_pos = new_tile([P, B * PACK], F32, "gate_pos")
        gate_neg = new_tile([P, B * PACK], F32, "gate_neg")
        gate_flat = gate[:].rearrange("p b t -> p (b t)")
        nc.gpsimd.tensor_scalar(out=gate_pos[:], in0=gate_flat, scalar1=0.25, scalar2=0.0, op0=ALU.mult, op1=ALU.add)
        nc.gpsimd.tensor_scalar(out=gate_neg[:], in0=gate_flat, scalar1=-0.25, scalar2=0.0, op0=ALU.mult, op1=ALU.add)
        q_group = [new_tile([P, W * PACK], BF16, "q_group%d" % b) for b in range(B)]
        k0_group = new_tile([P, W * PACK], BF16, "k_group0")
        weave_words("scalar", k0_group, k_pairs, 0, 0, N)
        deal_queries("vector", q_group[0][:], q_raw[0], 0, Q_ON_VECTOR[0])
        deal_queries("scalar", q_group[0][:], q_raw[0], Q_ON_VECTOR[0], P)
        k_group = [k0_group, new_tile([P, W * PACK], BF16, "k_group1")]
        weave_words("scalar", k_group[1], k_pairs, 1, 0, N)
        scores = []
        for b in range(B):
            if b == 1:
                deal_queries("vector", q_group[1][:], q_raw[1], 0, Q_ON_VECTOR[1])
                deal_queries("scalar", q_group[1][:], q_raw[1], Q_ON_VECTOR[1], P)
            k_op = quantize("k%d" % b, k_group[b][:], E4M3)
            q_op = quantize("q%d" % b, q_group[b][:], E4M3)
            banks = [new_bank(b * PACK + t) for t in range(PACK)]
            for t in range(PACK):
                product(banks[t][:], q_op, t, k_op, 0, N)
            scores.append(banks)

        v_pairs = new_tile([P, B * PACK * N], BF16, "v_pairs", "q_group1")
        for t in range(PACK - 1):
            gather_whole(v_pairs, value_planes[t], t)
        for b in range(B):
            gather_one(v_pairs, value_planes[PACK - 1], PACK - 1, b)
        do_raw = [load_rows(doT[0], "a0")]
        qm_raw = {(0, 0): load_rows(qm[0], "a1", 0, HALF)}
        do_raw.append(load_rows(doT[1], "a2"))
        qm_raw[(1, 0)] = load_rows(qm[1], "a3", 0, HALF)
        qm_raw[(0, 1)] = load_rows(qm[0], "q0", HALF, W)
        qm_raw[(1, 1)] = load_rows(qm[1], "q_group0", HALF, W)
        weights = []
        for b in range(B):
            weight = new_tile([P, PACK, N], F32, "weight%d" % b, ("q1", "weight1")[b])
            for t in range(PACK):
                nc.scalar.activation(out=weight[:, t, :], in_=scores[b][t][:], func=ACT.Tanh, scale=0.5)
                if t == 2:
                    nc.scalar.activation(out=weight[:, 0:2, :], in_=weight[:, 0:2, :], func=ACT.Square)
            for t in range(2, PACK):
                nc.scalar.activation(out=weight[:, t, :], in_=weight[:, t, :], func=ACT.Square)
            for t in range(PACK if b == 0 else EARLY_FACTORS):
                col = slice(b * PACK + t, b * PACK + t + 1)
                nc.gpsimd.tensor_scalar(
                    out=weight[:, t, :], in0=weight[:, t, :], scalar1=gate_neg[:, col], scalar2=gate_pos[:, col],
                    op0=ALU.mult, op1=ALU.add,
                )
            weights.append(weight)

        def weighted_gradient(b, do_op, v_op, ds_group, blocks):
            for c in blocks:
                acc = new_bank(b * PACK + c)
                for t in range(PACK):
                    product(acc[:, t * P : (t + 1) * P], do_op, t, v_op, c * P, (c + 1) * P)
                nc.vector.tensor_tensor(
                    out=ds_group[:, (c - blocks[0]) * W : (c - blocks[0] + 1) * W].rearrange("p (n i t) -> p n t i", i=4, t=PACK),
                    in0=acc[:].rearrange("p (t n i) -> p n t i", i=4, t=PACK),
                    in1=weights[b][:, :, c * P : (c + 1) * P].rearrange("p t (n i) -> p n t i", i=4),
                    op=ALU.mult,
                )

        v0_group = new_tile([P, W * PACK], BF16, "v0_group", "gate_neg")
        weave_words("gpsimd", v0_group, v_pairs, 0, 0, N)
        do0_group = new_tile([P, W * PACK], BF16, "do0_group")
        deal_queries("vector", do0_group[:], do_raw[0], 0, DO0_ON_VECTOR)
        deal_queries("scalar", do0_group[:], do_raw[0], DO0_ON_VECTOR, P)
        v0 = quantize("v0", v0_group[:], E4M3)
        do0 = quantize("do0", do0_group[:], E5M2)
        middle = new_tile([P, 6 * W], BF16, "middle")
        v1_group, qm00_group, ds0_first = middle[:, 0 : 4 * W], middle[:, 7 * HALF : 11 * HALF], middle[:, 4 * W : 6 * W]
        interleave("scalar", qm00_group, qm_raw[(0, 0)][:])
        qm_op = {(0, 0): quantize("qm00", qm00_group, E4M3, "do0_group")}
        weave_words("gpsimd", v1_group, v_pairs, 1, 0, N)
        late = new_tile([P, 6 * W], BF16, "late")
        do1_group = late[:, 0 : 4 * W]
        deal_queries("scalar", do1_group, do_raw[1], 0, P)

        def scatter(engine, j, e0, src):
            indirect_copy(engine, windows[j][:].indirect(entries(e0, e0 + src.shape[1])), src)

        def store(queue, j):
            queue.dma_start(out[j * P : (j + 1) * P, :], windows[j][:])

        halves = (slice(0, HALF), slice(HALF, W))
        ds0 = (new_tile([P, W], U32, "ds0_codes"), new_tile([P, W], U8, "ds0_scales"), E5M2)
        first = []
        for h, cols in enumerate(halves):
            ds_half = (ds0_first, late[:, 2 * W : 4 * W])[h]
            weighted_gradient(0, do0, v0, ds_half, range(2 * h, 2 * h + 2))
            nc.vector.quantize_mx(out=ds0[0][:, cols].bitcast(E5M2), scales=ds0[1][:, cols], in_=ds_half)
            first.append(new_bank(2 * h))
            for j in range(2):
                product(first[h][:, halves[j]], qm_op[(0, 0)], j, ds0, cols.start, cols.stop)
            if h == 0:
                early = new_tile([P, W], F32, "early")
                copy_on("scalar", early[:], first[0][:])
                for j in range(2):
                    scatter("scalar", j, 0, early[:, halves[j]])
                v1 = quantize("v1", v1_group, E4M3)
                do1 = quantize("do1", do1_group, E5M2)
                late_gate = late[:, 0 : 2 * PACK].bitcast(F32)
                nc.gpsimd.tensor_scalar(out=late_gate, in0=gate[:, 1, :], scalar1=-0.25, scalar2=0.0, op0=ALU.mult, op1=ALU.add)
                for t in range(EARLY_FACTORS, PACK):
                    nc.gpsimd.tensor_scalar(
                        out=weights[1][:, t, :], in0=weights[1][:, t, :], scalar1=late_gate[:, t : t + 1],
                        scalar2=gate_pos[:, PACK + t : PACK + t + 1], op0=ALU.mult, op1=ALU.add,
                    )
        ds = [ds0]

        qm10_group = late[:, 4 * W : 6 * W]
        interleave("scalar", qm10_group, qm_raw[(1, 0)][:])
        qm_op[(1, 0)] = quantize("qm10", qm10_group, E4M3)
        early1 = new_tile([P, W], F32, "early1")
        copy_on("scalar", early1[:], first[1][:])
        for j in range(2):
            scatter("scalar", j, HALF, early1[:, halves[j]])

        def key_gradient(b, j):
            acc = new_bank((1, 3)[j - 2] if b == 0 else PACK + j - (j == 1))
            product(acc[:], qm_op[(b, j // 2)], j % 2, ds[b], 0, N)
            return acc

        ds1_group = new_tile([P, W * PACK], BF16, "ds1_group", "k_group0")
        weighted_gradient(1, do1, v1, ds1_group[:], range(N // P))
        qm01_group = late[:, 3 * W : 5 * W]
        interleave("gpsimd", qm01_group, qm_raw[(0, 1)][:])
        ds.append(quantize("ds1", ds1_group[:], E5M2))
        qm_op[(0, 1)] = quantize("qm01", qm01_group, E4M3, "k_group0")

        qm11_group = qm01_group
        interleave("gpsimd", qm11_group, qm_raw[(1, 1)][:])
        dk2 = new_tile([P, B * N], F32, "dk2")
        dk3 = new_tile([P, B * N], F32, "dk3")
        dk10 = new_tile([P, N], F32, "dk10")
        copy_on("vector", dk10[:], key_gradient(1, 0)[:])
        copy_on("scalar", dk3[:, 0:N], key_gradient(0, 3)[:])
        copy_on("scalar", dk2[:, 0:N], key_gradient(0, 2)[:])
        acc11 = key_gradient(1, 1)
        scatter("vector", 0, N, dk10[:])
        store(nc.sync, 0)
        qm_op[(1, 1)] = quantize("qm11", qm11_group, E4M3)
        dk11 = qm11_group.bitcast(F32)
        copy_on("vector", dk11, acc11[:])
        copy_on("vector", dk3[:, N : 2 * N], key_gradient(1, 3)[:])
        scatter("vector", 1, N, dk11)
        store(nc.sync, 1)

        scatter("scalar", 3, 0, dk3[:, 0:HALF])
        scatter("scalar", 2, 0, dk2[:, 0:SCALAR_PIECE])
        copy_on("scalar", dk2[:, N : 2 * N], key_gradient(1, 2)[:])
        scatter("scalar", 2, SCALAR_PIECE, dk2[:, SCALAR_PIECE : 2 * SCALAR_PIECE])
        scatter("scalar", 2, 2 * SCALAR_PIECE, dk2[:, 2 * SCALAR_PIECE : 2 * N])
        store(nc.scalar, 2)
        scatter("vector", 3, HALF, dk3[:, HALF : 2 * N])
        store(nc.sync, 3)
